import numpy as np, ml_dtypes
CORES = [242,247,114,119]
N = 4
BF = ml_dtypes.bfloat16
def f(rng, *shape):
    return (rng.standard_normal(shape, dtype=np.float32) * np.exp2(rng.integers(-2, 3, shape[:-1] + (1,)))).astype(BF)
def wide(rng, *shape):
    v = f(rng, *shape).astype(np.float32); k = shape[:-2] + (1, shape[-1])
    return (v * np.exp2(rng.integers(-6, 7, k)) * (rng.random(k) > 0.0625)).astype(BF)
E, EP, A, AP, TY = 1024, 256, 16, 4, 128
TR, M, SH = 2048, 3, 4
CAPP, CAPO, L = 640, 192, 768
def vals(rng, v):
    return v
def held(ent, att, g):
    h = np.zeros(E * A, bool); h[(ent[:, g].astype(np.int64) * A + att[:, g]).reshape(-1)] = True
    return h
def places(cls, form, g):
    fo = form[:, g].reshape(N, TY, A)[np.arange(N)[:, None], cls[:, g]].reshape(E, A)
    return [np.arange(E)[:, None] * A + ((fo >> (SH * i)) & (A - 1)) for i in range(M)]
def present(ent, att, cls, form, g):
    h = held(ent, att, g); ok = np.ones((E, A), bool)
    for p in places(cls, form, g):
        ok = ok & h[p]
    return ok
def deal(rng):
    mean = TR // N; m = np.zeros((8, N, N), np.int64)
    for g in range(8):
        for r in range(N):
            o = rng.permutation(N); x = rng.integers(0, CAPP - mean + 1, N // 2); m[g, r, o[0::2]] = mean + x; m[g, r, o[1::2]] = mean - x
    return m
def triples(rng, m, late):
    ent = np.zeros((N, 8, TR), np.int32); att = np.zeros((N, 8, TR), np.int32)
    for g in range(8):
        mine = [[] for r in range(N)]
        for q in range(N):
            pri = rng.random((EP, A)) + late[g, q * EP:(q + 1) * EP, None]; pri[:, 0] = 9
            cuts = np.add.accumulate(m[g, :, q])
            k = rng.permutation(np.argsort(pri, axis=None)[:cuts[-1]]) + q * EP * A
            for r, part in enumerate(np.split(k, cuts[:-1])):
                mine[r].append(part)
        for r in range(N):
            k = rng.permutation(np.concatenate(mine[r])); ent[r, g] = k >> SH; att[r, g] = k & (A - 1)
    return ent, att
def formulas(rng, same):
    fs = rng.integers(1, A, (M, N, 8, TY * A)); fs = np.where(rng.random(fs.shape[1:]) < same, fs[:1], fs)
    return np.where(rng.random(fs.shape) < 0.015625, 0, fs)
def pack(fs):
    v = fs[0]
    for i in range(1, M):
        v = v + (fs[i] << (SH * i))
    return v.astype(np.int32)
def trim(rng, d, full=False):
    for g in range(8):
        ok = present(d["ent"], d["att"], d["cls"], d["form"], g).reshape(N, EP, A)
        for q in range(N):
            n = np.zeros((TY, A), np.int64); np.add.at(n, d["cls"][q, g], ok[q].astype(np.int64))
            for c in range(N):
                w = n[:, c * AP:(c + 1) * AP].reshape(-1)
                if np.sum(w) <= CAPO:
                    continue
                o = rng.permutation(TY * AP)
                if full:
                    o = o[np.argsort(-w[o], kind="stable")]
                s = 0; w = w.tolist()
                for i in o.tolist():
                    if s + w[i] > CAPO:
                        d["form"][q, g, (i // AP) * A + c * AP + (i & (AP - 1))] = 0
                    else:
                        s += w[i]
    return d
def setup_inputs(rng):
    ent, att = triples(rng, deal(rng), np.zeros((8, E)))
    d = {"val": vals(rng, f(rng, N, 128, TR)), "ent": ent, "att": att, "cls": rng.integers(0, TY, (N, 8, EP)).astype(np.int32), "form": pack(formulas(rng, 0.0625))}
    return trim(rng, d)
def setup_inputs_full(rng):
    d = setup_inputs(rng); m = np.zeros((8, N, N), np.int64); crowd = int(rng.integers(8)); odd = int(rng.integers(N))
    for g in range(8):
        s = int(rng.integers(N))
        for r in range(N):
            rest = TR
            for i in range(N):
                o = r + s + i
                if g == crowd:
                    o = s - i if r == odd else s + i
                c = min(CAPP, rest); m[g, r, o % N] = c; rest -= c
    d["ent"], d["att"] = triples(rng, m, np.zeros((8, E)))
    d["cls"] = rng.permuted(np.tile(np.arange(EP) % TY, (N, 8, 1)), axis=2).astype(np.int32)
    fs = np.zeros((M, N, 8, TY * A), np.int64)
    for g in range(8):
        h = held(d["ent"], d["att"], g).reshape(N, EP, A)
        for q in range(N):
            o = np.argsort(np.sum(h[q], axis=1), kind="stable"); rep = np.zeros(TY, np.int64); rep[d["cls"][q, g][o]] = o
            fs[:, q, g] = np.argmax(rng.random((M, TY, A, A)) * h[q][rep][None, :, None, :], axis=3).reshape(M, -1)
    d["form"] = pack(fs); return trim(rng, d, True)
def setup_inputs_ragged(rng):
    d = setup_inputs(rng)
    late = np.stack([np.concatenate([rng.permutation(np.repeat(np.array([-1.0, 0.0, 0.0, 1.0]), EP // 4)) for q in range(N)]) for g in range(8)])
    d["ent"], d["att"] = triples(rng, deal(rng), late); fo = pack(formulas(rng, 0.0625)).reshape(N, 8, TY, A)
    for g in range(8):
        for c in range(N):
            fo[:, g, :, c * AP + int(rng.integers(AP))] = 0
        q, c = int(rng.integers(N)), int(rng.integers(N)); fo[q, g, :, c * AP:(c + 1) * AP] = 0
    d["form"] = np.ascontiguousarray(fo.reshape(N, 8, TY * A)); return trim(rng, d)
def setup_inputs_one(rng):
    d = setup_inputs(rng); d["cls"] = np.repeat(rng.integers(0, TY, (N, 8, 1)), EP, axis=2).astype(np.int32)
    k = np.sort(d["ent"] * A + d["att"], axis=2); k[1::2] = k[1::2, :, ::-1].copy()
    d["ent"] = (k >> SH).astype(np.int32); d["att"] = (k & (A - 1)).astype(np.int32)
    d["form"] = pack(formulas(rng, 0.5)); return trim(rng, d)
def setup_inputs_spread(rng):
    d = setup_inputs(rng); d["val"] = vals(rng, wide(rng, N, 128, TR)); return d
def check_inputs(d):
    bad = []
    for name, lo, hi in (("ent", 0, E), ("att", 1, A), ("cls", 0, TY), ("form", 0, A ** M)):
        if not ((d[name] >= lo) & (d[name] < hi)).all():
            bad.append("range of " + name)
    if not (np.abs(d["val"].astype(np.float32)) < 2.0 ** 100).all():
        bad.append("finite")
    if bad:
        return bad
    ent, att = d["ent"], d["att"]
    for g in range(8):
        if np.count_nonzero(held(ent, att, g)) != N * TR:
            bad.append("distinct triples")
        if max(int(np.bincount(ent[r, g] // EP, minlength=N).max()) for r in range(N)) > CAPP:
            bad.append("triples of a rank for an owner")
        if np.sum(present(ent, att, d["cls"], d["form"], g).reshape(N, EP, N, AP), axis=(1, 3)).max() > CAPO:
            bad.append("derived cells of a pair of owners")
    return sorted(set(bad))
def reference(val, ent, att, cls, form):
    y = np.zeros((N, 128, L), BF); who = np.full((N, 8, L), -1, np.float32); cnt = np.zeros((N, 8, AP), np.float32)
    for g in range(8):
        cell = np.zeros((E * A, 16), np.float32)
        for r in range(N):
            cell[ent[r, g].astype(np.int64) * A + att[r, g]] = val[r, 16 * g:16 * g + 16].T.astype(np.float32)
        ps = places(cls, form, g); ok = present(ent, att, cls, form, g)
        new = cell[ps[0]] - cell[ps[1]]
        for p in ps[2:]:
            new = new + cell[p]
        for c in range(N):
            o = np.ascontiguousarray(ok[:, c * AP:(c + 1) * AP].T); a, e = np.nonzero(o); n = len(e)
            y[c, 16 * g:16 * g + 16, :n] = new[e, c * AP + a].T.astype(BF); who[c, g, :n] = e; cnt[c, g] = np.sum(o, axis=1)
    return {"y": y, "who": who, "cnt": cnt}

@@ -1,0 +1,446 @@
+import math
+from concourse.bass import DstId, RemoteDMATransfer
+from concourse.mybir import AluOpType as ALU, ActivationFunctionType as ACT
+
+S, P = "sbuf", "psum"
+F32, BF, I32, U16, F16 = "float32", "bfloat16", "int32", "uint16", "float16"
+V0 = 32
+SCRATCH = {
+    "entI": (S, [128, 128], I32), "attI": (S, [128, 128], I32), "kI": (S, [128, 128], I32), "kU": (S, [128, 128], U16),
+    "formI": (S, [128, 128], I32), "fI": (S, [128, 384], I32), "fB": (S, [128, 24, 16], BF),
+    "fS": (S, [128, 24, 2, 16], BF), "E1": (S, [128, 24, 2, 16], BF), "E2": (S, [128, 24, 2, 16], BF),
+    "tabD": (S, [128, 768], F32), "tabW": (S, [128, 768], F32), "tabR": (S, [128, 768], F32), "tabT": (S, [128, 768], F32),
+    "clsI": (S, [128, 32], I32), "clsF": (S, [128, 32], F32), "clsT": (S, [128, 32], F32), "clsU": (S, [128, 16], U16),
+    "zero": (S, [128, 512], F32), "win": (S, [128, 16384], F32), "pay": (S, [128, 2048], F32),
+    "tl": (S, [128, 1024], F32), "land": (S, [128, 1024], F32), "mg": (S, [128, 256], F32), "posU": (S, [128, 256], U16),
+    "Pm": (S, [128, 1024], BF), "Ms": (S, [128, 1024], F32), "keep3": (S, [128, 32, 16], BF), "keep": (S, [128, 512], BF),
+    "Mc": (S, [128, 4, 32], F32), "ML": (S, [128, 128], F32), "Mt": (S, [128, 32], F32),
+    "allv": (S, [128, V0 + 8192], BF), "VT": (S, [128, 4096], BF), "U": (S, [128, 512], I32), "ok": (S, [128, 256], BF),
+    "Gt": (S, [128, 256], F32), "incl": (S, [128, 16], BF), "ex": (S, [128, 16], F32),
+    "tz": (S, [128, 16], F32), "offU": (S, [128, 16], U16), "Gw": (S, [128, 1792], F32), "Ww": (S, [128, 1792], BF),
+    "Ds": (S, [128, 768], F32), "Ws": (S, [128, 768], BF), "phi": (S, [128, 768], F16), "neg": (S, [128, 768], BF),
+    "c125": (S, [128, 256], BF), "wid": (S, [128, 256], BF),
+    "ones": (S, [128, 128], BF), "c8192": (S, [128, 128], BF), "Id": (S, [128, 128], BF), "TRI": (S, [128, 128], BF),
+    "DT": (S, [128, 128], BF), "H": (S, [128, 144], BF), "H16": (S, [128, 144], F16), "R": (S, [128, 128], BF),
+    "Rn": (S, [128, 128], BF), "FS": (S, [128, 512], BF), "DD": (S, [128, 512], BF), "RA": (S, [128, 512], BF),
+    "pI": (S, [128, 8], I32), "pJ": (S, [128, 8], I32), "pF": (S, [128, 8], F32), "cvec": (S, [128, 2], BF),
+    "mI": (S, [128, 32], I32), "mU": (S, [128, 32], U16), "TR": (S, [128, 16], F32), "sw": (S, [128, 48], F32),
+    "Et": (S, [128, 1032], F32), "EL": (S, [128, 776], F32), "wo": (S, [128, 768], F32),
+    "wI": (S, [128, 48], I32), "b15": (S, [128, 48], F32), "e16": (S, [128, 48], F32), "S16": (S, [128, 48], I32),
+    "ab": (S, [128, 48], I32), "fm": (S, [128, 48], I32), "tp": (S, [128, 48], F32), "xI": (S, [128, 144], I32),
+    "kF": (S, [128, 144], F32), "kL": (S, [128, 144], U16), "msg": (S, [128, 48], U16), "msgL": (S, [128, 48], U16),
+    "cntL": (S, [128, 32], BF), "Bv": (S, [128, 768], F32), "tv": (S, [128, 768], F32), "ys": (S, [128, 768], BF),
+    "Yl": (S, [128, 784], BF), "yo": (S, [128, 768], BF), "X": (S, [128, 768], F16), "pm": (S, [128, 48], F32),
+    "sg": (S, [128, 48], F32), "sigU": (S, [128, 48], U16), "co": (S, [128, 4], F32),
+    "P0": (P, [128, 512], F32), "P1": (P, [128, 512], F32), "P2": (P, [128, 512], F32), "P3": (P, [128, 512], F32),
+    "P4": (P, [128, 512], F32), "P5": (P, [128, 512], F32), "P6": (P, [128, 512], F32), "P7": (P, [128, 512], F32),
+}
+NDMA = 24
+SEMAPHORES = ["qg", "qv", "qs", "qt", "rl", "vp0", "vp1", "vs", "vf", "ts", "to", "pa", "ca", "ma", "ya"] + ["d%d" % i for i in range(NDMA)]
+LN8 = math.log(8.0)
+DIG = sum(8 ** k for k in range(8))
+
+
+def msk(es):
+    return sum(1 << e for e in es)
+
+
+def relay_of(q, cores, topo):
+    far = [c for c in cores if c not in topo.cores_of(cores[q])][0]
+    return [c for c in topo.cores_of(far) if c not in cores and topo.die(c) == topo.die(cores[q]) and topo.may_write(cores[q], c)][0]
+
+
+def val_half(T, q, h):
+    c0 = V0 + 2048 * q + 1024 * h
+    return T.allv[:, c0:c0 + 1024]
+
+
+def relay_program(g, core, q, cores, T, topo):
+    here = [c for c in cores if c in topo.cores_of(core)]
+    n_in = len(topo.engines(cores[q], core))
+    es = topo.engines(core, here[0])
+    k = len(es) // len(here)
+    for h in range(2):
+        g.wait_ge(T.sem["vp%d" % h], n_in)
+        trs = []
+        for i, c in enumerate(here):
+            rid, pid = topo.addr(c, core)
+            trs.append(RemoteDMATransfer(dst_ids=[DstId(rid=rid, pnc=pid)], dma_engine_mask=msk(es[k * i:k * (i + 1)]),
+                                         remote_sem=T.sem.vf, src=val_half(T, q, h), dst=val_half(T, q, h)))
+        g.remote_dma_fused(trs, local_sem=T.sem.rl)
+    g.wait_ge(T.sem.rl, 2 * k * len(here))
+
+
+def rank_program(g, core, T, topo):
+    cores = list(T.cores)
+    N = len(cores)
+    r = T.rank_of(core)
+    if r is None:
+        for q in range(N):
+            if relay_of(q, cores, topo) == core:
+                relay_program(g, core, q, cores, T, topo)
+        return
+    others = [q for q in range(N) if q != r]
+    sib = [q for q in others if cores[q] in topo.cores_of(core)][0]
+    far = [q for q in others if q != sib]
+    peer = [q for q in far if topo.die(cores[q]) == topo.die(core)][0]
+    sibpeer = [q for q in far if q != peer][0]
+    off_eng = topo.engines(core, cores[peer])
+    on_eng = [e for e in topo.engines(core, cores[sib]) if e not in off_eng]
+    half = len(off_eng) // 2
+    n_off, n_on = len(off_eng), len(on_eng)
+    n_vf = sum(2 * (len(topo.engines(relay_of(q, cores, topo), core)) // 2) for q in far)
+
+    Q = {"g": g, "v": g.vector, "s": g.scalar, "t": g.tensor, "y": g.sync}
+    known = {k: {} for k in Q}
+    count = {}
+    wr, rd = {}, {}
+    ndma = [0]
+
+    def need(q, ev):
+        name, val, snap = ev
+        if known[q].get(name, 0) >= val:
+            return
+        Q[q].wait_ge(T.sem[name], val)
+        known[q][name] = val
+        for k, x in snap.items():
+            if known[q].get(k, 0) < x:
+                known[q][k] = x
+
+    def before(q, R, W):
+        evs = []
+        for t in list(R) + list(W):
+            evs += wr.get(t, [])
+        for t in W:
+            evs += rd.get(t, [])
+        for ev in sorted(evs, key=lambda e: -e[1]):
+            need(q, ev)
+
+    def after(ev, R, W):
+        for t in W:
+            wr[t] = [ev]
+            rd[t] = []
+        for t in R:
+            rd.setdefault(t, []).append(ev)
+
+    def do(q, calls, R, W):
+        before(q, R, W)
+        for c in calls[:-1]:
+            c()
+        name = "q" + q
+        calls[-1]().then_inc(T.sem[name], 1)
+        count[name] = count.get(name, 0) + 1
+        after((name, count[name], dict(known[q])), R, W)
+
+    def dma(q, out, in_, R, W):
+        before(q, R, W)
+        name = "d%d" % ndma[0]
+        ndma[0] += 1
+        Q[q].dma_start(out, in_).then_inc(T.sem[name], 16)
+        count[name] = 16
+        after((name, 16, dict(known[q])), R, W)
+
+    def send(items, R):
+        before("g", R, [])
+        trs = []
+        for c, es, sem, src, dst in items:
+            rid, pid = topo.addr(c, core)
+            trs.append(RemoteDMATransfer(dst_ids=[DstId(rid=rid, pnc=pid)], dma_engine_mask=msk(es), remote_sem=T.sem[sem], src=src, dst=dst))
+            count["rl"] = count.get("rl", 0) + len(es)
+        g.remote_dma_fused(trs, local_sem=T.sem.rl)
+
+    def three(sem_on, sem_off, src, dst):
+        return [(cores[peer], off_eng[:half], sem_off, src(peer), dst), (cores[sibpeer], off_eng[half:], sem_off, src(sibpeer), dst),
+                (cores[sib], on_eng, sem_on, src(sib), dst)]
+
+    for tok, sem, val in (("vs", "vs", 2 * n_on), ("vf", "vf", n_vf),
+                          ("land_s", "ts", n_on), ("land_o", "to", 2 * n_off), ("ML", "pa", n_on + n_off), ("cntL", "ca", n_on + n_off),
+                          ("msgL", "ma", n_on + n_off), ("Yl_r", "ya", n_on + n_off)):
+        wr[tok] = [(sem, val, {})]
+        count[sem] = val
+
+    v, s, t = g.vector, g.scalar, g.tensor
+
+    def ts(out, in0, s1, s2, o0, o1, R, W):
+        if o1 is None:
+            do("v", [lambda: v.tensor_scalar(out, in0, s1, None, o0)], R, W)
+        else:
+            do("v", [lambda: v.tensor_scalar(out, in0, s1, s2, o0, o1)], R, W)
+
+    def tt(out, a, b, op, R, W):
+        do("v", [lambda: v.tensor_tensor(out, a, b, op)], R, W)
+
+    def cp(out, a, R, W):
+        do("v", [lambda: v.tensor_copy(out, a)], R, W)
+
+    def ms(ap, c, W):
+        do("v", [lambda: v.memset(ap, c)], [], W)
+
+    def scan(out, a, b, init, o0, o1, R, W):
+        do("v", [lambda: v.tensor_tensor_scan(out, a, b, init, o0, o1)], R, W)
+
+    def act(out, a, fn, R, W, bias=0.0, scale=1.0):
+        if bias == 0.0 and scale == 1.0:
+            do("s", [lambda: s.activation(out, a, fn)], R, W)
+        else:
+            do("s", [lambda: s.activation(out, a, fn, bias=bias, scale=scale)], R, W)
+
+    def mm(groups, R, W):
+        calls = []
+        for out, a, b, st, sp in groups:
+            calls.append(lambda out=out, a=a, b=b, st=st, sp=sp: t.matmul(out, a, b, st, sp))
+        do("t", calls, R, W)
+
+    def wrap(out, Hm, src, R, W):
+        mm([(out, Hm[:, 15 - b:143 - b], src[:, b::16], b == 0, b == 15) for b in range(16)], R, W)
+
+    def iota(out, pat, base, cm, W, flt=True):
+        if flt:
+            do("g", [lambda: g.iota(out, pat, base, cm, allow_small_or_imprecise_dtypes=True)], [], W)
+        else:
+            do("g", [lambda: g.iota(out, pat, base, cm)], [], W)
+
+    def sel(out, a, pat, op, base, cm, R, W, fill=0.0):
+        do("g", [lambda: g.affine_select(out, a, pat, op, fill, base, cm)], R, W)
+
+    AND, SHR = ALU.bitwise_and, ALU.logical_shift_right
+    GM = [[-16, 8], [0, 16]]
+
+    dma("y", T.entI[:], T.ent[:], [], ["entI"])
+    dma("s", T.attI[:], T.att[:], [], ["attI"])
+    ms(T.zero[:], 0.0, ["zero"])
+    ms(T.clsI[:], 0, ["clsI0", "clsI1", "clsI2", "clsI3"])
+    iota(T.pay[:, 0:512], [[1, 32], [128, 16]], V0 + 2048 * r, 0, ["pay0"])
+    dma("s", T.formI[:], T.form[:], [], ["formI"])
+    for k in range(2):
+        dma("ys"[k], T.win[0:128:16, 8192 * k:8192 * (k + 1)], T.zero[:], ["zero"], ["win%d" % k])
+    for h in range(2):
+        dma("y", val_half(T, r, h), T.val[:, 1024 * h:1024 * (h + 1)], [], ["own%d" % h])
+    for k in range(1, 4):
+        act(T.pay[:, 512 * k:512 * (k + 1)], T.pay[:, 0:512], ACT.Identity, ["pay0"], ["pay%d" % k], bias=32.0 * k)
+    act(T.c125[:], T.pay[:, 0:256], ACT.Identity, ["pay0"], ["c125"], bias=-0.125, scale=0.0)
+    for G in range(4):
+        dma("y", T.clsI[32 * G:32 * G + 16, :], T.cls[2 * G:2 * G + 2, :], [], ["clsI%d" % G])
+    ms(T.ones[:], 1.0, ["ones"])
+    ms(T.allv[:, 0:V0], 0.0, ["allv0"])
+    ms(T.keep3[:, :, 0:8], 8.0, ["keep3a"])
+    ms(T.keep3[:, :, 8:16], 0.125, ["keep3b"])
+    ms(T.c8192[:], 8192.0, ["c8192"])
+    ms(T.H[:], 0.0, ["H"])
+    cp(T.keep[:], T.keep3[:], ["keep3a", "keep3b"], ["keep"])
+    ms(T.H[:, 15::16], 1.0, ["H"])
+    ms(T.keep[:, 0::8], 0.0, ["keep"])
+    ms(T.Yl[:, 768:784], 0.0, ["Yl_z"])
+    ms(T.EL[:, 768:776], -1.0, ["EL_z"])
+    ms(T.Et[:, 1024:1032], -1.0, ["Et_z"])
+    iota(T.pI[:], [[0, 8]], 0, 1, ["pI"], False)
+    iota(T.mI[:], [[1, 32]], 0, 0, ["mI"], False)
+    sel(T.Id[:], T.ones[:], [[-1, 128]], ALU.is_equal, 0, 1, ["ones"], ["Id"])
+    iota(T.TR[:], [[1, 16]], 768, 0, ["TR"])
+    iota(T.sw[:], [[16, 48]], 0, 0, ["sw"])
+    iota(T.Et[:, 0:1024], [[1, 1024]], 0, 0, ["Et"])
+
+    ts(T.kI[:], T.entI[:], 1025, None, ALU.mult, None, ["entI"], ["kI"])
+    ts(T.fI[:, 0:128], T.formI[:], 15, None, AND, None, ["formI"], ["fI0"])
+    ts(T.kI[:], T.kI[:], 0x3FF0, None, AND, None, ["kI"], ["kI"])
+    ts(T.fI[:, 128:256], T.formI[:], 4, 15, SHR, AND, ["formI"], ["fI1"])
+    tt(T.kI[:], T.kI[:], T.attI[:], ALU.add, ["kI", "attI"], ["kI"])
+    ts(T.fI[:, 256:384], T.formI[:], 8, None, SHR, None, ["formI"], ["fI2"])
+    cp(T.kU[:], T.kI[:], ["kI"], ["kU"])
+    cp(T.fB[:], T.fI[:], ["fI0", "fI1", "fI2"], ["fB"])
+    cp(T.win[:, 0:16384].indirect(T.kU[:, 0:128]), T.pay[:], ["kU", "pay0", "pay1", "pay2", "pay3"], ["win0", "win1"])
+
+    for h in range(2):
+        ap = val_half(T, r, h)
+        send([(relay_of(r, cores, topo), off_eng, "vp%d" % h, ap, ap), (cores[sib], on_eng, "vs", ap, ap)], ["own%d" % h])
+    sel(T.TRI[:], T.c8192[:], GM, ALU.is_ge, 0, 1, ["c8192"], ["TRI"])
+    sel(T.DT[:], T.ones[:], [[-4, 32], [0, 4]], ALU.is_ge, 0, 1, ["ones"], ["DT"])
+    sel(T.H[:, 15::16], T.H[:, 15::16], [[-16, 9]], ALU.is_ge, 0, 1, ["H"], ["H"])
+    sel(T.TRI[:], T.TRI[:], [[1, 128]], ALU.is_ge, 0, -1, ["TRI"], ["TRI"])
+    sel(T.H[:, 15::16], T.H[:, 15::16], [[16, 9]], ALU.is_ge, 15, -1, ["H"], ["H"])
+    sel(T.TRI[:], T.TRI[:], [[1, 128]], ALU.not_equal, 0, -1, ["TRI"], ["TRI"], fill=4096.0)
+
+    for h in range(2):
+        act(T.E1[:, :, h, :], T.fB[:], ACT.Exp, ["fB"], ["E1%d" % h], bias=7 * LN8, scale=-LN8)
+    for h in range(2):
+        act(T.E2[:, :, h, :], T.fB[:], ACT.Exp, ["fB"], ["E2%d" % h], bias=-8 * LN8, scale=LN8)
+    for i in range(3):
+        for h in range(2):
+            act(T.fS[:, 8 * i:8 * (i + 1), h, :], T.fB[:, 8 * i:8 * (i + 1), :], ACT.Identity, ["fB"], ["fS%d%d" % (i, h)], scale=float(16 ** i))
+    for k, E in enumerate((T.E1, T.E2)):
+        o = T.P0[:, 256 * k:256 * (k + 1)]
+        mm([(o, T.Id[:], T.c125[:], True, False)] + [(o, T.Id[:], E[:, 8 * i:8 * (i + 1)], False, i == 2) for i in range(3)],
+           ["Id", "c125", "E%d0" % (k + 1), "E%d1" % (k + 1)], ["P0"])
+    mm([(T.P1[:, 0:256], T.Id[:], T.fS[:, 8 * i:8 * (i + 1)], i == 0, i == 2) for i in range(3)],
+       ["Id"] + ["fS%d%d" % (i, h) for i in range(3) for h in range(2)], ["P1"])
+    act(T.tabD[:, 0:512], T.P0[:, 0:512], ACT.Identity, [], ["P0", "tabD0"], bias=float(3 * DIG))
+    act(T.tabD[:, 512:768], T.P1[:, 0:256], ACT.Identity, [], ["P1", "tabD1"], bias=-6144.0)
+
+    dma("y", T.tl[:], T.win[0:128:16, :], ["win0", "win1"], ["tl"])
+
+    def tpart(q, es, sem, h):
+        return (cores[q], es, sem, T.tl[:, 256 * q + 128 * h:256 * q + 128 * (h + 1)], T.land[:, 256 * r + 128 * h:256 * r + 128 * (h + 1)])
+    send([tpart(peer, off_eng[:half], "to", 0), tpart(sibpeer, off_eng[half:], "to", 0),
+          tpart(sib, on_eng[:n_on // 2], "ts", 0), tpart(sib, on_eng[n_on // 2:], "ts", 1)], ["tl"])
+    sel(T.DT[:], T.DT[:], [[1, 128]], ALU.is_gt, 0, -1, ["DT"], ["DT"])
+
+    ts(T.pJ[:, 1:2], T.pI[:, 0:1], 8, None, AND, None, ["pI"], ["pJ1"])
+    ts(T.clsI[:], T.clsI[:], 257, None, ALU.mult, None, [], ["clsI0", "clsI1", "clsI2", "clsI3"])
+    ts(T.pF[:, 1:2], T.pJ[:, 1:2], 2.0, None, ALU.mult, None, ["pJ1"], ["pF1"])
+    ts(T.clsI[:], T.clsI[:], 3, 0xEF, SHR, AND, [], ["clsI0"])
+    ts(T.pJ[:, 0:1], T.pI[:, 0:1], 15, None, AND, None, ["pI"], ["pJ0"])
+    ts(T.clsF[:], T.clsI[:], T.pF[:, 1:2], None, ALU.add, None, ["clsI0", "pF1"], ["clsF"])
+    do("v", [lambda: v.transpose(T.tabW[:], T.tabD[:])], ["tabD0", "tabD1"], ["tabW"])
+    do("v", [lambda: v.transpose(T.clsT[:], T.clsF[:])], ["clsF"], ["clsT"])
+    for gl in range(2):
+        cp(T.clsU[:, gl::2], T.clsT[:, 8 * gl:8 * gl + 8], ["clsT"], ["clsU%d" % gl])
+    cU = ["clsU0", "clsU1", "tabW"]
+    act(T.tabR[:, 512:768], T.tabW[:, 512:768].indirect(T.clsU[:, 0:16]), ACT.Copy, cU, ["tabR2"])
+    for k in range(2):
+        cp(T.tabR[:, 256 * k:256 * (k + 1)], T.tabW[:, 256 * k:256 * (k + 1)].indirect(T.clsU[:, 0:16]), cU, ["tabR%d" % k])
+    do("v", [lambda: v.transpose(T.tabT[:], T.tabR[:])], ["tabR0", "tabR1", "tabR2"], ["tabT"])
+    for h in range(2):
+        act(T.Pm[:, 512 * h:512 * (h + 1)], T.tl[:, 512 * h:512 * (h + 1)], ACT.Sign, ["tl"], ["Pm%d" % h])
+        scan(T.Ms[:, 512 * h:512 * (h + 1)], T.keep[:], T.Pm[:, 512 * h:512 * (h + 1)], 0.0, ALU.mult, ALU.add, ["keep", "Pm%d" % h], ["Ms%d" % h])
+    ts(T.Mc[:, :, 0:16], T.Ms[:, 7::16], -3.0, None, ALU.mult, None, ["Ms0", "Ms1"], ["McA"])
+    ts(T.Mc[:, :, 16:32], T.Ms[:, 15::16], -3.0 * 8 ** 7, None, ALU.mult, None, ["Ms0", "Ms1"], ["McB"])
+    send(three("pa", "pa", lambda q: T.Mc[:, q, :], T.ML[:, 32 * r:32 * (r + 1)]), ["McA", "McB"])
+    send([tpart(peer, off_eng[:half], "to", 1), tpart(sibpeer, off_eng[half:], "to", 1)], ["tl"])
+
+    act(T.neg[:], T.pay[:, 0:768], ACT.Identity, ["pay0", "pay1"], ["neg"], bias=-8192.0, scale=0.0)
+    act(T.Gw[:, 0:768], T.pay[:, 0:768], ACT.Identity, ["pay0", "pay1"], ["Gw"], bias=-8388608.0, scale=0.0)
+    act(T.Ww[:, 0:768], T.pay[:, 0:768], ACT.Identity, ["pay0", "pay1"], ["Ww"], bias=0.0, scale=0.0)
+    iota(T.wid[:], [[1, 16], [16, 16]], 0, 0, ["wid"])
+    sel(T.R[:], T.ones[:], GM, ALU.is_ge, -4 * r, 1, ["ones"], ["R"])
+    sel(T.R[:], T.R[:], [[16, 8], [0, 16]], ALU.is_ge, 4 * r + 3, -1, ["R"], ["R"])
+    for q in range(4):
+        sel(T.FS[:, 128 * q:128 * (q + 1)], T.R[:], [[64, 8], [1, 16]], ALU.is_gt, 16 * r - q, -4, ["R"], ["FS%d" % q])
+    cp(T.mU[:], T.mI[:], ["mI"], ["mU"])
+    cp(T.H16[:], T.H[:], ["H"], ["H16"])
+    ts(T.pJ[:, 2:3], T.pI[:, 0:1], 12, None, AND, None, ["pI"], ["pJ2"])
+    ts(T.pJ[:, 3:4], T.pI[:, 0:1], 3, None, AND, None, ["pI"], ["pJ3"])
+    ts(T.pF[:, 0:1], T.pJ[:, 0:1], 1.0, None, ALU.mult, None, ["pJ0"], ["pF0"])
+    ts(T.pF[:, 4:5], T.pJ[:, 0:1], 16.0, None, ALU.mult, None, ["pJ0"], ["pF4"])
+    ts(T.pF[:, 5:6], T.pJ[:, 0:1], 0.0, None, ALU.is_gt, None, ["pJ0"], ["pF5"])
+    ts(T.pF[:, 2:3], T.pJ[:, 2:3], 48.0, None, ALU.mult, None, ["pJ2"], ["pF2"])
+    ts(T.pF[:, 3:4], T.pJ[:, 3:4], 0.0, -768.0, ALU.is_equal, ALU.mult, ["pJ3"], ["pF3"])
+    ts(T.TR[:], T.TR[:], T.pF[:, 4:5], None, ALU.add, None, ["pF4"], ["TR"])
+    ts(T.sw[:], T.sw[:], T.pF[:, 0:1], None, ALU.add, None, ["pF0"], ["sw"])
+    ts(T.cvec[:, 0:1], T.pF[:, 3:4], 192.0, T.pF[:, 5:6], ALU.add, ALU.mult, ["pF3", "pF5"], ["cvec"])
+    ms(T.DD[:], 0.0, ["DD"])
+    act(T.Rn[:], T.R[:], ACT.Identity, ["R"], ["Rn"], scale=-1.0)
+
+    def blk(A, q, n=256):
+        return A[:, n * q:n * (q + 1)]
+    pm_ = T.P1[:, 0:256]
+    tt(pm_, blk(T.tl, r), blk(T.land, sib), ALU.add, ["tl", "land_s"], ["P1"])
+    tt(T.Mt[:], T.Mc[:, r, :], blk(T.ML, sib, 32), ALU.add, ["McA", "McB", "ML"], ["Mt"])
+    tt(blk(T.ML, r, 32), blk(T.ML, peer, 32), blk(T.ML, sibpeer, 32), ALU.add, ["ML"], ["MLr"])
+    tt(T.Mt[:], T.Mt[:], blk(T.ML, r, 32), ALU.add, ["MLr"], ["Mt"])
+    tt(T.U[:], T.Mt[:, 0:32].indirect(T.mU[:, 0:32]), T.tabT[:, 0:512], ALU.add, ["Mt", "mU", "tabT"], ["U0", "U1"])
+    ts(T.U[:, 0:256], T.U[:, 0:256], 4 * DIG, None, AND, None, [], ["U0"])
+    ts(T.U[:, 256:512], T.U[:, 256:512], 4 * DIG, 1, AND, SHR, [], ["U1"])
+    tt(T.ok[:], T.U[:, 0:256], T.U[:, 256:512], ALU.is_equal, ["U0", "U1"], ["ok"])
+
+    nw = T.P3[:, 0:16]
+    wrap(nw, T.H, T.ok, ["H", "ok"], ["P3"])
+    mm([(T.P2[:, 0:256], T.TRI[:], T.ok[:], True, True)], ["TRI", "ok"], ["P2"])
+    tt(pm_, pm_, blk(T.land, peer), ALU.add, ["land_o"], ["P1"])
+    tt(T.mg[:], pm_, blk(T.land, sibpeer), ALU.add, ["land_o"], ["P1", "mg"])
+    cp(T.posU[:], T.mg[:], ["mg"], ["posU"])
+    act(T.VT[:], T.allv[:, 0:V0 + 8192].indirect(T.posU[:, 0:256]), ACT.Copy,
+        ["posU", "allv0", "own0", "own1", "vs", "vf"], ["VT"])
+    scan(T.incl[:], T.ones[:, 0:16], nw, 0.0, ALU.mult, ALU.add, ["ones"], ["P3", "incl"])
+    mm([(T.P4[:, 0:1], T.DT[:], T.incl[:, 15:16], True, True)], ["DT", "incl"], ["P4"])
+    send(three("ca", "ca", lambda q: T.incl[:, 8:16], T.cntL[:, 8 * r:8 * r + 8]), ["incl"])
+    for q in range(4):
+        sel(T.DD[:, 128 * q + q:128 * (q + 1):4], T.R[:, q::4], [[16, 8], [1, 4]], ALU.is_gt, 4 * r, -1, ["R", "DD"], ["DDa%d" % q])
+        q1 = (q + 1) % 4
+        sel(T.DD[:, 128 * q + q1:128 * (q + 1):4], T.Rn[:, q1::4], [[16, 8], [1, 4]], ALU.is_gt if q1 == 0 else ALU.is_ge, 4 * r, -1,
+            ["Rn", "DD"], ["DDb%d" % q])
+    for q in range(4):
+        sel(T.RA[:, 128 * q:128 * (q + 1)], T.ones[:], GM, ALU.is_equal, -4 * r - q, 1, ["ones"], ["RA%d" % q])
+    ts(T.tz[:], nw, 0.0, None, ALU.is_equal, None, [], ["P3r", "tz"])
+    tt(T.ex[:], T.incl[:], nw, ALU.subtract, ["incl"], ["P3s", "ex"])
+    tt(T.tz[:], T.tz[:], T.TR[:], ALU.mult, ["TR"], ["tz"])
+    tt(T.ex[:], T.ex[:], T.tz[:], ALU.max, ["tz"], ["ex"])
+    ts(T.offU[:], T.ex[:], T.P4[:, 0:1], T.pF[:, 2:3], ALU.add, ALU.add, ["ex", "pF2"], ["P4", "offU"])
+    tt(T.Gt[:], T.tabT[:, 512:768], T.P2[:, 0:256], ALU.add, ["tabT"], ["P2", "Gt"])
+    cp(T.Ww[:, 0:1792].indirect(T.offU[:, 0:16]), T.wid[:], ["offU", "wid"], ["Ww"])
+    cp(T.Gw[:, 0:1792].indirect(T.offU[:, 0:16]), T.Gt[:], ["offU", "Gt"], ["Gw"])
+    scan(T.Ws[:], T.Ww[:, 0:768], T.Ww[:, 0:768], 0.0, ALU.max, ALU.max, ["Ww"], ["Ws"])
+    scan(T.Ds[:], T.neg[:], T.Gw[:, 0:768], -8388608.0, ALU.add, ALU.max, ["Gw", "neg"], ["Ds"])
+    wrap(T.P5[:, 0:48], T.H, T.Ws, ["H", "Ws"], ["P5"])
+    ts(T.phi[:], T.Ds[:], -2048.0, 2048.0, ALU.max, ALU.min, ["Ds"], ["phi"])
+    wrap(T.P6[:, 0:48], T.H16, T.phi, ["H16", "phi"], ["P6"])
+    ts(T.wI[:], T.P5[:, 0:48], 16.0, None, ALU.mult, None, [], ["P5", "wI"])
+    ts(T.wI[:], T.wI[:], 3840, None, AND, None, [], ["wI"])
+    ts(T.b15[:], T.wI[:], 15.0, None, ALU.add, None, ["wI"], ["b15"])
+    ts(T.e16[:], T.wI[:], 0.0625, float(256 * r + 15), ALU.mult, ALU.add, ["wI"], ["e16"])
+    ts(T.S16[:], T.P6[:, 0:48], 32768.0, 16.0, ALU.add, ALU.mult, [], ["P6", "S16"])
+    ts(T.ab[:], T.S16[:], 16, None, SHR, None, ["S16"], ["ab"])
+    ts(T.xI[:, 48:96], T.S16[:], 4, 240, SHR, AND, ["S16"], ["xI1"])
+    tt(T.b15[:], T.b15[:], T.ab[:], ALU.subtract, ["ab"], ["b15"])
+    ts(T.xI[:, 0:48], T.S16[:], 240, None, AND, None, ["S16"], ["xI0"])
+    tt(T.kF[:, 48:96], T.xI[:, 48:96], T.b15[:], ALU.add, ["xI1", "b15"], ["kF1"])
+    ts(T.xI[:, 96:144], T.S16[:], 8, 240, SHR, AND, ["S16"], ["xI2"])
+    cp(T.kL[:, 48:96], T.kF[:, 48:96], ["kF1"], ["kL1"])
+    for i in (0, 2):
+        tt(T.kF[:, 48 * i:48 * (i + 1)], T.xI[:, 48 * i:48 * (i + 1)], T.b15[:], ALU.add, ["xI%d" % i, "b15"], ["kF%d" % i])
+    ts(T.fm[:], T.S16[:], 65535, None, AND, None, ["S16"], ["fm"])
+    tt(T.e16[:], T.e16[:], T.ab[:], ALU.subtract, ["ab"], ["e16"])
+    for i in (0, 2):
+        cp(T.kL[:, 48 * i:48 * (i + 1)], T.kF[:, 48 * i:48 * (i + 1)], ["kF%d" % i], ["kL%d" % i])
+    ts(T.tp[:], T.fm[:], 0.0, 1024.0, ALU.is_equal, ALU.mult, ["fm"], ["tp"])
+
+    def cn(q):
+        return T.incl[:, 15:16] if q == r else T.cntL[:, 8 * q + 7:8 * q + 8]
+    DDs = ["DDa%d" % q for q in range(4)] + ["DDb%d" % q for q in range(4)]
+    mm([(T.P3[:, 0:1], T.FS[:, 128 * q:128 * (q + 1)], cn(q), q == 0, q == 3) for q in range(4)]
+       + [(T.P3[:, 1:2], T.Id[:], T.cvec[:, 0:1], True, False)]
+       + [(T.P3[:, 1:2], T.DD[:, 128 * q:128 * (q + 1)], cn(q), False, q == 3) for q in range(4)]
+       + [(T.P3[:, 2:3], T.R[:], cn(q), q == 0, q == 3) for q in range(4)],
+       ["cntL", "incl", "cvec", "R", "FS0", "FS1", "FS2", "FS3"] + DDs, ["P3", "P3r", "P3s"])
+
+    lo = min(far)
+    parts = [(lo, 2, T.ys)] if max(far) == lo + 1 else [(far[0], 1, T.ys), (far[1], 1, T.ys)]
+    parts += [(sib, 1, T.ys), (r, 1, T.Yl)]
+    VTw = T.VT[:, 0:4096]
+    for d, n, dst in parts:
+        act(T.Bv[:, 192 * d:192 * (d + n)], VTw.indirect(T.kL[:, 48 + 12 * d:48 + 12 * (d + n)]), ACT.Copy, ["VT", "kL1"], ["Bv%d" % d])
+    tt(T.tp[:], T.tp[:], T.e16[:], ALU.max, ["e16"], ["tp"])
+    cp(T.msg[:], T.tp[:], ["tp"], ["msg"])
+    send(three("ma", "ma", lambda q: T.msg[:, 12 * q:12 * (q + 1)], T.msgL[:, 12 * r:12 * (r + 1)]), ["msg"])
+    dma("y", T.msgL[:, 12 * r:12 * (r + 1)], T.msg[:, 12 * r:12 * (r + 1)], ["msg"], ["msgO"])
+    mine = T.Yl[:, 192 * r:192 * (r + 1)]
+    for d, n, dst in parts:
+        a, b = 192 * d, 192 * (d + n)
+        if d == r:
+            ts(T.X[:], T.Et[:, 0:768], T.P3[:, 0:1], T.P3[:, 1:2], ALU.is_ge, ALU.mult, ["Et"], ["P3", "X"])
+            wrap(T.P5[:, 0:48], T.H16, T.X, ["H16", "X"], ["P5"])
+            ts(T.pm[:], T.sw[:], T.P3[:, 2:3], 768.0, ALU.is_ge, ALU.mult, ["sw"], ["P3", "pm"])
+        tt(T.tv[:, a:b], VTw.indirect(T.kL[:, 12 * d:12 * (d + n)]), T.Bv[:, a:b], ALU.subtract, ["VT", "kL0", "Bv%d" % d], ["tv%d" % d])
+        tt(dst[:, a:b], VTw.indirect(T.kL[:, 96 + 12 * d:96 + 12 * (d + n)]), T.tv[:, a:b], ALU.add, ["VT", "kL2", "tv%d" % d], ["ys%d" % d])
+        if d == parts[-3][0]:
+            send([(cores[peer], off_eng[:half], "ya", T.ys[:, 192 * peer:192 * (peer + 1)], mine),
+                  (cores[sibpeer], off_eng[half:], "ya", T.ys[:, 192 * sibpeer:192 * (sibpeer + 1)], mine)], ["ys%d" % p[0] for p in parts[:-2]])
+        if d == sib:
+            send([(cores[sib], on_eng, "ya", T.ys[:, a:b], mine)], ["ys%d" % d])
+    mm([(T.P4[:, al:al + 1], T.RA[:, 128 * al:128 * (al + 1)], cn(q), q == 0, q == 3) for al in range(4) for q in range(4)],
+       ["cntL", "incl", "RA0", "RA1", "RA2", "RA3"], ["P4"])
+    act(T.EL[:, 0:768], T.Et[:, 0:1032].indirect(T.msgL[:, 0:48]), ACT.Copy, ["Et", "Et_z", "msgL", "msgO"], ["EL"])
+
+    tt(T.sg[:], T.P5[:, 0:48], T.sw[:], ALU.add, ["sw"], ["P5", "sg"])
+    tt(T.sg[:], T.sg[:], T.pm[:], ALU.max, ["pm"], ["sg"])
+    ts(T.sigU[:], T.sg[:], 768.0, None, ALU.min, None, ["sg"], ["sigU"])
+    cp(T.co[:], T.P4[:, 0:4], [], ["P4", "co"])
+    dma("y", T.cnt[:], T.co[0:128:16, :], ["co"], ["cnt"])
+    act(T.wo[:], T.EL[:, 0:776].indirect(T.sigU[:, 0:48]), ACT.Copy, ["EL", "EL_z", "sigU"], ["wo"])
+    dma("s", T.who[:], T.wo[0:128:16, :], ["wo"], ["who"])
+    YR = ["sigU", "Yl_z", "Yl_r", "ys%d" % r]
+    cp(T.yo[:, 0:448], T.Yl[:, 0:784].indirect(T.sigU[:, 0:28]), YR, ["yo0"])
+    dma("y", T.y[:, 0:448], T.yo[:, 0:448], ["yo0"], ["y0"])
+    act(T.yo[:, 448:768], T.Yl[:, 0:784].indirect(T.sigU[:, 28:48]), ACT.Copy, YR, ["yo1"])
+    dma("s", T.y[:, 448:768], T.yo[:, 448:768], ["yo1"], ["y1"])
+    for name, val in count.items():
+        need("g", (name, val, {}))

@@ -1,74 +1,92 @@
-import math
 from concourse.bass import DstId, RemoteDMATransfer
 from concourse.mybir import AluOpType as ALU, ActivationFunctionType as ACT
 
 S, P = "sbuf", "psum"
 F32, BF, I32, U16, F16 = "float32", "bfloat16", "int32", "uint16", "float16"
-V0 = 32
+KV, KS = 62, 66
+NV = 16 * KV
+REG, GAP, MID = 2080, 16, 503
+WIDE = 3584
 SCRATCH = {
     "entI": (S, [128, 128], I32), "attI": (S, [128, 128], I32), "kI": (S, [128, 128], I32), "kU": (S, [128, 128], U16),
-    "formI": (S, [128, 128], I32), "fI": (S, [128, 384], I32), "fB": (S, [128, 24, 16], BF),
-    "fS": (S, [128, 24, 2, 16], BF), "E1": (S, [128, 24, 2, 16], BF), "E2": (S, [128, 24, 2, 16], BF),
-    "tabD": (S, [128, 768], F32), "tabW": (S, [128, 768], F32), "tabR": (S, [128, 768], F32), "tabT": (S, [128, 768], F32),
+    "formI": (S, [128, 2, 64], I32), "fI": (S, [128, 3, 2, 64], I32), "fB": (S, [128, 12, 2, 16], BF),
+    "E1": (S, [128, 384], BF), "E2": (S, [128, 384], BF), "tabW": (S, [128, 384], F32), "tabR": (S, [128, 512], F32),
+    "frm": (S, [128, 256], F32), "frmT": (S, [128, 8, 2, 16], F32),
     "clsI": (S, [128, 32], I32), "clsF": (S, [128, 32], F32), "clsT": (S, [128, 32], F32), "clsU": (S, [128, 16], U16),
-    "zero": (S, [128, 512], F32), "win": (S, [128, 16384], F32), "pay": (S, [128, 2048], F32),
-    "tl": (S, [128, 1024], F32), "land": (S, [128, 1024], F32), "mg": (S, [128, 256], F32), "posU": (S, [128, 256], U16),
-    "Pm": (S, [128, 1024], BF), "Ms": (S, [128, 1024], F32), "keep3": (S, [128, 32, 16], BF), "keep": (S, [128, 512], BF),
-    "Mc": (S, [128, 4, 32], F32), "ML": (S, [128, 128], F32), "Mt": (S, [128, 32], F32),
-    "allv": (S, [128, V0 + 8192], BF), "VT": (S, [128, 4096], BF), "U": (S, [128, 512], I32), "ok": (S, [128, 256], BF),
-    "Gt": (S, [128, 256], F32), "incl": (S, [128, 16], BF), "ex": (S, [128, 16], F32),
-    "tz": (S, [128, 16], F32), "offU": (S, [128, 16], U16), "Gw": (S, [128, 1792], F32), "Ww": (S, [128, 1792], BF),
-    "Ds": (S, [128, 768], F32), "Ws": (S, [128, 768], BF), "phi": (S, [128, 768], F16), "neg": (S, [128, 768], BF),
-    "c125": (S, [128, 256], BF), "wid": (S, [128, 256], BF),
-    "ones": (S, [128, 128], BF), "c8192": (S, [128, 128], BF), "Id": (S, [128, 128], BF), "TRI": (S, [128, 128], BF),
-    "DT": (S, [128, 128], BF), "H": (S, [128, 144], BF), "H16": (S, [128, 144], F16), "R": (S, [128, 128], BF),
-    "Rn": (S, [128, 128], BF), "FS": (S, [128, 512], BF), "DD": (S, [128, 512], BF), "RA": (S, [128, 512], BF),
-    "pI": (S, [128, 8], I32), "pJ": (S, [128, 8], I32), "pF": (S, [128, 8], F32), "cvec": (S, [128, 2], BF),
-    "mI": (S, [128, 32], I32), "mU": (S, [128, 32], U16), "TR": (S, [128, 16], F32), "sw": (S, [128, 48], F32),
-    "Et": (S, [128, 1032], F32), "EL": (S, [128, 776], F32), "wo": (S, [128, 768], F32),
-    "wI": (S, [128, 48], I32), "b15": (S, [128, 48], F32), "e16": (S, [128, 48], F32), "S16": (S, [128, 48], I32),
-    "ab": (S, [128, 48], I32), "fm": (S, [128, 48], I32), "tp": (S, [128, 48], F32), "xI": (S, [128, 144], I32),
-    "kF": (S, [128, 144], F32), "kL": (S, [128, 144], U16), "msg": (S, [128, 48], U16), "msgL": (S, [128, 48], U16),
-    "cntL": (S, [128, 32], BF), "Bv": (S, [128, 768], F32), "tv": (S, [128, 768], F32), "ys": (S, [128, 768], BF),
-    "Yl": (S, [128, 784], BF), "yo": (S, [128, 768], BF), "X": (S, [128, 768], F16), "pm": (S, [128, 48], F32),
-    "sg": (S, [128, 48], F32), "sigU": (S, [128, 48], U16), "co": (S, [128, 4], F32),
+    "zero": (S, [128, 512], F32), "zeroB": (S, [128, 512], BF), "winV": (S, [128, 16384], BF), "winS": (S, [128, 16384], F32), "kJ": (S, [128, 128], I32),
+    "payV": (S, [128, NV], F32), "payS": (S, [128, 16 * KS], F32), "baseV": (S, [128, 8 * KV // 2], F32), "baseS": (S, [128, 16 * KS // 3], F32),
+    "tlV": (S, [128, 1024], BF), "tlS": (S, [128, 1024], F32), "tq": (S, [128, 1024], F16), "land": (S, [128, 1024], F16),
+    "pres": (S, [128, 1024], BF), "clp": (S, [128, 1024], F16), "posU": (S, [128, 256], U16),
+    "allv": (S, [128, 4 * REG], BF), "VT": (S, [128, 4096], BF), "U": (S, [128, 512], I32), "ok": (S, [128, 256], BF),
+    "okT": (S, [128, 8, 2, 16], BF), "cum": (S, [128, 272], BF), "Gt": (S, [128, 256], F32),
+    "tz": (S, [128, 16], F32), "offU": (S, [128, 16], U16), "Gw": (S, [128, WIDE], F32), "Ww": (S, [128, WIDE], BF),
+    "Ds": (S, [128, 768], F32), "Ws": (S, [128, 768], BF), "phi": (S, [128, 768], F16),
+    "wid": (S, [128, 256], BF), "ones": (S, [128, 512], BF), "mone": (S, [128, 768], BF), "lo": (S, [128, 256], BF),
+    "Id": (S, [128, 160], BF), "IdS": (S, [128, 6, 128], BF), "Id16": (S, [128, 2, 128], F16), "GB": (S, [128, 160], BF),
+    "STR": (S, [128, 128], BF), "INC": (S, [128, 160], BF), "DT": (S, [128, 128], BF), "DD": (S, [128, 128], BF),
+    "TM": (S, [128, 2, 160], BF), "IM": (S, [128, 2, 160], F32), "Wn": (S, [128, 2, 128], BF), "Sel": (S, [128, 512], BF),
+    "dI": (S, [128, 132], I32), "dA": (S, [128, 132], BF), "dB": (S, [128, 128], BF),
+    "w0": (S, [128, 64], F32), "w1": (S, [128, 64], F32), "rows": (S, [128, 224], F32), "cols": (S, [128, 224], F32),
+    "H": (S, [128, 144], BF), "H4": (S, [128, 144], BF), "Hn": (S, [128, 144], F16), "TR": (S, [128, 16], F32),
+    "sw": (S, [128, 48], F32), "sw16": (S, [128, 48], F16),
+    "Et": (S, [128, 1024], F32), "EL": (S, [128, 776], F32), "wo": (S, [128, 768], F32),
+    "Z": (S, [128, 48], I32), "zI": (S, [128, 5, 48], I32), "kF": (S, [128, 96], I32), "kL": (S, [128, 144], U16),
+    "msg": (S, [128, 48], U16), "msgL": (S, [128, 64], U16), "cntL": (S, [128, 32], BF), "nS": (S, [128, 8], BF), "cv": (S, [128, 8], BF),
+    "Bv": (S, [128, 768], F32), "tv": (S, [128, 768], F32), "ys": (S, [128, 768], BF),
+    "Yl": (S, [128, 784], BF), "yo": (S, [128, 768], BF), "X": (S, [128, 768], F16), "sigU": (S, [128, 48], U16), "co": (S, [128, 4], F32),
     "P0": (P, [128, 512], F32), "P1": (P, [128, 512], F32), "P2": (P, [128, 512], F32), "P3": (P, [128, 512], F32),
     "P4": (P, [128, 512], F32), "P5": (P, [128, 512], F32), "P6": (P, [128, 512], F32), "P7": (P, [128, 512], F32),
 }
-NDMA = 24
-SEMAPHORES = ["qg", "qv", "qs", "qt", "rl", "vp0", "vp1", "vs", "vf", "ts", "to", "pa", "ca", "ma", "ya"] + ["d%d" % i for i in range(NDMA)]
-LN8 = math.log(8.0)
+NDMA = 40
+SEMAPHORES = ["qg", "qv", "qs", "qt", "rl", "va0", "va1", "vb0", "vb1", "vs", "vf", "ts", "to", "ca", "ma", "ya"] + ["d%d" % i for i in range(NDMA)]
 DIG = sum(8 ** k for k in range(8))
+POW0, POW1 = -70.10015395, -2.10671760
 
 
 def msk(es):
     return sum(1 << e for e in es)
 
 
-def relay_of(q, cores, topo):
-    far = [c for c in cores if c not in topo.cores_of(cores[q])][0]
-    return [c for c in topo.cores_of(far) if c not in cores and topo.die(c) == topo.die(cores[q]) and topo.may_write(cores[q], c)][0]
+def helpers(q, cores, topo):
+    return [c for c in topo.cores_of(cores[q]) if c not in cores and topo.die(c) == topo.die(cores[q])][:2]
 
 
-def val_half(T, q, h):
-    c0 = V0 + 2048 * q + 1024 * h
-    return T.allv[:, c0:c0 + 1024]
+def roles(r, cores, topo):
+    others = [q for q in range(len(cores)) if q != r]
+    sib = [q for q in others if cores[q] in topo.cores_of(cores[r])][0]
+    far = [q for q in others if q != sib]
+    peer = [q for q in far if topo.die(cores[q]) == topo.die(cores[r])][0]
+    return sib, far, peer
 
 
-def relay_program(g, core, q, cores, T, topo):
-    here = [c for c in cores if c in topo.cores_of(core)]
-    n_in = len(topo.engines(cores[q], core))
-    es = topo.engines(core, here[0])
-    k = len(es) // len(here)
-    for h in range(2):
-        g.wait_ge(T.sem["vp%d" % h], n_in)
-        trs = []
-        for i, c in enumerate(here):
-            rid, pid = topo.addr(c, core)
-            trs.append(RemoteDMATransfer(dst_ids=[DstId(rid=rid, pnc=pid)], dma_engine_mask=msk(es[k * i:k * (i + 1)]),
-                                         remote_sem=T.sem.vf, src=val_half(T, q, h), dst=val_half(T, q, h)))
-        g.remote_dma_fused(trs, local_sem=T.sem.rl)
-    g.wait_ge(T.sem.rl, 2 * k * len(here))
+def piece(T, q, i, h):
+    c0 = REG * q + REG // 4 * (2 * i + h)
+    return T.allv[:, c0:c0 + REG // 4]
+
+
+def transfer(T, topo, core, c, es, sem, src, dst):
+    rid, pid = topo.addr(c, core)
+    return RemoteDMATransfer(dst_ids=[DstId(rid=rid, pnc=pid)], dma_engine_mask=msk(es), remote_sem=T.sem[sem], src=src, dst=dst)
+
+
+def helper_program(g, core, q, h, cores, T, topo):
+    sib, far, peer = roles(q, cores, topo)
+    across = helpers(peer, cores, topo)[h]
+    off = topo.engines(core, across)
+    es = topo.engines(core, cores[q])
+    on = [e for e in es if e not in off]
+    k = len(es) // 2
+    for i in range(2):
+        g.wait_ge(T.sem["va%d" % i], k)
+        ap = piece(T, q, i, h)
+        g.remote_dma_fused([transfer(T, topo, core, across, off, "vb%d" % i, ap, ap), transfer(T, topo, core, cores[sib], on, "vs", ap, ap)],
+                           local_sem=T.sem.rl)
+    for i in range(2):
+        g.wait_ge(T.sem["vb%d" % i], len(off))
+        ap = piece(T, peer, i, h)
+        g.remote_dma_fused([transfer(T, topo, core, cores[q], es[:k], "vf", ap, ap), transfer(T, topo, core, cores[sib], es[k:], "vf", ap, ap)],
+                           local_sem=T.sem.rl)
+    g.wait_ge(T.sem.rl, 2 * (len(off) + len(on)) + 4 * k)
 
 
 def rank_program(g, core, T, topo):
@@ -77,19 +95,19 @@ def rank_program(g, core, T, topo):
     r = T.rank_of(core)
     if r is None:
         for q in range(N):
-            if relay_of(q, cores, topo) == core:
-                relay_program(g, core, q, cores, T, topo)
+            hs = helpers(q, cores, topo)
+            if core in hs:
+                helper_program(g, core, q, hs.index(core), cores, T, topo)
         return
-    others = [q for q in range(N) if q != r]
-    sib = [q for q in others if cores[q] in topo.cores_of(core)][0]
-    far = [q for q in others if q != sib]
-    peer = [q for q in far if topo.die(cores[q]) == topo.die(core)][0]
-    sibpeer = [q for q in far if q != peer][0]
+    sib, far, peer = roles(r, cores, topo)
+    others = far + [sib]
     off_eng = topo.engines(core, cores[peer])
-    on_eng = [e for e in topo.engines(core, cores[sib]) if e not in off_eng]
+    all_eng = topo.engines(core, cores[sib])
+    on_eng = [e for e in all_eng if e not in off_eng]
     half = len(off_eng) // 2
-    n_off, n_on = len(off_eng), len(on_eng)
-    n_vf = sum(2 * (len(topo.engines(relay_of(q, cores, topo), core)) // 2) for q in far)
+    n_off, n_on, n_all = len(off_eng), len(on_eng), len(all_eng)
+    eng_to = {far[0]: off_eng[:half], far[1]: off_eng[half:], sib: on_eng}
+    hf, hn = far[0] // 2, r // 2
 
     Q = {"g": g, "v": g.vector, "s": g.scalar, "t": g.tensor, "y": g.sync}
     known = {k: {} for k in Q}
@@ -142,20 +160,15 @@ def rank_program(g, core, T, topo):
 
     def send(items, R):
         before("g", R, [])
-        trs = []
-        for c, es, sem, src, dst in items:
-            rid, pid = topo.addr(c, core)
-            trs.append(RemoteDMATransfer(dst_ids=[DstId(rid=rid, pnc=pid)], dma_engine_mask=msk(es), remote_sem=T.sem[sem], src=src, dst=dst))
-            count["rl"] = count.get("rl", 0) + len(es)
-        g.remote_dma_fused(trs, local_sem=T.sem.rl)
+        for it in items:
+            count["rl"] = count.get("rl", 0) + len(it[1])
+        g.remote_dma_fused([transfer(T, topo, core, *it) for it in items], local_sem=T.sem.rl)
 
-    def three(sem_on, sem_off, src, dst):
-        return [(cores[peer], off_eng[:half], sem_off, src(peer), dst), (cores[sibpeer], off_eng[half:], sem_off, src(sibpeer), dst),
-                (cores[sib], on_eng, sem_on, src(sib), dst)]
+    def to(qs, sem, src, dst):
+        return [(cores[q], eng_to[q], sem, src(q), dst) for q in qs]
 
-    for tok, sem, val in (("vs", "vs", 2 * n_on), ("vf", "vf", n_vf),
-                          ("land_s", "ts", n_on), ("land_o", "to", 2 * n_off), ("ML", "pa", n_on + n_off), ("cntL", "ca", n_on + n_off),
-                          ("msgL", "ma", n_on + n_off), ("Yl_r", "ya", n_on + n_off)):
+    for tok, sem, val in (("vs", "vs", 4 * n_on), ("vf", "vf", 4 * n_all), ("land_s", "ts", n_on), ("land_o", "to", n_off),
+                          ("cntL", "ca", n_on + n_off), ("msgL", "ma", n_on + n_off), ("Yl_r", "ya", n_on + n_off)):
         wr[tok] = [(sem, val, {})]
         count[sem] = val
 
@@ -173,6 +186,9 @@ def rank_program(g, core, T, topo):
     def cp(out, a, R, W):
         do("v", [lambda: v.tensor_copy(out, a)], R, W)
 
+    def tr(out, a, R, W):
+        do("v", [lambda: v.transpose(out, a)], R, W)
+
     def ms(ap, c, W):
         do("v", [lambda: v.memset(ap, c)], [], W)
 
@@ -180,10 +196,13 @@ def rank_program(g, core, T, topo):
         do("v", [lambda: v.tensor_tensor_scan(out, a, b, init, o0, o1)], R, W)
 
     def act(out, a, fn, R, W, bias=0.0, scale=1.0):
-        if bias == 0.0 and scale == 1.0:
-            do("s", [lambda: s.activation(out, a, fn)], R, W)
-        else:
-            do("s", [lambda: s.activation(out, a, fn, bias=bias, scale=scale)], R, W)
+        do("s", [lambda: s.activation(out, a, fn, bias=bias, scale=scale)], R, W)
+
+    def gather(out, a, fn, R, W):
+        do("s", [lambda: s.activation(out, a, fn)], R, W)
+
+    def fill(out, n, c, W):
+        act(out, T.payS[:, 0:n], ACT.Identity, [], W, bias=c, scale=0.0)
 
     def mm(groups, R, W):
         calls = []
@@ -191,8 +210,8 @@ def rank_program(g, core, T, topo):
             calls.append(lambda out=out, a=a, b=b, st=st, sp=sp: t.matmul(out, a, b, st, sp))
         do("t", calls, R, W)
 
-    def wrap(out, Hm, src, R, W):
-        mm([(out, Hm[:, 15 - b:143 - b], src[:, b::16], b == 0, b == 15) for b in range(16)], R, W)
+    def wrap(out, Hm, src, first, last):
+        return [(out, Hm[:, 15 - b:143 - b], src[:, b::16], first and b == 0, last and b == 15) for b in range(16)]
 
     def iota(out, pat, base, cm, W, flt=True):
         if flt:
@@ -203,244 +222,295 @@ def rank_program(g, core, T, topo):
     def sel(out, a, pat, op, base, cm, R, W, fill=0.0):
         do("g", [lambda: g.affine_select(out, a, pat, op, fill, base, cm)], R, W)
 
+    def blk(A, q, n=1, w=256):
+        return A[:, w * q:w * (q + n)]
+
+    def col(i):
+        return T.cols[:, 32 * i:32 * i + 1]
+
     AND, SHR = ALU.bitwise_and, ALU.logical_shift_right
-    GM = [[-16, 8], [0, 16]]
+    MUL, ADD = ALU.mult, ALU.add
+    Id, GB = T.Id[:, 16:144], T.GB[:, 16:144]
+    hs = helpers(r, cores, topo)
+    own = REG * r
 
-    dma("y", T.entI[:], T.ent[:], [], ["entI"])
-    dma("s", T.attI[:], T.att[:], [], ["attI"])
+    def val_out(i):
+        send([(hs[h], all_eng[n_all // 2 * h:n_all // 2 * (h + 1)], "va%d" % i, piece(T, r, i, h), piece(T, r, i, h)) for h in range(2)],
+             ["own0", "own1", "gap0"] if i == 0 else ["own2", "gap1"])
+
+    for q, src, dst, tag in (("y", T.ent, T.entI, "ent"), ("s", T.att, T.attI, "att")):
+        dma(q, dst[:, KV:128], src[:, NV:2048], [], [tag + "S"])
+        for m in range(4):
+            dma(q, dst[m::4, 0:KV], src[:, 4 * KV * m:4 * KV * (m + 1)], [], [tag + str(m)])
+    ent, att = [[tag + x for x in "S0123"] for tag in ("ent", "att")]
+    ms(T.zeroB[:], 0.0, ["zeroB"])
     ms(T.zero[:], 0.0, ["zero"])
-    ms(T.clsI[:], 0, ["clsI0", "clsI1", "clsI2", "clsI3"])
-    iota(T.pay[:, 0:512], [[1, 32], [128, 16]], V0 + 2048 * r, 0, ["pay0"])
-    dma("s", T.formI[:], T.form[:], [], ["formI"])
+    iota(T.baseS[:], [[1, KS // 3], [KS, 16]], NV - 742, 0, ["baseS"])
     for k in range(2):
-        dma("ys"[k], T.win[0:128:16, 8192 * k:8192 * (k + 1)], T.zero[:], ["zero"], ["win%d" % k])
-    for h in range(2):
-        dma("y", val_half(T, r, h), T.val[:, 1024 * h:1024 * (h + 1)], [], ["own%d" % h])
-    for k in range(1, 4):
-        act(T.pay[:, 512 * k:512 * (k + 1)], T.pay[:, 0:512], ACT.Identity, ["pay0"], ["pay%d" % k], bias=32.0 * k)
-    act(T.c125[:], T.pay[:, 0:256], ACT.Identity, ["pay0"], ["c125"], bias=-0.125, scale=0.0)
-    for G in range(4):
-        dma("y", T.clsI[32 * G:32 * G + 16, :], T.cls[2 * G:2 * G + 2, :], [], ["clsI%d" % G])
-    ms(T.ones[:], 1.0, ["ones"])
-    ms(T.allv[:, 0:V0], 0.0, ["allv0"])
-    ms(T.keep3[:, :, 0:8], 8.0, ["keep3a"])
-    ms(T.keep3[:, :, 8:16], 0.125, ["keep3b"])
-    ms(T.c8192[:], 8192.0, ["c8192"])
-    ms(T.H[:], 0.0, ["H"])
-    cp(T.keep[:], T.keep3[:], ["keep3a", "keep3b"], ["keep"])
-    ms(T.H[:, 15::16], 1.0, ["H"])
-    ms(T.keep[:, 0::8], 0.0, ["keep"])
-    ms(T.Yl[:, 768:784], 0.0, ["Yl_z"])
-    ms(T.EL[:, 768:776], -1.0, ["EL_z"])
-    ms(T.Et[:, 1024:1032], -1.0, ["Et_z"])
-    iota(T.pI[:], [[0, 8]], 0, 1, ["pI"], False)
-    iota(T.mI[:], [[1, 32]], 0, 0, ["mI"], False)
-    sel(T.Id[:], T.ones[:], [[-1, 128]], ALU.is_equal, 0, 1, ["ones"], ["Id"])
-    iota(T.TR[:], [[1, 16]], 768, 0, ["TR"])
-    iota(T.sw[:], [[16, 48]], 0, 0, ["sw"])
-    iota(T.Et[:, 0:1024], [[1, 1024]], 0, 0, ["Et"])
-
-    ts(T.kI[:], T.entI[:], 1025, None, ALU.mult, None, ["entI"], ["kI"])
-    ts(T.fI[:, 0:128], T.formI[:], 15, None, AND, None, ["formI"], ["fI0"])
-    ts(T.kI[:], T.kI[:], 0x3FF0, None, AND, None, ["kI"], ["kI"])
-    ts(T.fI[:, 128:256], T.formI[:], 4, 15, SHR, AND, ["formI"], ["fI1"])
-    tt(T.kI[:], T.kI[:], T.attI[:], ALU.add, ["kI", "attI"], ["kI"])
-    ts(T.fI[:, 256:384], T.formI[:], 8, None, SHR, None, ["formI"], ["fI2"])
-    cp(T.kU[:], T.kI[:], ["kI"], ["kU"])
-    cp(T.fB[:], T.fI[:], ["fI0", "fI1", "fI2"], ["fB"])
-    cp(T.win[:, 0:16384].indirect(T.kU[:, 0:128]), T.pay[:], ["kU", "pay0", "pay1", "pay2", "pay3"], ["win0", "win1"])
-
-    for h in range(2):
-        ap = val_half(T, r, h)
-        send([(relay_of(r, cores, topo), off_eng, "vp%d" % h, ap, ap), (cores[sib], on_eng, "vs", ap, ap)], ["own%d" % h])
-    sel(T.TRI[:], T.c8192[:], GM, ALU.is_ge, 0, 1, ["c8192"], ["TRI"])
-    sel(T.DT[:], T.ones[:], [[-4, 32], [0, 4]], ALU.is_ge, 0, 1, ["ones"], ["DT"])
-    sel(T.H[:, 15::16], T.H[:, 15::16], [[-16, 9]], ALU.is_ge, 0, 1, ["H"], ["H"])
-    sel(T.TRI[:], T.TRI[:], [[1, 128]], ALU.is_ge, 0, -1, ["TRI"], ["TRI"])
-    sel(T.H[:, 15::16], T.H[:, 15::16], [[16, 9]], ALU.is_ge, 15, -1, ["H"], ["H"])
-    sel(T.TRI[:], T.TRI[:], [[1, 128]], ALU.not_equal, 0, -1, ["TRI"], ["TRI"], fill=4096.0)
-
-    for h in range(2):
-        act(T.E1[:, :, h, :], T.fB[:], ACT.Exp, ["fB"], ["E1%d" % h], bias=7 * LN8, scale=-LN8)
-    for h in range(2):
-        act(T.E2[:, :, h, :], T.fB[:], ACT.Exp, ["fB"], ["E2%d" % h], bias=-8 * LN8, scale=LN8)
-    for i in range(3):
-        for h in range(2):
-            act(T.fS[:, 8 * i:8 * (i + 1), h, :], T.fB[:, 8 * i:8 * (i + 1), :], ACT.Identity, ["fB"], ["fS%d%d" % (i, h)], scale=float(16 ** i))
-    for k, E in enumerate((T.E1, T.E2)):
-        o = T.P0[:, 256 * k:256 * (k + 1)]
-        mm([(o, T.Id[:], T.c125[:], True, False)] + [(o, T.Id[:], E[:, 8 * i:8 * (i + 1)], False, i == 2) for i in range(3)],
-           ["Id", "c125", "E%d0" % (k + 1), "E%d1" % (k + 1)], ["P0"])
-    mm([(T.P1[:, 0:256], T.Id[:], T.fS[:, 8 * i:8 * (i + 1)], i == 0, i == 2) for i in range(3)],
-       ["Id"] + ["fS%d%d" % (i, h) for i in range(3) for h in range(2)], ["P1"])
-    act(T.tabD[:, 0:512], T.P0[:, 0:512], ACT.Identity, [], ["P0", "tabD0"], bias=float(3 * DIG))
-    act(T.tabD[:, 512:768], T.P1[:, 0:256], ACT.Identity, [], ["P1", "tabD1"], bias=-6144.0)
-
-    dma("y", T.tl[:], T.win[0:128:16, :], ["win0", "win1"], ["tl"])
-
-    def tpart(q, es, sem, h):
-        return (cores[q], es, sem, T.tl[:, 256 * q + 128 * h:256 * q + 128 * (h + 1)], T.land[:, 256 * r + 128 * h:256 * r + 128 * (h + 1)])
-    send([tpart(peer, off_eng[:half], "to", 0), tpart(sibpeer, off_eng[half:], "to", 0),
-          tpart(sib, on_eng[:n_on // 2], "ts", 0), tpart(sib, on_eng[n_on // 2:], "ts", 1)], ["tl"])
-    sel(T.DT[:], T.DT[:], [[1, 128]], ALU.is_gt, 0, -1, ["DT"], ["DT"])
-
-    ts(T.pJ[:, 1:2], T.pI[:, 0:1], 8, None, AND, None, ["pI"], ["pJ1"])
-    ts(T.clsI[:], T.clsI[:], 257, None, ALU.mult, None, [], ["clsI0", "clsI1", "clsI2", "clsI3"])
-    ts(T.pF[:, 1:2], T.pJ[:, 1:2], 2.0, None, ALU.mult, None, ["pJ1"], ["pF1"])
-    ts(T.clsI[:], T.clsI[:], 3, 0xEF, SHR, AND, [], ["clsI0"])
-    ts(T.pJ[:, 0:1], T.pI[:, 0:1], 15, None, AND, None, ["pI"], ["pJ0"])
-    ts(T.clsF[:], T.clsI[:], T.pF[:, 1:2], None, ALU.add, None, ["clsI0", "pF1"], ["clsF"])
-    do("v", [lambda: v.transpose(T.tabW[:], T.tabD[:])], ["tabD0", "tabD1"], ["tabW"])
-    do("v", [lambda: v.transpose(T.clsT[:], T.clsF[:])], ["clsF"], ["clsT"])
+        dma("ys"[k], T.winV[0:128:16, 8192 * k:8192 * (k + 1)], T.zeroB[:], ["zeroB"], ["winV%d" % k])
+    for k in range(2):
+        dma("ys"[k], T.winS[0:128:16, 8192 * k:8192 * (k + 1)], T.zero[:], ["zero"], ["winS%d" % k])
+    n1 = NV // 2
+    dma("y", T.allv[:, own:own + n1], T.val[:, 0:n1], [], ["own0"])
+    dma("y", T.allv[:, own + n1 + GAP:own + 1024 + GAP], T.val[:, n1:1024], [], ["own1"])
+    dma("y", T.allv[:, own + 1024 + GAP:own + 2048 + GAP], T.val[:, 1024:2048], [], ["own2"])
     for gl in range(2):
-        cp(T.clsU[:, gl::2], T.clsT[:, 8 * gl:8 * gl + 8], ["clsT"], ["clsU%d" % gl])
-    cU = ["clsU0", "clsU1", "tabW"]
-    act(T.tabR[:, 512:768], T.tabW[:, 512:768].indirect(T.clsU[:, 0:16]), ACT.Copy, cU, ["tabR2"])
+        dma("y", T.formI[:, gl, :], T.form[gl::2, :], [], ["formI%d" % gl])
+    iota(T.baseV[:], [[1, KV], [KV, 4]], 0, 0, ["baseV"])
+    iota(T.payV[:, 0::4], [[1, KV], [KV, 4]], 255 - MID, 0, ["payV0"])
+    iota(T.payV[:, 3::4], [[1, KV], [KV, 4]], 12 * KV + GAP - MID - 255, 0, ["payV3"])
+    for k in range(3):
+        act(blk(T.payS, k, 1, 16 * KS // 3), T.baseS[:], ACT.Silu, ["baseS"], ["payS%d" % k], bias=float(KS // 3 * k))
+    ms(T.ones[:], 1.0, ["ones"])
+    ms(T.clsI[:], 0, ["clsI%d" % k for k in range(8)])
+    for k in range(8):
+        dma("y", T.clsI[32 * (k // 2):32 * (k // 2) + 16, 16 * (k % 2):16 * (k % 2) + 16], T.cls[k:k + 1, :], [], ["clsI%d" % k])
+    ms(T.w0[:, 0:32], 0.125, ["w0"])
+    ms(T.w1[:], 0.0, ["w1"])
+    for m in (1, 2):
+        ts(T.payV[:, m::4], T.baseV[:], float(4 * KV * m + GAP * (m - 1) - MID), 1.0 / 256, ADD, MUL, ["baseV"], ["payV%d" % m])
+    ts(T.kI[:], T.attI[:], 512, None, MUL, None, att, ["kI"])
+    ts(T.kJ[:], T.entI[:], 512.0, 7680.0, ALU.is_ge, MUL, ent, ["kJ"])
+    tt(T.kI[:], T.kI[:], T.entI[:], ADD, ["kI"] + ent, ["kI"])
+    ms(T.allv[:, own + n1:own + n1 + GAP], 0.0, ["gap0"])
+    tt(T.kI[:], T.kI[:], T.kJ[:], ADD, ["kI", "kJ"], ["kI"])
+    ms(T.allv[:, own + 2048 + GAP:own + REG], 0.0, ["gap1"])
+    cp(T.kU[:], T.kI[:], ["kI"], ["kU"])
+    cp(T.winV[:, 0:16384].indirect(T.kU[:, 0:KV]), T.payV[:], ["kU"] + ["payV%d" % k for k in range(4)], ["winV0", "winV1"])
+    for h in (hf, hn):
+        dma("y", blk(T.tlV, h, 1, 512), T.winV[0:128:16, 8192 * h:8192 * (h + 1)], ["winV0", "winV1"], ["tlV%d" % h])
+    gather(T.winS[:, 0:16384].indirect(T.kU[:, KV:128]), T.payS[:], ACT.Silu, ["kU", "payS0", "payS1", "payS2"], ["winS0", "winS1"])
+    for h, q in ((hf, "s"), (hn, "y")):
+        dma(q, blk(T.tlS, h, 1, 512), T.winS[0:128:16, 8192 * h:8192 * (h + 1)], ["winS0", "winS1"], ["tlS%d" % h])
+
+    sel(T.Id[:], T.ones[:, 0:160], [[-1, 160]], ALU.is_equal, 16, 1, ["ones"], ["Id"])
+    sel(T.GB[:], T.ones[:, 0:160], [[-16, 10], [0, 16]], ALU.is_ge, 16, 1, ["ones"], ["GB"])
+    iota(T.w0[:, 32:64], [[0, 32]], 8, 0, ["w0h"])
+    sel(T.GB[:], T.GB[:], [[16, 10], [0, 16]], ALU.is_ge, -1, -1, ["GB"], ["GB"])
+    before("g", ["w0", "w0h", "w1"], [])
+    for a in (0, 1):
+        iota(T.w0[:, a::16], [[0, 4]], 0, 0, ["w0%d" % a])
+    val_out(0)
+    iota(T.w0[:, 8:32:16], [[0, 2]], 0, 0, ["w08"])
+    for h, a, c in ((0, 0, 2 ** 21), (0, 1, -3 * 8 ** 6), (1, 0, 2 ** 23), (1, 8, -3)):
+        iota(T.w1[:, 32 * h + a:32 * h + 32:16], [[0, 2]], c, 0, ["w1%d%d" % (h, a)])
+    val_out(1)
+    iota(T.rows[:, 192:224], [[0, 32]], -192, 0, ["rows6"])
+    iota(T.rows[:, 64:96], [[0, 2], [1, 16]], 0, 0, ["rows2"])
+    iota(T.rows[:, 192:224:4], [[0, 8]], 576, 0, ["rows6"])
+    iota(T.rows[:, 96:128], [[0, 2], [192, 4], [0, 4]], 0, 0, ["rows3"])
+    iota(T.rows[:, 192:224:16], [[0, 2]], -1024, 0, ["rows6"])
+    iota(T.rows[:, 128:160], [[-1, 2], [0, 16]], 1, 0, ["rows4"])
+    iota(T.rows[:, 160:192], [[1, 2], [0, 16]], 0, 0, ["rows5"])
+    sel(T.INC[:], T.GB[:], [[1, 160]], ALU.is_ge, -16, -1, ["GB"], ["INC"])
+    iota(T.dI[:], [[1, 132]], 127, -1, ["dI"], False)
+    sel(T.INC[:], T.INC[:], [[1, 160]], ALU.not_equal, -16, -1, [], ["INC"], fill=0.5)
+
+    fo = ["formI0", "formI1"]
+    ts(T.fI[:, 0], T.formI[:], 15, None, AND, None, fo, ["fI0"])
+    ts(T.fI[:, 1], T.formI[:], 4, 15, SHR, AND, fo, ["fI1"])
+    ts(T.fI[:, 2], T.formI[:], 8, None, SHR, None, fo, ["fI2"])
+    ts(T.IdS[:, 0, :], Id, 2.0 ** 58, -2.0 ** 58, MUL, MUL, ["Id"], ["IdS0"])
+    for gl in range(2):
+        cp(T.fB[:, :, gl, :], T.fI[:, :, gl, :], ["fI0", "fI1", "fI2"], ["fB%d" % gl])
+    fB = ["fB0", "fB1"]
+    act(T.E1[:], T.fB[:], ACT.Silu, fB, ["E1"], bias=POW0, scale=POW1)
+    act(T.E2[:], T.fB[:], ACT.Silu, fB, ["E2"], bias=POW0 + 15 * POW1, scale=-POW1)
+    for i, c in ((1, 256.0), (2, 16.0)):
+        ts(T.IdS[:, i, :], Id, c, None, MUL, None, ["Id"], ["IdS%d" % i])
+    mm([(T.P7[:, 256:384], Id if i == 0 else T.IdS[:, i, :], T.fB[:, 4 * i:4 * (i + 1)], i == 0, i == 2) for i in range(3)], fB + ["IdS1", "IdS2"], ["P7"])
+    for k, E in enumerate((T.E1, T.E2)):
+        mm([(blk(T.P7, k, 1, 128), T.IdS[:, 0, :], blk(E, i, 1, 128), i == 0, i == 2) for i in range(3)], ["IdS0", "E%d" % (k + 1)], ["P7"])
+    PV = (T.P5, T.P6)
+    for h in (hf, hn):
+        mm([(PV[h][:], Id, blk(T.tlV, h, 1, 512), True, True)], ["tlV%d" % h], ["PV%d" % h])
+    cl = ["clsI%d" % k for k in range(8)]
+    ts(T.clsI[:], T.clsI[:], 129, None, MUL, None, [], cl)
+    ms(T.mone[:], -1.0, ["mone"])
+    ts(T.clsI[:], T.clsI[:], 2, 127, SHR, AND, [], cl)
+    scan(T.rows[:, 0:64], T.w0[:], T.w1[:], 0.0, MUL, ADD, ["w00", "w01", "w08", "w100", "w101", "w110", "w118"], ["rows0"])
+    cp(T.clsF[:], T.clsI[:], cl, ["clsF"])
+    ms(T.H[:], 0.0, ["H"])
+    tr(T.clsT[:], T.clsF[:], ["clsF"], ["clsT"])
+    tr(T.cols[:], T.rows[:], ["rows0"] + ["rows%d" % k for k in range(2, 7)], ["cols"])
+    cp(T.clsU[:], T.clsT[:, 0:16], ["clsT"], ["clsU"])
+    tr(T.tabW[:], T.P7[:, 0:384], [], ["P7", "tabW"])
+    cp(T.Id16[:, 0, :], Id, ["Id"], ["Id16"])
+    ts(T.Id16[:, 1, :], Id, 255.0, None, MUL, None, ["Id"], ["Id255"])
+    for q in range(1, N):
+        act(T.IdS[:, 2 + q, :], Id, ACT.Identity, ["Id"], ["IdQ%d" % q], scale=float(REG * q))
     for k in range(2):
-        cp(T.tabR[:, 256 * k:256 * (k + 1)], T.tabW[:, 256 * k:256 * (k + 1)].indirect(T.clsU[:, 0:16]), cU, ["tabR%d" % k])
-    do("v", [lambda: v.transpose(T.tabT[:], T.tabR[:])], ["tabR0", "tabR1", "tabR2"], ["tabT"])
-    for h in range(2):
-        act(T.Pm[:, 512 * h:512 * (h + 1)], T.tl[:, 512 * h:512 * (h + 1)], ACT.Sign, ["tl"], ["Pm%d" % h])
-        scan(T.Ms[:, 512 * h:512 * (h + 1)], T.keep[:], T.Pm[:, 512 * h:512 * (h + 1)], 0.0, ALU.mult, ALU.add, ["keep", "Pm%d" % h], ["Ms%d" % h])
-    ts(T.Mc[:, :, 0:16], T.Ms[:, 7::16], -3.0, None, ALU.mult, None, ["Ms0", "Ms1"], ["McA"])
-    ts(T.Mc[:, :, 16:32], T.Ms[:, 15::16], -3.0 * 8 ** 7, None, ALU.mult, None, ["Ms0", "Ms1"], ["McB"])
-    send(three("pa", "pa", lambda q: T.Mc[:, q, :], T.ML[:, 32 * r:32 * (r + 1)]), ["McA", "McB"])
-    send([tpart(peer, off_eng[:half], "to", 1), tpart(sibpeer, off_eng[half:], "to", 1)], ["tl"])
+        act(T.Wn[:, k, :], GB, ACT.Identity, ["GB", "cols"], ["Wn%d" % k], scale=col(k))
+    act(T.frm[:], blk(T.tabW, 2, 1, 128).indirect(T.clsU[:, 0:16]), ACT.Identity, ["tabW", "clsU"], ["frm"], bias=1.0 - 2049.0 / 8192, scale=-1.0 / 8192)
+    for k in range(2):
+        act(blk(T.tabR, k), blk(T.tabW, k, 1, 128).indirect(T.clsU[:, 0:16]), ACT.Identity, ["tabW", "clsU"], ["tabR%d" % k], bias=2.0 ** 23)
+    for x in range(2):
+        act(T.IM[:, x, :], T.Id[:], ACT.Identity, ["Id", "cols"], ["IM%d" % x], scale=col(4 + x))
+    for x in range(2):
+        act(T.TM[:, x, :], T.INC[:], ACT.Identity, ["INC", "cols"], ["TM%d" % x], scale=col(4 + x))
+    fill(T.cum[:, 0:16], 16, 0.0, ["cum0"])
+    fill(T.Gw[:, 0:768], 768, -0.25, ["Gw"])
+    fill(T.Yl[:, 768:784], 16, 0.0, ["Yl_z"])
+    fill(T.EL[:, 768:776], 8, -1.0, ["EL_z"])
+    act(T.cv[:, 0:1], col(6), ACT.Identity, ["cols"], ["cv"])
 
-    act(T.neg[:], T.pay[:, 0:768], ACT.Identity, ["pay0", "pay1"], ["neg"], bias=-8192.0, scale=0.0)
-    act(T.Gw[:, 0:768], T.pay[:, 0:768], ACT.Identity, ["pay0", "pay1"], ["Gw"], bias=-8388608.0, scale=0.0)
-    act(T.Ww[:, 0:768], T.pay[:, 0:768], ACT.Identity, ["pay0", "pay1"], ["Ww"], bias=0.0, scale=0.0)
-    iota(T.wid[:], [[1, 16], [16, 16]], 0, 0, ["wid"])
-    sel(T.R[:], T.ones[:], GM, ALU.is_ge, -4 * r, 1, ["ones"], ["R"])
-    sel(T.R[:], T.R[:], [[16, 8], [0, 16]], ALU.is_ge, 4 * r + 3, -1, ["R"], ["R"])
-    for q in range(4):
-        sel(T.FS[:, 128 * q:128 * (q + 1)], T.R[:], [[64, 8], [1, 16]], ALU.is_gt, 16 * r - q, -4, ["R"], ["FS%d" % q])
-    cp(T.mU[:], T.mI[:], ["mI"], ["mU"])
-    cp(T.H16[:], T.H[:], ["H"], ["H16"])
-    ts(T.pJ[:, 2:3], T.pI[:, 0:1], 12, None, AND, None, ["pI"], ["pJ2"])
-    ts(T.pJ[:, 3:4], T.pI[:, 0:1], 3, None, AND, None, ["pI"], ["pJ3"])
-    ts(T.pF[:, 0:1], T.pJ[:, 0:1], 1.0, None, ALU.mult, None, ["pJ0"], ["pF0"])
-    ts(T.pF[:, 4:5], T.pJ[:, 0:1], 16.0, None, ALU.mult, None, ["pJ0"], ["pF4"])
-    ts(T.pF[:, 5:6], T.pJ[:, 0:1], 0.0, None, ALU.is_gt, None, ["pJ0"], ["pF5"])
-    ts(T.pF[:, 2:3], T.pJ[:, 2:3], 48.0, None, ALU.mult, None, ["pJ2"], ["pF2"])
-    ts(T.pF[:, 3:4], T.pJ[:, 3:4], 0.0, -768.0, ALU.is_equal, ALU.mult, ["pJ3"], ["pF3"])
-    ts(T.TR[:], T.TR[:], T.pF[:, 4:5], None, ALU.add, None, ["pF4"], ["TR"])
-    ts(T.sw[:], T.sw[:], T.pF[:, 0:1], None, ALU.add, None, ["pF0"], ["sw"])
-    ts(T.cvec[:, 0:1], T.pF[:, 3:4], 192.0, T.pF[:, 5:6], ALU.add, ALU.mult, ["pF3", "pF5"], ["cvec"])
-    ms(T.DD[:], 0.0, ["DD"])
-    act(T.Rn[:], T.R[:], ACT.Identity, ["R"], ["Rn"], scale=-1.0)
+    def near(A, q):
+        return A[:, 256 * (q % 2):256 * (q % 2 + 1)]
+    sel(T.H[:, 15::16], T.ones[:, 0:9], [[-16, 9]], ALU.is_ge, 0, 1, ["ones"], ["H"])
+    sel(T.STR[:], GB, [[1, 128]], ALU.is_gt, 0, -1, ["GB"], ["STR"])
+    sel(T.H[:, 15::16], T.H[:, 15::16], [[16, 9]], ALU.is_ge, 15, -1, [], ["H"])
+    tt(blk(T.tq, hf, 1, 512), blk(T.tlS, hf, 1, 512), PV[hf][:], ADD, ["tlS%d" % hf], ["PV%d" % hf, "tqf"])
+    send(to(far, "to", lambda q: blk(T.tq, q), blk(T.land, r)), ["tqf"])
+    tt(blk(T.tq, sib), blk(T.tlS, sib), near(PV[hn], sib), ADD, ["tlS%d" % hn], ["PV%d" % hn, "tqs"])
+    send(to([sib], "ts", lambda q: blk(T.tq, q), blk(T.land, r)), ["tqs"])
+    tt(blk(T.land, r), blk(T.tlS, r), near(PV[hn], r), ADD, [], ["PV%d" % hn, "land_r"])
+    sel(T.DT[:], T.STR[:], [[-4, 32], [0, 4]], ALU.is_ge, 0, 1, ["STR"], ["DT"])
+    iota(T.TR[:], [[1, 16]], 768, 16, ["TR"])
+    iota(T.wid[:], [[1, 2], [2, 8], [16, 16]], 0, 0, ["wid"])
+    iota(T.sw[:], [[16, 48]], 0, 0, ["sw"])
+    act(T.H4[:], T.H[:], ACT.Identity, ["H"], ["H4"], scale=4096.0)
 
-    def blk(A, q, n=256):
-        return A[:, n * q:n * (q + 1)]
-    pm_ = T.P1[:, 0:256]
-    tt(pm_, blk(T.tl, r), blk(T.land, sib), ALU.add, ["tl", "land_s"], ["P1"])
-    tt(T.Mt[:], T.Mc[:, r, :], blk(T.ML, sib, 32), ALU.add, ["McA", "McB", "ML"], ["Mt"])
-    tt(blk(T.ML, r, 32), blk(T.ML, peer, 32), blk(T.ML, sibpeer, 32), ALU.add, ["ML"], ["MLr"])
-    tt(T.Mt[:], T.Mt[:], blk(T.ML, r, 32), ALU.add, ["MLr"], ["Mt"])
-    tt(T.U[:], T.Mt[:, 0:32].indirect(T.mU[:, 0:32]), T.tabT[:, 0:512], ALU.add, ["Mt", "mU", "tabT"], ["U0", "U1"])
-    ts(T.U[:, 0:256], T.U[:, 0:256], 4 * DIG, None, AND, None, [], ["U0"])
-    ts(T.U[:, 256:512], T.U[:, 256:512], 4 * DIG, 1, AND, SHR, [], ["U1"])
-    tt(T.ok[:], T.U[:, 0:256], T.U[:, 256:512], ALU.is_equal, ["U0", "U1"], ["ok"])
+    def marks(q, n, R, tag):
+        ts(blk(T.pres, q, n), blk(T.land, q, n), 0.0, None, ALU.not_equal, None, R, ["pres" + tag])
+        ts(blk(T.clp, q, n), blk(T.land, q, n), -1.0, 1.0, ALU.max, ALU.min, R, ["clp" + tag])
+    ms(T.Ww[:, 0:768], 0.0, ["Ww"])
+    marks(r, 1, ["land_r"], "r")
+    tr(T.frmT[:], T.frm[:], ["frm"], ["frmT"])
+    ts(T.dI[:], T.dI[:], 3, None, AND, None, [], ["dI"])
+    ts(T.Hn[:], T.H[:], -1.0, None, MUL, None, ["H"], ["Hn"])
+    ts(T.dA[:], T.dI[:], 0.0, None, ALU.is_equal, None, ["dI"], ["dA"])
+    marks(sib, 1, ["land_s"], "s")
 
-    nw = T.P3[:, 0:16]
-    wrap(nw, T.H, T.ok, ["H", "ok"], ["P3"])
-    mm([(T.P2[:, 0:256], T.TRI[:], T.ok[:], True, True)], ["TRI", "ok"], ["P2"])
-    tt(pm_, pm_, blk(T.land, peer), ALU.add, ["land_o"], ["P1"])
-    tt(T.mg[:], pm_, blk(T.land, sibpeer), ALU.add, ["land_o"], ["P1", "mg"])
-    cp(T.posU[:], T.mg[:], ["mg"], ["posU"])
-    act(T.VT[:], T.allv[:, 0:V0 + 8192].indirect(T.posU[:, 0:256]), ACT.Copy,
-        ["posU", "allv0", "own0", "own1", "vs", "vf"], ["VT"])
-    scan(T.incl[:], T.ones[:, 0:16], nw, 0.0, ALU.mult, ALU.add, ["ones"], ["P3", "incl"])
-    mm([(T.P4[:, 0:1], T.DT[:], T.incl[:, 15:16], True, True)], ["DT", "incl"], ["P4"])
-    send(three("ca", "ca", lambda q: T.incl[:, 8:16], T.cntL[:, 8 * r:8 * r + 8]), ["incl"])
-    for q in range(4):
-        sel(T.DD[:, 128 * q + q:128 * (q + 1):4], T.R[:, q::4], [[16, 8], [1, 4]], ALU.is_gt, 4 * r, -1, ["R", "DD"], ["DDa%d" % q])
-        q1 = (q + 1) % 4
-        sel(T.DD[:, 128 * q + q1:128 * (q + 1):4], T.Rn[:, q1::4], [[16, 8], [1, 4]], ALU.is_gt if q1 == 0 else ALU.is_ge, 4 * r, -1,
-            ["Rn", "DD"], ["DDb%d" % q])
-    for q in range(4):
-        sel(T.RA[:, 128 * q:128 * (q + 1)], T.ones[:], GM, ALU.is_equal, -4 * r - q, 1, ["ones"], ["RA%d" % q])
-    ts(T.tz[:], nw, 0.0, None, ALU.is_equal, None, [], ["P3r", "tz"])
-    tt(T.ex[:], T.incl[:], nw, ALU.subtract, ["incl"], ["P3s", "ex"])
-    tt(T.tz[:], T.tz[:], T.TR[:], ALU.mult, ["TR"], ["tz"])
-    tt(T.ex[:], T.ex[:], T.tz[:], ALU.max, ["tz"], ["ex"])
-    ts(T.offU[:], T.ex[:], T.P4[:, 0:1], T.pF[:, 2:3], ALU.add, ALU.add, ["ex", "pF2"], ["P4", "offU"])
-    tt(T.Gt[:], T.tabT[:, 512:768], T.P2[:, 0:256], ALU.add, ["tabT"], ["P2", "Gt"])
-    cp(T.Ww[:, 0:1792].indirect(T.offU[:, 0:16]), T.wid[:], ["offU", "wid"], ["Ww"])
-    cp(T.Gw[:, 0:1792].indirect(T.offU[:, 0:16]), T.Gt[:], ["offU", "Gt"], ["Gw"])
+    def digits(k, qs, first, last):
+        o = (T.P0, T.P1)[k][:, 0:256]
+        return ([(o, T.Wn[:, k, :], T.mone[:, 0:256], True, False)] if first else []) + \
+            [(o, T.Wn[:, k, :], blk(T.pres, q), False, last and q == qs[-1]) for q in qs]
+
+    def places(qs, first, last):
+        o, out = T.P2[:, 0:256], []
+        for q in qs:
+            if q:
+                out.append((o, T.IdS[:, 2 + q, :], blk(T.pres, q), first and not out, False))
+            out.append((o, T.Id16[:, 0, :], blk(T.land, q), first and not out, False))
+            out.append((o, T.Id16[:, 1, :], blk(T.clp, q), False, last and q == qs[-1]))
+        return out
+
+    def turned(M, src, last):
+        return [(T.P3[:, 128 * x:128 * (x + 1)], M[:, x, 16 - 16 * (gl - x):144 - 16 * (gl - x)], src[:, :, gl, :], False, last and x + gl == 2)
+                for x in range(2) for gl in range(2)]
+
+    IdQ = ["IdQ%d" % q for q in range(1, N)]
+    mm(digits(0, [r], True, False), ["Wn0", "mone", "presr"], ["P0"])
+    mm(digits(1, [r], True, False), ["Wn1"], ["P1"])
+    mm(places([r], True, False), ["Id16", "Id255", "land_r", "clpr"] + IdQ, ["P2"])
+    mm(digits(0, [sib], False, False), ["press"], ["P0"])
+    mm(digits(1, [sib], False, False), [], ["P1"])
+    mm(places([sib], False, False), ["land_s", "clps"], ["P2"])
+
+    marks(far[0], 2, ["land_o"], "o")
+    mm(digits(0, far, False, True), ["preso"], ["P0"])
+    mm(digits(1, far, False, True), [], ["P1"])
+    mm(places(far, False, True), ["land_o", "clpo"], ["P2"])
+    mm([(T.P3[:, 0:256], Id, T.mone[:, 0:256], True, False)] + turned(T.IM, T.frmT, False), ["IM0", "IM1", "frmT"], ["P3"])
+    tt(T.dB[:], T.dA[:, 0:128], T.dA[:, 1:129], ALU.subtract, ["dA"], ["dB"])
+    tt(blk(T.U, 0), blk(T.tabR, 0), T.P0[:, 0:256], ADD, ["tabR0"], ["P0", "U0"])
+    tt(blk(T.U, 1), blk(T.tabR, 1), T.P1[:, 0:256], ADD, ["tabR1"], ["P1", "U1"])
+    ts(blk(T.U, 0), blk(T.U, 0), 4 * DIG, None, AND, None, [], ["U0"])
+    ts(blk(T.U, 1), blk(T.U, 1), 4 * DIG, 1, AND, SHR, [], ["U1"])
+    ts(T.posU[:], T.P2[:, 0:256], float(MID), None, ADD, None, [], ["P2", "posU"])
+    gather(T.VT[:], T.allv[:, 0:4 * REG].indirect(T.posU[:, 0:256]), ACT.Copy, ["posU", "own0", "own1", "own2", "gap0", "gap1", "vs", "vf"], ["VT"])
+    tt(T.ok[:], blk(T.U, 0), blk(T.U, 1), ALU.is_equal, ["U0", "U1"], ["ok"])
+    iota(T.lo[:], [[1, 256]], 0, 0, ["lo"])
+
+    scan(T.cum[:, 16:272], T.ones[:, 0:256], T.ok[:], 0.0, MUL, ADD, ["ones", "ok"], ["cum"])
+    tr(T.okT[:], T.ok[:], ["ok"], ["okT"])
+    mine_n = T.cum[:, 271:272]
+    mm([(T.P4[:, 0:1], T.DT[:], mine_n, True, True)], ["DT", "cum"], ["P4"])
+    mm(turned(T.TM, T.okT, True), ["TM0", "TM1", "okT"], ["P3"])
+    send(to(others, "ca", lambda q: T.cum[:, 264:272], blk(T.cntL, r, 1, 8)), ["cum"])
+    lo_, hi_ = T.cum[:, 15:271:16], T.cum[:, 31:272:16]
+    tt(T.tz[:], lo_, hi_, ALU.is_equal, ["cum", "cum0"], ["tz"])
+    ts(T.sw16[:], T.sw[:], col(2), None, ADD, None, ["sw", "cols"], ["sw16"])
+    tt(T.tz[:], T.tz[:], T.TR[:], MUL, ["TR"], ["tz"])
+    tt(T.tz[:], T.tz[:], lo_, ALU.max, [], ["tz"])
+    ts(T.Gt[:], T.P3[:, 0:256], -0.25, None, ALU.max, None, [], ["P3", "Gt"])
+    for x in range(2):
+        ts(T.offU[:, 8 * x:8 * (x + 1)], T.tz[:, x::2], T.P4[:, 0:1], col(3), ADD, ADD, ["tz", "cols"], ["P4", "offU%d" % x])
+    sel(T.Sel[:], T.ones[:], [[1, 4], [-64, 8], [-1, 16]], ALU.is_equal, -16 * r, 4, ["ones"], ["Sel"])
+    sel(T.DD[:], T.dB[:], [[-16, 8], [0, 16]], ALU.is_ge, 0, 1, ["dB"], ["DD"])
+    sel(T.STR[:, 0::16], T.GB[:, 16:144:16], [[0, 8]], ALU.is_ge, 0, 0, ["GB"], ["STR"])
+    sel(T.DD[:], T.DD[:], [[1, 128]], ALU.is_gt, 0, -1, [], ["DD"])
+    iota(T.Et[:], [[1, 1024]], 0, 0, ["Et"])
+    oU = ["offU0", "offU1"]
+    cp(T.Ww[:, 0:WIDE].indirect(T.offU[:, 0:16]), T.wid[:], oU + ["wid"], ["Ww"])
+    cp(T.Gw[:, 0:WIDE].indirect(T.offU[:, 0:16]), T.Gt[:], oU + ["Gt"], ["Gw"])
     scan(T.Ws[:], T.Ww[:, 0:768], T.Ww[:, 0:768], 0.0, ALU.max, ALU.max, ["Ww"], ["Ws"])
-    scan(T.Ds[:], T.neg[:], T.Gw[:, 0:768], -8388608.0, ALU.add, ALU.max, ["Gw", "neg"], ["Ds"])
-    wrap(T.P5[:, 0:48], T.H, T.Ws, ["H", "Ws"], ["P5"])
-    ts(T.phi[:], T.Ds[:], -2048.0, 2048.0, ALU.max, ALU.min, ["Ds"], ["phi"])
-    wrap(T.P6[:, 0:48], T.H16, T.phi, ["H16", "phi"], ["P6"])
-    ts(T.wI[:], T.P5[:, 0:48], 16.0, None, ALU.mult, None, [], ["P5", "wI"])
-    ts(T.wI[:], T.wI[:], 3840, None, AND, None, [], ["wI"])
-    ts(T.b15[:], T.wI[:], 15.0, None, ALU.add, None, ["wI"], ["b15"])
-    ts(T.e16[:], T.wI[:], 0.0625, float(256 * r + 15), ALU.mult, ALU.add, ["wI"], ["e16"])
-    ts(T.S16[:], T.P6[:, 0:48], 32768.0, 16.0, ALU.add, ALU.mult, [], ["P6", "S16"])
-    ts(T.ab[:], T.S16[:], 16, None, SHR, None, ["S16"], ["ab"])
-    ts(T.xI[:, 48:96], T.S16[:], 4, 240, SHR, AND, ["S16"], ["xI1"])
-    tt(T.b15[:], T.b15[:], T.ab[:], ALU.subtract, ["ab"], ["b15"])
-    ts(T.xI[:, 0:48], T.S16[:], 240, None, AND, None, ["S16"], ["xI0"])
-    tt(T.kF[:, 48:96], T.xI[:, 48:96], T.b15[:], ALU.add, ["xI1", "b15"], ["kF1"])
-    ts(T.xI[:, 96:144], T.S16[:], 8, 240, SHR, AND, ["S16"], ["xI2"])
-    cp(T.kL[:, 48:96], T.kF[:, 48:96], ["kF1"], ["kL1"])
-    for i in (0, 2):
-        tt(T.kF[:, 48 * i:48 * (i + 1)], T.xI[:, 48 * i:48 * (i + 1)], T.b15[:], ALU.add, ["xI%d" % i, "b15"], ["kF%d" % i])
-    ts(T.fm[:], T.S16[:], 65535, None, AND, None, ["S16"], ["fm"])
-    tt(T.e16[:], T.e16[:], T.ab[:], ALU.subtract, ["ab"], ["e16"])
-    for i in (0, 2):
-        cp(T.kL[:, 48 * i:48 * (i + 1)], T.kF[:, 48 * i:48 * (i + 1)], ["kF%d" % i], ["kL%d" % i])
-    ts(T.tp[:], T.fm[:], 0.0, 1024.0, ALU.is_equal, ALU.mult, ["fm"], ["tp"])
+    scan(T.Ds[:], T.mone[:], T.Gw[:, 0:768], -0.25, ADD, ALU.max, ["Gw", "mone"], ["Ds"])
 
     def cn(q):
-        return T.incl[:, 15:16] if q == r else T.cntL[:, 8 * q + 7:8 * q + 8]
-    DDs = ["DDa%d" % q for q in range(4)] + ["DDb%d" % q for q in range(4)]
-    mm([(T.P3[:, 0:1], T.FS[:, 128 * q:128 * (q + 1)], cn(q), q == 0, q == 3) for q in range(4)]
-       + [(T.P3[:, 1:2], T.Id[:], T.cvec[:, 0:1], True, False)]
-       + [(T.P3[:, 1:2], T.DD[:, 128 * q:128 * (q + 1)], cn(q), False, q == 3) for q in range(4)]
-       + [(T.P3[:, 2:3], T.R[:], cn(q), q == 0, q == 3) for q in range(4)],
-       ["cntL", "incl", "cvec", "R", "FS0", "FS1", "FS2", "FS3"] + DDs, ["P3", "P3r", "P3s"])
+        return mine_n if q == r else T.cntL[:, 8 * q + 7:8 * q + 8]
+    mm([(T.P7[:, 0:1], blk(T.Sel, q, 1, 128), cn(q), q == 0, q == N - 1) for q in range(N)], ["Sel", "cntL", "cum"], ["P7"])
+    mm([(T.P1[:, 0:1], blk(T.Sel, 0, 1, 128), cn(q), q == 0, q == N - 1) for q in range(N)], [], ["P1"])
+    mm(wrap(T.P5[:, 0:48], T.H4, T.Ws, True, False), ["H4", "Ws"], ["PV0"])
+    cp(T.nS[:, 0:1], T.P7[:, 0:1], [], ["P7", "nS"])
+    ts(T.phi[:], T.Ds[:], 8192.0, 2048.0, MUL, ALU.min, ["Ds"], ["phi"])
+    m1 = T.mone[:, 0:1]
+    mm([x for k in range(3) for x in [(T.P0[:, k:k + 1], T.IdS[:, 1, :], m1, i == 0, False) for i in range(k)]
+        + [(T.P0[:, k:k + 1], T.STR[:], T.nS[:, 0:1], k == 0, True)]]
+       + [(T.P0[:, 3:4], T.DD[:], T.nS[:, 0:1], True, False), (T.P0[:, 3:4], Id, T.cv[:, 0:1], False, True)], ["STR", "DD", "nS", "cv"], ["P0"])
+    mm(wrap(T.P5[:, 0:48], T.Hn, T.phi, False, True), ["Hn", "phi"], ["PV0"])
+    for k in range(3):
+        ts(blk(T.X, k), T.lo[:], T.P0[:, k:k + 1], T.P0[:, 3:4], ALU.is_ge, MUL, ["lo", "P0"], ["X%d" % k])
+    mm([(T.P6[:, 0:48], T.Id16[:, 0, :], T.sw16[:], True, False)] + wrap(T.P6[:, 0:48], T.Hn, T.X, False, True), ["sw16", "X0", "X1", "X2"], ["PV1"])
 
-    lo = min(far)
-    parts = [(lo, 2, T.ys)] if max(far) == lo + 1 else [(far[0], 1, T.ys), (far[1], 1, T.ys)]
-    parts += [(sib, 1, T.ys), (r, 1, T.Yl)]
+    ts(T.Z[:], T.P5[:, 0:48], 32767.0, None, ADD, None, [], ["PV0", "Z"])
+    cp(T.co[:, 0:1], T.P1[:, 0:1], [], ["P1", "co"])
+    dma("y", T.cnt[:], T.co[0:128:4, 0:1], ["co"], ["cnt"])
+    ts(T.zI[:, 0, :], T.Z[:], 8, 0xFFF, SHR, AND, ["Z"], ["z0"])
+    ts(T.zI[:, 1, :], T.Z[:], 8, 0xFF0, SHR, AND, ["Z"], ["z1"])
+    ts(T.zI[:, 2, :], T.Z[:], 15, None, AND, None, ["Z"], ["z2"])
+    cp(T.kL[:, 96:144], T.zI[:, 0, :], ["z0"], ["kB"])
+    tt(T.kF[:, 0:48], T.zI[:, 1, :], T.zI[:, 2, :], ADD, ["z1", "z2"], ["kF0"])
+    ts(T.zI[:, 3, :], T.Z[:], 4, 15, SHR, AND, ["Z"], ["z3"])
+    ts(T.zI[:, 4, :], T.Z[:], 12, 255, SHR, AND, ["Z"], ["z4"])
+    cp(T.kL[:, 0:48], T.kF[:, 0:48], ["kF0"], ["kA"])
+    tt(T.kF[:, 48:96], T.zI[:, 1, :], T.zI[:, 3, :], ADD, ["z1", "z3"], ["kF1"])
+
     VTw = T.VT[:, 0:4096]
-    for d, n, dst in parts:
-        act(T.Bv[:, 192 * d:192 * (d + n)], VTw.indirect(T.kL[:, 48 + 12 * d:48 + 12 * (d + n)]), ACT.Copy, ["VT", "kL1"], ["Bv%d" % d])
-    tt(T.tp[:], T.tp[:], T.e16[:], ALU.max, ["e16"], ["tp"])
-    cp(T.msg[:], T.tp[:], ["tp"], ["msg"])
-    send(three("ma", "ma", lambda q: T.msg[:, 12 * q:12 * (q + 1)], T.msgL[:, 12 * r:12 * (r + 1)]), ["msg"])
-    dma("y", T.msgL[:, 12 * r:12 * (r + 1)], T.msg[:, 12 * r:12 * (r + 1)], ["msg"], ["msgO"])
-    mine = T.Yl[:, 192 * r:192 * (r + 1)]
-    for d, n, dst in parts:
-        a, b = 192 * d, 192 * (d + n)
-        if d == r:
-            ts(T.X[:], T.Et[:, 0:768], T.P3[:, 0:1], T.P3[:, 1:2], ALU.is_ge, ALU.mult, ["Et"], ["P3", "X"])
-            wrap(T.P5[:, 0:48], T.H16, T.X, ["H16", "X"], ["P5"])
-            ts(T.pm[:], T.sw[:], T.P3[:, 2:3], 768.0, ALU.is_ge, ALU.mult, ["sw"], ["P3", "pm"])
-        tt(T.tv[:, a:b], VTw.indirect(T.kL[:, 12 * d:12 * (d + n)]), T.Bv[:, a:b], ALU.subtract, ["VT", "kL0", "Bv%d" % d], ["tv%d" % d])
-        tt(dst[:, a:b], VTw.indirect(T.kL[:, 96 + 12 * d:96 + 12 * (d + n)]), T.tv[:, a:b], ALU.add, ["VT", "kL2", "tv%d" % d], ["ys%d" % d])
-        if d == parts[-3][0]:
-            send([(cores[peer], off_eng[:half], "ya", T.ys[:, 192 * peer:192 * (peer + 1)], mine),
-                  (cores[sibpeer], off_eng[half:], "ya", T.ys[:, 192 * sibpeer:192 * (sibpeer + 1)], mine)], ["ys%d" % p[0] for p in parts[:-2]])
-        if d == sib:
-            send([(cores[sib], on_eng, "ya", T.ys[:, a:b], mine)], ["ys%d" % d])
-    mm([(T.P4[:, al:al + 1], T.RA[:, 128 * al:128 * (al + 1)], cn(q), q == 0, q == 3) for al in range(4) for q in range(4)],
-       ["cntL", "incl", "RA0", "RA1", "RA2", "RA3"], ["P4"])
-    act(T.EL[:, 0:768], T.Et[:, 0:1032].indirect(T.msgL[:, 0:48]), ACT.Copy, ["Et", "Et_z", "msgL", "msgO"], ["EL"])
+    for d in far + [sib, r]:
+        gather(blk(T.Bv, d, 1, 192), VTw.indirect(T.kL[:, 96 + 12 * d:96 + 12 * (d + 1)]), ACT.Copy, ["VT", "kB"], ["Bv%d" % d])
+    mine = blk(T.Yl, r, 1, 192)
 
-    tt(T.sg[:], T.P5[:, 0:48], T.sw[:], ALU.add, ["sw"], ["P5", "sg"])
-    tt(T.sg[:], T.sg[:], T.pm[:], ALU.max, ["pm"], ["sg"])
-    ts(T.sigU[:], T.sg[:], 768.0, None, ALU.min, None, ["sg"], ["sigU"])
-    cp(T.co[:], T.P4[:, 0:4], [], ["P4", "co"])
-    dma("y", T.cnt[:], T.co[0:128:16, :], ["co"], ["cnt"])
-    act(T.wo[:], T.EL[:, 0:776].indirect(T.sigU[:, 0:48]), ACT.Copy, ["EL", "EL_z", "sigU"], ["wo"])
+    def first(d):
+        tt(blk(T.tv, d, 1, 192), VTw.indirect(blk(T.kL, d, 1, 12)), blk(T.Bv, d, 1, 192), ALU.subtract, ["VT", "kA", "Bv%d" % d], ["tv%d" % d])
+
+    def second(d):
+        tt(mine if d == r else blk(T.ys, d, 1, 192), VTw.indirect(T.kL[:, 48 + 12 * d:48 + 12 * (d + 1)]), blk(T.tv, d, 1, 192), ADD,
+           ["tv%d" % d, "kC"], ["ys%d" % d])
+    ts(T.msg[:], T.zI[:, 4, :], 256.0 * r, None, ADD, None, ["z4"], ["msg"])
+    send(to(others, "ma", lambda q: blk(T.msg, q, 1, 12), T.msgL[:, 16 * r:16 * r + 12]), ["msg"])
+    first(far[0])
+    cp(T.kL[:, 48:96], T.kF[:, 48:96], ["kF1"], ["kC"])
+    first(far[1])
+    second(far[0])
+    second(far[1])
+    send(to(far, "ya", lambda q: blk(T.ys, q, 1, 192), mine), ["ys%d" % q for q in far])
+    first(sib)
+    ts(T.sigU[:], T.P6[:, 0:48], 768.0, None, ALU.min, None, [], ["PV1", "sigU"])
+    second(sib)
+    send(to([sib], "ya", lambda q: blk(T.ys, q, 1, 192), mine), ["ys%d" % sib])
+    first(r)
+    second(r)
+    gather(blk(T.EL, r, 1, 192), T.Et[:, 0:1024].indirect(blk(T.msg, r, 1, 12)), ACT.Copy, ["Et", "msg"], ["EL%d" % r])
+    for q in others:
+        gather(blk(T.EL, q, 1, 192), T.Et[:, 0:1024].indirect(T.msgL[:, 16 * q:16 * q + 12]), ACT.Copy, ["msgL"], ["EL%d" % q])
+
+    gather(T.wo[:], T.EL[:, 0:776].indirect(T.sigU[:, 0:48]), ACT.Copy, ["EL%d" % q for q in range(N)] + ["EL_z", "sigU"], ["wo"])
     dma("s", T.who[:], T.wo[0:128:16, :], ["wo"], ["who"])
     YR = ["sigU", "Yl_z", "Yl_r", "ys%d" % r]
     cp(T.yo[:, 0:448], T.Yl[:, 0:784].indirect(T.sigU[:, 0:28]), YR, ["yo0"])
     dma("y", T.y[:, 0:448], T.yo[:, 0:448], ["yo0"], ["y0"])
-    act(T.yo[:, 448:768], T.Yl[:, 0:784].indirect(T.sigU[:, 28:48]), ACT.Copy, YR, ["yo1"])
+    gather(T.yo[:, 448:768], T.Yl[:, 0:784].indirect(T.sigU[:, 28:48]), ACT.Copy, YR, ["yo1"])
     dma("s", T.y[:, 448:768], T.yo[:, 448:768], ["yo1"], ["y1"])
     for name, val in count.items():
         need("g", (name, val, {}))

@@ -11,34 +11,44 @@ SCRATCH = {
     "entI": (S, [128, 128], I32), "attI": (S, [128, 128], I32), "kI": (S, [128, 128], I32), "kU": (S, [128, 128], U16),
     "formI": (S, [128, 2, 64], I32), "fI": (S, [128, 3, 2, 64], I32), "fB": (S, [128, 12, 2, 16], BF),
     "E1": (S, [128, 384], BF), "E2": (S, [128, 384], BF), "tabW": (S, [128, 384], F32), "tabR": (S, [128, 512], F32),
-    "frm": (S, [128, 256], F32), "frmT": (S, [128, 8, 2, 16], F32),
+    "frm": (S, [128, 256], F16), "frmT": (S, [128, 8, 2, 16], F16), "Id32": (S, [128, 128], F32),
     "clsI": (S, [128, 32], I32), "clsF": (S, [128, 32], F32), "clsT": (S, [128, 32], F32), "clsU": (S, [128, 16], U16),
     "zero": (S, [128, 512], F32), "zeroB": (S, [128, 512], BF), "winV": (S, [128, 16384], BF), "winS": (S, [128, 16384], F32), "kJ": (S, [128, 128], I32),
     "payV": (S, [128, NV], F32), "payS": (S, [128, 16 * KS], F32), "baseV": (S, [128, 8 * KV // 2], F32), "baseS": (S, [128, 16 * KS // 3], F32),
     "tlV": (S, [128, 1024], BF), "tlS": (S, [128, 1024], F32), "tq": (S, [128, 1024], F16), "land": (S, [128, 1024], F16),
-    "pres": (S, [128, 1024], BF), "clp": (S, [128, 1024], F16), "posU": (S, [128, 256], U16),
+    "pres": (S, [128, 1024], BF), "clp": (S, [128, 256], F16), "posU": (S, [128, 256], U16),
     "allv": (S, [128, 4 * REG], BF), "VT": (S, [128, 4096], BF), "U": (S, [128, 512], I32), "ok": (S, [128, 256], BF),
     "okT": (S, [128, 8, 2, 16], BF), "cum": (S, [128, 272], BF), "Gt": (S, [128, 256], F32),
     "tz": (S, [128, 16], F32), "offU": (S, [128, 16], U16), "Gw": (S, [128, WIDE], F32), "Ww": (S, [128, WIDE], BF),
     "Ds": (S, [128, 768], F32), "Ws": (S, [128, 768], BF), "phi": (S, [128, 768], F16),
     "wid": (S, [128, 256], BF), "ones": (S, [128, 512], BF), "mone": (S, [128, 768], BF), "lo": (S, [128, 256], BF),
-    "Id": (S, [128, 160], BF), "IdS": (S, [128, 6, 128], BF), "Id16": (S, [128, 2, 128], F16), "GB": (S, [128, 160], BF),
+    "Id": (S, [128, 160], BF), "IdS": (S, [128, 9, 128], BF), "GB": (S, [128, 160], BF),
     "STR": (S, [128, 128], BF), "INC": (S, [128, 160], BF), "DT": (S, [128, 128], BF), "DD": (S, [128, 128], BF),
-    "TM": (S, [128, 2, 160], BF), "IM": (S, [128, 2, 160], F32), "Wn": (S, [128, 2, 128], BF), "Sel": (S, [128, 512], BF),
-    "dI": (S, [128, 132], I32), "dA": (S, [128, 132], BF), "dB": (S, [128, 128], BF),
+    "TM": (S, [128, 2, 160], BF), "IM": (S, [128, 2, 160], BF), "Wn": (S, [128, 2, 128], BF), "Sel": (S, [128, 512], BF),
+    "dN": (S, [128, 132], BF), "dA": (S, [128, 132], BF), "dB": (S, [128, 128], BF),
     "w0": (S, [128, 64], F32), "w1": (S, [128, 64], F32), "rows": (S, [128, 224], F32), "cols": (S, [128, 224], F32),
-    "H": (S, [128, 144], BF), "H4": (S, [128, 144], BF), "Hn": (S, [128, 144], F16), "TR": (S, [128, 16], F32),
-    "sw": (S, [128, 48], F32), "sw16": (S, [128, 48], F16),
+    "H": (S, [128, 144], BF), "H4": (S, [128, 144], BF), "Hn": (S, [128, 144], BF), "TR": (S, [128, 16], F32),
+    "sw": (S, [128, 48], BF),
     "Et": (S, [128, 1024], F32), "EL": (S, [128, 776], F32), "wo": (S, [128, 768], F32),
     "Z": (S, [128, 48], I32), "zI": (S, [128, 5, 48], I32), "kF": (S, [128, 96], I32), "kL": (S, [128, 144], U16),
     "msg": (S, [128, 48], U16), "msgL": (S, [128, 64], U16), "cntL": (S, [128, 32], BF), "nS": (S, [128, 8], BF), "cv": (S, [128, 8], BF),
     "Bv": (S, [128, 768], F32), "tv": (S, [128, 768], F32), "ys": (S, [128, 768], BF),
     "Yl": (S, [128, 784], BF), "yo": (S, [128, 768], BF), "X": (S, [128, 768], F16), "sigU": (S, [128, 48], U16), "co": (S, [128, 4], F32),
-    "P0": (P, [128, 512], F32), "P1": (P, [128, 512], F32), "P2": (P, [128, 512], F32), "P3": (P, [128, 512], F32),
+    "P0": (P, [128, 512], F32), "P1": (P, [128, 512], F32), "P2": (P, [128, 512], F32), "P3": (P, [128, 8, 2, 16], F32),
     "P4": (P, [128, 512], F32), "P5": (P, [128, 512], F32), "P6": (P, [128, 512], F32), "P7": (P, [128, 512], F32),
 }
+WORLD = 256
+TWO_PLANES = True
+NM = 2
+EARLY = ["val0", "fillV", "fillS", "val1"]
+CUTS = [0, 512, REG]
+NP = len(CUTS) - 1
+STEPS = [(0, 0, 1), (1, 0, 1)]
+THIRD = True
+YSPLIT = False
+WV, YV = 16, 26
 NDMA = 40
-SEMAPHORES = ["qg", "qv", "qs", "qt", "rl", "va0", "va1", "vb0", "vb1", "vs", "vf", "ts", "to", "ca", "ma", "ya"] + ["d%d" % i for i in range(NDMA)]
+SEMAPHORES = ["qg", "qv", "qs", "qt", "rl", "va0", "va1", "va2", "vb0", "vb1", "vb2", "vs", "vf", "ts", "to", "ca", "ma", "ya"] + ["d%d" % i for i in range(NDMA)]
 DIG = sum(8 ** k for k in range(8))
 POW0, POW1 = -70.10015395, -2.10671760
 
@@ -48,7 +58,10 @@ def msk(es):
 
 
 def helpers(q, cores, topo):
-    return [c for c in topo.cores_of(cores[q]) if c not in cores and topo.die(c) == topo.die(cores[q])][:2]
+    free = [c for c in topo.cores_of(cores[q]) if c not in cores and topo.die(c) == topo.die(cores[q])]
+    mate = [c for c in range(WORLD) if topo.mates(c, cores[q])][0]
+    inner = [c for c in free if not topo.may_write(c, mate)]
+    return [inner[0], [c for c in free if topo.may_write(c, mate)][0], inner[1]]
 
 
 def roles(r, cores, topo):
@@ -59,9 +72,10 @@ def roles(r, cores, topo):
     return sib, far, peer
 
 
-def piece(T, q, i, h):
-    c0 = REG * q + REG // 4 * (2 * i + h)
-    return T.allv[:, c0:c0 + REG // 4]
+def piece(T, q, i, h, j=0, parts=1):
+    n = (CUTS[i + 1] - CUTS[i]) // 2
+    c0 = REG * q + CUTS[i] + n * h + n // parts * j
+    return T.allv[:, c0:c0 + n // parts]
 
 
 def transfer(T, topo, core, c, es, sem, src, dst):
@@ -69,24 +83,46 @@ def transfer(T, topo, core, c, es, sem, src, dst):
     return RemoteDMATransfer(dst_ids=[DstId(rid=rid, pnc=pid)], dma_engine_mask=msk(es), remote_sem=T.sem[sem], src=src, dst=dst)
 
 
-def helper_program(g, core, q, h, cores, T, topo):
-    sib, far, peer = roles(q, cores, topo)
-    across = helpers(peer, cores, topo)[h]
-    off = topo.engines(core, across)
-    es = topo.engines(core, cores[q])
-    on = [e for e in es if e not in off]
-    k = len(es) // 2
-    for i in range(2):
-        g.wait_ge(T.sem["va%d" % i], k)
-        ap = piece(T, q, i, h)
-        g.remote_dma_fused([transfer(T, topo, core, across, off, "vb%d" % i, ap, ap), transfer(T, topo, core, cores[sib], on, "vs", ap, ap)],
-                           local_sem=T.sem.rl)
-    for i in range(2):
-        g.wait_ge(T.sem["vb%d" % i], len(off))
-        ap = piece(T, peer, i, h)
-        g.remote_dma_fused([transfer(T, topo, core, cores[q], es[:k], "vf", ap, ap), transfer(T, topo, core, cores[sib], es[k:], "vf", ap, ap)],
-                           local_sem=T.sem.rl)
-    g.wait_ge(T.sem.rl, 2 * (len(off) + len(on)) + 4 * k)
+def lander(q, h, cores, topo):
+    if h == 0 or not TWO_PLANES:
+        return [helpers(q, cores, topo)[2 if THIRD else h]]
+    return [c for c in range(WORLD) if topo.mates(c, cores[q]) and topo.die(c) == topo.die(cores[q]) and topo.may_write(c, cores[q])][:NM]
+
+
+def helper_program(g, core, cores, T, topo):
+    sent = 0
+    for q in range(len(cores)):
+        sib, far, peer = roles(q, cores, topo)
+        for h in range(2):
+            if helpers(q, cores, topo)[h] == core:
+                across = lander(peer, h, cores, topo)
+                n = len(across)
+                off = topo.engines(core, across[0])
+                es = topo.engines(core, cores[q])
+                on = [e for e in es if e not in off]
+                for x, (i, u, m) in enumerate(STEPS):
+                    if u == 0:
+                        g.wait_ge(T.sem["va%d" % i], len(es) // 2)
+                    trs = []
+                    for j, c in enumerate(across):
+                        ap = piece(T, q, i, h, n * u + j, n * m)
+                        trs += [transfer(T, topo, core, c, off[len(off) // n * j:len(off) // n * (j + 1)], "vb%d" % x, ap, ap),
+                                transfer(T, topo, core, cores[sib], on[len(on) // n * j:len(on) // n * (j + 1)], "vs", ap, ap)]
+                    g.remote_dma_fused(trs, local_sem=T.sem.rl)
+                    sent += len(es)
+        for h in range(2):
+            here = lander(q, h, cores, topo)
+            if core in here:
+                es = topo.engines(core, cores[q])
+                k = len(es) // 2
+                for x, (i, u, m) in enumerate(STEPS):
+                    g.wait_ge(T.sem["vb%d" % x], len(topo.engines(helpers(peer, cores, topo)[h], core)) // len(here))
+                    ap = piece(T, peer, i, h, len(here) * u + here.index(core), len(here) * m)
+                    g.remote_dma_fused([transfer(T, topo, core, cores[q], es[:k], "vf", ap, ap),
+                                        transfer(T, topo, core, cores[sib], es[k:], "vf", ap, ap)], local_sem=T.sem.rl)
+                    sent += len(es)
+    if sent:
+        g.wait_ge(T.sem.rl, sent)
 
 
 def rank_program(g, core, T, topo):
@@ -94,10 +130,7 @@ def rank_program(g, core, T, topo):
     N = len(cores)
     r = T.rank_of(core)
     if r is None:
-        for q in range(N):
-            hs = helpers(q, cores, topo)
-            if core in hs:
-                helper_program(g, core, q, hs.index(core), cores, T, topo)
+        helper_program(g, core, cores, T, topo)
         return
     sib, far, peer = roles(r, cores, topo)
     others = far + [sib]
@@ -107,6 +140,7 @@ def rank_program(g, core, T, topo):
     half = len(off_eng) // 2
     n_off, n_on, n_all = len(off_eng), len(on_eng), len(all_eng)
     eng_to = {far[0]: off_eng[:half], far[1]: off_eng[half:], sib: on_eng}
+    n_vf = sum(len(STEPS) * len(topo.engines(c, core)) // 2 for q in (r, sib) for h in range(2) for c in lander(q, h, cores, topo))
     hf, hn = far[0] // 2, r // 2
 
     Q = {"g": g, "v": g.vector, "s": g.scalar, "t": g.tensor, "y": g.sync}
@@ -167,8 +201,11 @@ def rank_program(g, core, T, topo):
     def to(qs, sem, src, dst):
         return [(cores[q], eng_to[q], sem, src(q), dst) for q in qs]
 
-    for tok, sem, val in (("vs", "vs", 4 * n_on), ("vf", "vf", 4 * n_all), ("land_s", "ts", n_on), ("land_o", "to", n_off),
-                          ("cntL", "ca", n_on + n_off), ("msgL", "ma", n_on + n_off), ("Yl_r", "ya", n_on + n_off)):
+    def one(q, sem, src, dst):
+        return [(cores[q], on_eng if q == sib else off_eng, sem, src, dst)]
+
+    for tok, sem, val in (("vs", "vs", 2 * len(STEPS) * n_on), ("vf", "vf", n_vf), ("land_s", "ts", n_on), ("land_o", "to", n_off),
+                          ("cntL", "ca", n_on + n_off), ("msgL", "ma", n_on + n_off), ("Yl_r", "ya", n_on + (2 if YSPLIT else 1) * n_off)):
         wr[tok] = [(sem, val, {})]
         count[sem] = val
 
@@ -236,7 +273,17 @@ def rank_program(g, core, T, topo):
 
     def val_out(i):
         send([(hs[h], all_eng[n_all // 2 * h:n_all // 2 * (h + 1)], "va%d" % i, piece(T, r, i, h), piece(T, r, i, h)) for h in range(2)],
-             ["own0", "own1", "gap0"] if i == 0 else ["own2", "gap1"])
+             loaded[i] + ["gap0", "gap1"])
+
+    loaded = []
+
+    def val_in(i):
+        loaded.append([])
+        for lo, hi, shift in ((0, NV // 2, 0), (NV // 2 + GAP, 2048 + GAP, GAP)):
+            a, b = max(lo, CUTS[i]), min(hi, CUTS[i + 1])
+            if a < b:
+                loaded[i].append("own%d" % a)
+                dma("sy"[i], T.allv[:, own + a:own + b], T.val[:, a - shift:b - shift], [], [loaded[i][-1]])
 
     for q, src, dst, tag in (("y", T.ent, T.entI, "ent"), ("s", T.att, T.attI, "att")):
         dma(q, dst[:, KV:128], src[:, NV:2048], [], [tag + "S"])
@@ -246,36 +293,41 @@ def rank_program(g, core, T, topo):
     ms(T.zeroB[:], 0.0, ["zeroB"])
     ms(T.zero[:], 0.0, ["zero"])
     iota(T.baseS[:], [[1, KS // 3], [KS, 16]], NV - 742, 0, ["baseS"])
-    for k in range(2):
-        dma("ys"[k], T.winV[0:128:16, 8192 * k:8192 * (k + 1)], T.zeroB[:], ["zeroB"], ["winV%d" % k])
-    for k in range(2):
-        dma("ys"[k], T.winS[0:128:16, 8192 * k:8192 * (k + 1)], T.zero[:], ["zero"], ["winS%d" % k])
     n1 = NV // 2
-    dma("y", T.allv[:, own:own + n1], T.val[:, 0:n1], [], ["own0"])
-    dma("y", T.allv[:, own + n1 + GAP:own + 1024 + GAP], T.val[:, n1:1024], [], ["own1"])
-    dma("y", T.allv[:, own + 1024 + GAP:own + 2048 + GAP], T.val[:, 1024:2048], [], ["own2"])
+    for what in EARLY:
+        if what == "fillV":
+            for k in range(2):
+                dma("ys"[k], T.winV[0:128:16, 8192 * k:8192 * (k + 1)], T.zeroB[:], ["zeroB"], ["winV%d" % k])
+        if what == "fillS":
+            for k in range(2):
+                dma("y", T.winS[0:128:16, 8192 * k:8192 * (k + 1)], T.zero[:], ["zero"], ["winS%d" % k])
+        if what[:3] == "val":
+            val_in(int(what[3]))
     for gl in range(2):
         dma("y", T.formI[:, gl, :], T.form[gl::2, :], [], ["formI%d" % gl])
     iota(T.baseV[:], [[1, KV], [KV, 4]], 0, 0, ["baseV"])
     iota(T.payV[:, 0::4], [[1, KV], [KV, 4]], 255 - MID, 0, ["payV0"])
     iota(T.payV[:, 3::4], [[1, KV], [KV, 4]], 12 * KV + GAP - MID - 255, 0, ["payV3"])
+    act(T.allv[:, own + n1:own + n1 + GAP], T.zeroB[:, 0:GAP], ACT.Silu, ["zeroB"], ["gap0"])
     for k in range(3):
         act(blk(T.payS, k, 1, 16 * KS // 3), T.baseS[:], ACT.Silu, ["baseS"], ["payS%d" % k], bias=float(KS // 3 * k))
     ms(T.ones[:], 1.0, ["ones"])
     ms(T.clsI[:], 0, ["clsI%d" % k for k in range(8)])
     for k in range(8):
         dma("y", T.clsI[32 * (k // 2):32 * (k // 2) + 16, 16 * (k % 2):16 * (k % 2) + 16], T.cls[k:k + 1, :], [], ["clsI%d" % k])
-    ms(T.w0[:, 0:32], 0.125, ["w0"])
-    ms(T.w1[:], 0.0, ["w1"])
-    for m in (1, 2):
-        ts(T.payV[:, m::4], T.baseV[:], float(4 * KV * m + GAP * (m - 1) - MID), 1.0 / 256, ADD, MUL, ["baseV"], ["payV%d" % m])
-    ts(T.kI[:], T.attI[:], 512, None, MUL, None, att, ["kI"])
-    ts(T.kJ[:], T.entI[:], 512.0, 7680.0, ALU.is_ge, MUL, ent, ["kJ"])
-    tt(T.kI[:], T.kI[:], T.entI[:], ADD, ["kI"] + ent, ["kI"])
-    ms(T.allv[:, own + n1:own + n1 + GAP], 0.0, ["gap0"])
-    tt(T.kI[:], T.kI[:], T.kJ[:], ADD, ["kI", "kJ"], ["kI"])
     ms(T.allv[:, own + 2048 + GAP:own + REG], 0.0, ["gap1"])
+    ms(T.w0[:, 0:32], 0.125, ["w0"])
+
+    def small(m):
+        ts(T.payV[:, m::4], T.baseV[:], float(4 * KV * m + GAP * (m - 1) - MID), 1.0 / 256, ADD, MUL, ["baseV"], ["payV%d" % m])
+    ts(T.P0[:, 0:128], T.attI[:], 512.0, None, MUL, None, att, ["P0"])
+    ts(T.P1[:, 0:128], T.entI[:], 512.0, 7680.0, ALU.is_ge, MUL, ent, ["P1"])
+    tt(T.kI[:], T.entI[:], T.P0[:, 0:128], ADD, ent, ["P0", "kI"])
+    ms(T.w1[:], 0.0, ["w1"])
+    tt(T.kI[:], T.kI[:], T.P1[:, 0:128], ADD, [], ["P1", "kI"])
+    small(1)
     cp(T.kU[:], T.kI[:], ["kI"], ["kU"])
+    small(2)
     cp(T.winV[:, 0:16384].indirect(T.kU[:, 0:KV]), T.payV[:], ["kU"] + ["payV%d" % k for k in range(4)], ["winV0", "winV1"])
     for h in (hf, hn):
         dma("y", blk(T.tlV, h, 1, 512), T.winV[0:128:16, 8192 * h:8192 * (h + 1)], ["winV0", "winV1"], ["tlV%d" % h])
@@ -283,18 +335,20 @@ def rank_program(g, core, T, topo):
     for h, q in ((hf, "s"), (hn, "y")):
         dma(q, blk(T.tlS, h, 1, 512), T.winS[0:128:16, 8192 * h:8192 * (h + 1)], ["winS0", "winS1"], ["tlS%d" % h])
 
+    val_out(0)
     sel(T.Id[:], T.ones[:, 0:160], [[-1, 160]], ALU.is_equal, 16, 1, ["ones"], ["Id"])
     sel(T.GB[:], T.ones[:, 0:160], [[-16, 10], [0, 16]], ALU.is_ge, 16, 1, ["ones"], ["GB"])
     iota(T.w0[:, 32:64], [[0, 32]], 8, 0, ["w0h"])
     sel(T.GB[:], T.GB[:], [[16, 10], [0, 16]], ALU.is_ge, -1, -1, ["GB"], ["GB"])
+    val_out(1)
     before("g", ["w0", "w0h", "w1"], [])
     for a in (0, 1):
         iota(T.w0[:, a::16], [[0, 4]], 0, 0, ["w0%d" % a])
-    val_out(0)
     iota(T.w0[:, 8:32:16], [[0, 2]], 0, 0, ["w08"])
     for h, a, c in ((0, 0, 2 ** 21), (0, 1, -3 * 8 ** 6), (1, 0, 2 ** 23), (1, 8, -3)):
         iota(T.w1[:, 32 * h + a:32 * h + 32:16], [[0, 2]], c, 0, ["w1%d%d" % (h, a)])
-    val_out(1)
+    for i in range(2, NP):
+        val_out(i)
     iota(T.rows[:, 192:224], [[0, 32]], -192, 0, ["rows6"])
     iota(T.rows[:, 64:96], [[0, 2], [1, 16]], 0, 0, ["rows2"])
     iota(T.rows[:, 192:224:4], [[0, 8]], 576, 0, ["rows6"])
@@ -302,9 +356,6 @@ def rank_program(g, core, T, topo):
     iota(T.rows[:, 192:224:16], [[0, 2]], -1024, 0, ["rows6"])
     iota(T.rows[:, 128:160], [[-1, 2], [0, 16]], 1, 0, ["rows4"])
     iota(T.rows[:, 160:192], [[1, 2], [0, 16]], 0, 0, ["rows5"])
-    sel(T.INC[:], T.GB[:], [[1, 160]], ALU.is_ge, -16, -1, ["GB"], ["INC"])
-    iota(T.dI[:], [[1, 132]], 127, -1, ["dI"], False)
-    sel(T.INC[:], T.INC[:], [[1, 160]], ALU.not_equal, -16, -1, [], ["INC"], fill=0.5)
 
     fo = ["formI0", "formI1"]
     ts(T.fI[:, 0], T.formI[:], 15, None, AND, None, fo, ["fI0"])
@@ -314,138 +365,140 @@ def rank_program(g, core, T, topo):
     for gl in range(2):
         cp(T.fB[:, :, gl, :], T.fI[:, :, gl, :], ["fI0", "fI1", "fI2"], ["fB%d" % gl])
     fB = ["fB0", "fB1"]
+    for i, c in ((1, 256.0), (2, 16.0)):
+        act(T.IdS[:, i, :], Id, ACT.Identity, ["Id"], ["IdS%d" % i], scale=c)
+    fill(T.mone[:, 0:256], 256, -1.0, ["mone"])
     act(T.E1[:], T.fB[:], ACT.Silu, fB, ["E1"], bias=POW0, scale=POW1)
     act(T.E2[:], T.fB[:], ACT.Silu, fB, ["E2"], bias=POW0 + 15 * POW1, scale=-POW1)
-    for i, c in ((1, 256.0), (2, 16.0)):
-        ts(T.IdS[:, i, :], Id, c, None, MUL, None, ["Id"], ["IdS%d" % i])
     mm([(T.P7[:, 256:384], Id if i == 0 else T.IdS[:, i, :], T.fB[:, 4 * i:4 * (i + 1)], i == 0, i == 2) for i in range(3)], fB + ["IdS1", "IdS2"], ["P7"])
+    PV = (T.P5, T.P6)
+    mm([(PV[hf][:], Id, blk(T.tlV, hf, 1, 512), True, True)], ["tlV%d" % hf], ["PV%d" % hf])
     for k, E in enumerate((T.E1, T.E2)):
         mm([(blk(T.P7, k, 1, 128), T.IdS[:, 0, :], blk(E, i, 1, 128), i == 0, i == 2) for i in range(3)], ["IdS0", "E%d" % (k + 1)], ["P7"])
-    PV = (T.P5, T.P6)
-    for h in (hf, hn):
-        mm([(PV[h][:], Id, blk(T.tlV, h, 1, 512), True, True)], ["tlV%d" % h], ["PV%d" % h])
+    mm([(PV[hn][:], Id, blk(T.tlV, hn, 1, 512), True, True)], ["tlV%d" % hn], ["PV%d" % hn])
     cl = ["clsI%d" % k for k in range(8)]
     ts(T.clsI[:], T.clsI[:], 129, None, MUL, None, [], cl)
-    ms(T.mone[:], -1.0, ["mone"])
-    ts(T.clsI[:], T.clsI[:], 2, 127, SHR, AND, [], cl)
     scan(T.rows[:, 0:64], T.w0[:], T.w1[:], 0.0, MUL, ADD, ["w00", "w01", "w08", "w100", "w101", "w110", "w118"], ["rows0"])
-    cp(T.clsF[:], T.clsI[:], cl, ["clsF"])
-    ms(T.H[:], 0.0, ["H"])
-    tr(T.clsT[:], T.clsF[:], ["clsF"], ["clsT"])
+    ts(T.clsI[:], T.clsI[:], 2, 127, SHR, AND, [], cl)
     tr(T.cols[:], T.rows[:], ["rows0"] + ["rows%d" % k for k in range(2, 7)], ["cols"])
+    cp(T.clsF[:], T.clsI[:], cl, ["clsF"])
+    tr(T.clsT[:], T.clsF[:], ["clsF"], ["clsT"])
+    tt(blk(T.tq, hf, 1, 512), blk(T.tlS, hf, 1, 512), PV[hf][:], ADD, ["tlS%d" % hf], ["PV%d" % hf, "tqf"])
     cp(T.clsU[:], T.clsT[:, 0:16], ["clsT"], ["clsU"])
     tr(T.tabW[:], T.P7[:, 0:384], [], ["P7", "tabW"])
-    cp(T.Id16[:, 0, :], Id, ["Id"], ["Id16"])
-    ts(T.Id16[:, 1, :], Id, 255.0, None, MUL, None, ["Id"], ["Id255"])
-    for q in range(1, N):
-        act(T.IdS[:, 2 + q, :], Id, ACT.Identity, ["Id"], ["IdQ%d" % q], scale=float(REG * q))
     for k in range(2):
         act(T.Wn[:, k, :], GB, ACT.Identity, ["GB", "cols"], ["Wn%d" % k], scale=col(k))
-    act(T.frm[:], blk(T.tabW, 2, 1, 128).indirect(T.clsU[:, 0:16]), ACT.Identity, ["tabW", "clsU"], ["frm"], bias=1.0 - 2049.0 / 8192, scale=-1.0 / 8192)
-    for k in range(2):
-        act(blk(T.tabR, k), blk(T.tabW, k, 1, 128).indirect(T.clsU[:, 0:16]), ACT.Identity, ["tabW", "clsU"], ["tabR%d" % k], bias=2.0 ** 23)
+    for q in range(1, N):
+        act(T.IdS[:, 2 + q, :], Id, ACT.Identity, ["Id"], ["IdQ%d" % q], scale=float(REG * q))
+    act(T.Id32[:], Id, ACT.Identity, ["Id"], ["Id32"])
     for x in range(2):
         act(T.IM[:, x, :], T.Id[:], ACT.Identity, ["Id", "cols"], ["IM%d" % x], scale=col(4 + x))
-    for x in range(2):
-        act(T.TM[:, x, :], T.INC[:], ACT.Identity, ["INC", "cols"], ["TM%d" % x], scale=col(4 + x))
+    for k in range(2):
+        act(blk(T.tabR, k), blk(T.tabW, k, 1, 128).indirect(T.clsU[:, 0:16]), ACT.Identity, ["tabW", "clsU"], ["tabR%d" % k], bias=2.0 ** 23)
+    act(T.IdS[:, 7, :], Id, ACT.Identity, ["Id"], ["Id255"], scale=255.0)
+    act(T.IdS[:, 6, :], Id, ACT.Identity, ["Id"], ["IdN"], scale=-2.0 * REG)
     fill(T.cum[:, 0:16], 16, 0.0, ["cum0"])
     fill(T.Gw[:, 0:768], 768, -0.25, ["Gw"])
-    fill(T.Yl[:, 768:784], 16, 0.0, ["Yl_z"])
-    fill(T.EL[:, 768:776], 8, -1.0, ["EL_z"])
+    fill(T.mone[:, 256:768], 512, -1.0, ["mone2"])
     act(T.cv[:, 0:1], col(6), ACT.Identity, ["cols"], ["cv"])
+    act(T.IdS[:, 8, :], Id, ACT.Identity, ["Id", "cols"], ["IdP"], scale=col(2))
 
     def near(A, q):
         return A[:, 256 * (q % 2):256 * (q % 2 + 1)]
-    sel(T.H[:, 15::16], T.ones[:, 0:9], [[-16, 9]], ALU.is_ge, 0, 1, ["ones"], ["H"])
-    sel(T.STR[:], GB, [[1, 128]], ALU.is_gt, 0, -1, ["GB"], ["STR"])
-    sel(T.H[:, 15::16], T.H[:, 15::16], [[16, 9]], ALU.is_ge, 15, -1, [], ["H"])
-    tt(blk(T.tq, hf, 1, 512), blk(T.tlS, hf, 1, 512), PV[hf][:], ADD, ["tlS%d" % hf], ["PV%d" % hf, "tqf"])
+    iota(T.TR[:], [[1, 16]], 768, 16, ["TR"])
+    iota(T.sw[:], [[16, 48]], 0, 0, ["sw"])
+    sel(T.INC[:], T.GB[:], [[1, 160]], ALU.is_ge, -16, -1, ["GB"], ["INC"])
+    sel(T.H[:], T.GB[:, 16:160], [[0, 9], [1, 16]], ALU.is_equal, -15, 0, ["GB"], ["H"])
     send(to(far, "to", lambda q: blk(T.tq, q), blk(T.land, r)), ["tqf"])
     tt(blk(T.tq, sib), blk(T.tlS, sib), near(PV[hn], sib), ADD, ["tlS%d" % hn], ["PV%d" % hn, "tqs"])
     send(to([sib], "ts", lambda q: blk(T.tq, q), blk(T.land, r)), ["tqs"])
     tt(blk(T.land, r), blk(T.tlS, r), near(PV[hn], r), ADD, [], ["PV%d" % hn, "land_r"])
+    sel(T.INC[:], T.INC[:], [[1, 160]], ALU.not_equal, -16, -1, [], ["INC"], fill=0.5)
+    sel(T.dA[0:4, :], T.ones[0:4, 0:132], [[0, 33], [1, 4]], ALU.is_equal, 0, -1, ["ones"], ["dA"])
+    sel(T.dN[0:4, :], T.zeroB[0:4, 0:132], [[0, 33], [1, 4]], ALU.not_equal, 0, -1, ["zeroB"], ["dN"], fill=-1.0)
+    sel(T.STR[:], GB, [[1, 128]], ALU.is_gt, 0, -1, ["GB"], ["STR"])
     sel(T.DT[:], T.STR[:], [[-4, 32], [0, 4]], ALU.is_ge, 0, 1, ["STR"], ["DT"])
-    iota(T.TR[:], [[1, 16]], 768, 16, ["TR"])
-    iota(T.wid[:], [[1, 2], [2, 8], [16, 16]], 0, 0, ["wid"])
-    iota(T.sw[:], [[16, 48]], 0, 0, ["sw"])
+    iota(T.wid[:], [[1, 16], [16, 16]], 0, 0, ["wid"])
+    iota(T.Ww[:, 0:768], [[0, 768]], 0, 0, ["Ww"])
+    for x in range(2):
+        act(T.TM[:, x, :], T.INC[:], ACT.Identity, ["INC", "cols"], ["TM%d" % x], scale=col(4 + x))
     act(T.H4[:], T.H[:], ACT.Identity, ["H"], ["H4"], scale=4096.0)
+    act(T.Hn[:], T.H[:], ACT.Identity, ["H"], ["Hn"], scale=-1.0)
 
-    def marks(q, n, R, tag):
+    def mark(q, n, R, tag):
         ts(blk(T.pres, q, n), blk(T.land, q, n), 0.0, None, ALU.not_equal, None, R, ["pres" + tag])
-        ts(blk(T.clp, q, n), blk(T.land, q, n), -1.0, 1.0, ALU.max, ALU.min, R, ["clp" + tag])
-    ms(T.Ww[:, 0:768], 0.0, ["Ww"])
-    marks(r, 1, ["land_r"], "r")
+    ts(T.frm[:], blk(T.tabW, 2, 1, 128).indirect(T.clsU[:, 0:16]), -1.0 / 8192, 2047.0 / 8192, MUL, ADD, ["tabW", "clsU"], ["frm"])
+    mark(r, 1, ["land_r"], "r")
     tr(T.frmT[:], T.frm[:], ["frm"], ["frmT"])
-    ts(T.dI[:], T.dI[:], 3, None, AND, None, [], ["dI"])
-    ts(T.Hn[:], T.H[:], -1.0, None, MUL, None, ["H"], ["Hn"])
-    ts(T.dA[:], T.dI[:], 0.0, None, ALU.is_equal, None, ["dI"], ["dA"])
-    marks(sib, 1, ["land_s"], "s")
+    mark(sib, 1, ["land_s"], "s")
 
     def digits(k, qs, first, last):
         o = (T.P0, T.P1)[k][:, 0:256]
         return ([(o, T.Wn[:, k, :], T.mone[:, 0:256], True, False)] if first else []) + \
             [(o, T.Wn[:, k, :], blk(T.pres, q), False, last and q == qs[-1]) for q in qs]
 
-    def places(qs, first, last):
-        o, out = T.P2[:, 0:256], []
-        for q in qs:
-            if q:
-                out.append((o, T.IdS[:, 2 + q, :], blk(T.pres, q), first and not out, False))
-            out.append((o, T.Id16[:, 0, :], blk(T.land, q), first and not out, False))
-            out.append((o, T.Id16[:, 1, :], blk(T.clp, q), False, last and q == qs[-1]))
-        return out
+    def tables(A, qs, first, last):
+        return [(A[:, 0:256], Id, blk(T.land, q), first, last and q == qs[-1]) for q in qs]
+
+    def shifts(qs):
+        return [(T.P4[:, 0:256], T.IdS[:, 2 + q, :], blk(T.pres, q), False, False) for q in qs if q]
 
     def turned(M, src, last):
-        return [(T.P3[:, 128 * x:128 * (x + 1)], M[:, x, 16 - 16 * (gl - x):144 - 16 * (gl - x)], src[:, :, gl, :], False, last and x + gl == 2)
+        return [(T.P3[:, :, x, :], M[:, x, 16 - 16 * (gl - x):144 - 16 * (gl - x)], src[:, :, gl, :], False, last and x + gl == 2)
                 for x in range(2) for gl in range(2)]
 
     IdQ = ["IdQ%d" % q for q in range(1, N)]
-    mm(digits(0, [r], True, False), ["Wn0", "mone", "presr"], ["P0"])
-    mm(digits(1, [r], True, False), ["Wn1"], ["P1"])
-    mm(places([r], True, False), ["Id16", "Id255", "land_r", "clpr"] + IdQ, ["P2"])
+    mm(digits(0, [], True, False), ["Wn0", "mone"], ["P0"])
+    mm(digits(1, [], True, False), ["Wn1"], ["P1"])
+    mm([(T.P6[:, 0:16], T.Id32[:], T.TR[:], True, False)], ["TR", "Id32"], ["PV1"])
+    mm(tables(T.P2, [r], True, False), ["land_r"], ["P2"])
+    mm(tables(T.P4, [r], True, False), [], ["P4"])
+    mm(digits(0, [r], False, False), ["presr"], ["P0"])
+    mm(digits(1, [r], False, False), [], ["P1"])
+    mm(tables(T.P2, [sib], False, False), ["land_s"], ["P2"])
     mm(digits(0, [sib], False, False), ["press"], ["P0"])
-    mm(digits(1, [sib], False, False), [], ["P1"])
-    mm(places([sib], False, False), ["land_s", "clps"], ["P2"])
 
-    marks(far[0], 2, ["land_o"], "o")
+    mm(tables(T.P2, far, False, True), ["land_o"], ["P2"])
+    mark(far[0], 2, ["land_o"], "o")
+    ts(T.clp[:], T.P2[:, 0:256], -1.0, 1.0, ALU.max, ALU.min, [], ["P2", "clp"])
     mm(digits(0, far, False, True), ["preso"], ["P0"])
-    mm(digits(1, far, False, True), [], ["P1"])
-    mm(places(far, False, True), ["land_o", "clpo"], ["P2"])
-    mm([(T.P3[:, 0:256], Id, T.mone[:, 0:256], True, False)] + turned(T.IM, T.frmT, False), ["IM0", "IM1", "frmT"], ["P3"])
-    tt(T.dB[:], T.dA[:, 0:128], T.dA[:, 1:129], ALU.subtract, ["dA"], ["dB"])
+    mm(digits(1, others, False, True), [], ["P1"])
+    mm(tables(T.P4, others, False, False) + shifts(range(N)) + [(T.P4[:, 0:256], T.IdS[:, 7, :], T.clp[:], False, True)],
+       ["clp", "Id255"] + IdQ, ["P4"])
+    mm([(T.P3[:], Id, T.mone[:, 0:256], True, False)] + turned(T.IM, T.frmT, False), ["IM0", "IM1", "frmT"], ["P3"])
+    mm([(T.P2[:, 0:128], T.dA[0:4, 1:129], T.dA[0:4, 0:128], True, False), (T.P2[:, 0:128], T.dA[0:4, 1:129], T.dN[0:4, 1:129], False, True)],
+       ["dA", "dN"], ["P2"])
     tt(blk(T.U, 0), blk(T.tabR, 0), T.P0[:, 0:256], ADD, ["tabR0"], ["P0", "U0"])
     tt(blk(T.U, 1), blk(T.tabR, 1), T.P1[:, 0:256], ADD, ["tabR1"], ["P1", "U1"])
     ts(blk(T.U, 0), blk(T.U, 0), 4 * DIG, None, AND, None, [], ["U0"])
     ts(blk(T.U, 1), blk(T.U, 1), 4 * DIG, 1, AND, SHR, [], ["U1"])
-    ts(T.posU[:], T.P2[:, 0:256], float(MID), None, ADD, None, [], ["P2", "posU"])
-    gather(T.VT[:], T.allv[:, 0:4 * REG].indirect(T.posU[:, 0:256]), ACT.Copy, ["posU", "own0", "own1", "own2", "gap0", "gap1", "vs", "vf"], ["VT"])
+    ts(T.posU[:], T.P4[:, 0:256], float(MID), None, ADD, None, [], ["P4", "posU"])
+    gather(T.VT[:], T.allv[:, 0:4 * REG].indirect(T.posU[:, 0:256]), ACT.Copy, ["posU", "gap0", "gap1", "vs", "vf"] + sum(loaded, []), ["VT"])
     tt(T.ok[:], blk(T.U, 0), blk(T.U, 1), ALU.is_equal, ["U0", "U1"], ["ok"])
-    iota(T.lo[:], [[1, 256]], 0, 0, ["lo"])
 
     scan(T.cum[:, 16:272], T.ones[:, 0:256], T.ok[:], 0.0, MUL, ADD, ["ones", "ok"], ["cum"])
     tr(T.okT[:], T.ok[:], ["ok"], ["okT"])
     mine_n = T.cum[:, 271:272]
+    lo_, hi_ = T.cum[:, 15:271:16], T.cum[:, 31:272:16]
+    mm([(T.P6[:, 0:16], T.IdS[:, 4, :], lo_, False, False), (T.P6[:, 0:16], T.IdS[:, 6, :], hi_, False, True)], ["cum", "cum0", "IdN"], ["PV1"])
     mm([(T.P4[:, 0:1], T.DT[:], mine_n, True, True)], ["DT", "cum"], ["P4"])
     mm(turned(T.TM, T.okT, True), ["TM0", "TM1", "okT"], ["P3"])
     send(to(others, "ca", lambda q: T.cum[:, 264:272], blk(T.cntL, r, 1, 8)), ["cum"])
-    lo_, hi_ = T.cum[:, 15:271:16], T.cum[:, 31:272:16]
-    tt(T.tz[:], lo_, hi_, ALU.is_equal, ["cum", "cum0"], ["tz"])
-    ts(T.sw16[:], T.sw[:], col(2), None, ADD, None, ["sw", "cols"], ["sw16"])
-    tt(T.tz[:], T.tz[:], T.TR[:], MUL, ["TR"], ["tz"])
-    tt(T.tz[:], T.tz[:], lo_, ALU.max, [], ["tz"])
-    ts(T.Gt[:], T.P3[:, 0:256], -0.25, None, ALU.max, None, [], ["P3", "Gt"])
-    for x in range(2):
-        ts(T.offU[:, 8 * x:8 * (x + 1)], T.tz[:, x::2], T.P4[:, 0:1], col(3), ADD, ADD, ["tz", "cols"], ["P4", "offU%d" % x])
+    cp(T.dB[:], T.P2[:, 0:128], [], ["P2", "dB"])
+    tt(T.tz[:], lo_, T.P6[:, 0:16], ALU.max, ["cum0"], ["PV1", "tz"])
+    ts(T.offU[:], T.tz[:], T.P4[:, 0:1], col(3), ADD, ADD, ["tz", "cols"], ["P4", "offU"])
+    ts(T.Gt[:], T.P3[:], 0.5, -0.25, ADD, ALU.max, [], ["P3", "Gt"])
     sel(T.Sel[:], T.ones[:], [[1, 4], [-64, 8], [-1, 16]], ALU.is_equal, -16 * r, 4, ["ones"], ["Sel"])
     sel(T.DD[:], T.dB[:], [[-16, 8], [0, 16]], ALU.is_ge, 0, 1, ["dB"], ["DD"])
-    sel(T.STR[:, 0::16], T.GB[:, 16:144:16], [[0, 8]], ALU.is_ge, 0, 0, ["GB"], ["STR"])
     sel(T.DD[:], T.DD[:], [[1, 128]], ALU.is_gt, 0, -1, [], ["DD"])
+    sel(T.STR[:, 0::16], T.GB[:, 16:144:16], [[0, 8]], ALU.is_ge, 0, 0, ["GB"], ["STR"])
+    iota(T.lo[:], [[1, 256]], 0, 0, ["lo"])
     iota(T.Et[:], [[1, 1024]], 0, 0, ["Et"])
-    oU = ["offU0", "offU1"]
+    oU = ["offU"]
     cp(T.Ww[:, 0:WIDE].indirect(T.offU[:, 0:16]), T.wid[:], oU + ["wid"], ["Ww"])
     cp(T.Gw[:, 0:WIDE].indirect(T.offU[:, 0:16]), T.Gt[:], oU + ["Gt"], ["Gw"])
     scan(T.Ws[:], T.Ww[:, 0:768], T.Ww[:, 0:768], 0.0, ALU.max, ALU.max, ["Ww"], ["Ws"])
-    scan(T.Ds[:], T.mone[:], T.Gw[:, 0:768], -0.25, ADD, ALU.max, ["Gw", "mone"], ["Ds"])
+    scan(T.Ds[:], T.mone[:], T.Gw[:, 0:768], -0.25, ADD, ALU.max, ["Gw", "mone", "mone2"], ["Ds"])
 
     def cn(q):
         return mine_n if q == r else T.cntL[:, 8 * q + 7:8 * q + 8]
@@ -453,28 +506,31 @@ def rank_program(g, core, T, topo):
     mm([(T.P1[:, 0:1], blk(T.Sel, 0, 1, 128), cn(q), q == 0, q == N - 1) for q in range(N)], [], ["P1"])
     mm(wrap(T.P5[:, 0:48], T.H4, T.Ws, True, False), ["H4", "Ws"], ["PV0"])
     cp(T.nS[:, 0:1], T.P7[:, 0:1], [], ["P7", "nS"])
-    ts(T.phi[:], T.Ds[:], 8192.0, 2048.0, MUL, ALU.min, ["Ds"], ["phi"])
     m1 = T.mone[:, 0:1]
     mm([x for k in range(3) for x in [(T.P0[:, k:k + 1], T.IdS[:, 1, :], m1, i == 0, False) for i in range(k)]
         + [(T.P0[:, k:k + 1], T.STR[:], T.nS[:, 0:1], k == 0, True)]]
        + [(T.P0[:, 3:4], T.DD[:], T.nS[:, 0:1], True, False), (T.P0[:, 3:4], Id, T.cv[:, 0:1], False, True)], ["STR", "DD", "nS", "cv"], ["P0"])
-    mm(wrap(T.P5[:, 0:48], T.Hn, T.phi, False, True), ["Hn", "phi"], ["PV0"])
-    for k in range(3):
+    for k in range(2):
+        ts(T.phi[:, k::2], T.Ds[:, k::2], 8192.0, 2048.0, MUL, ALU.min, ["Ds"], ["phi%d" % k])
+        mm(wrap(T.P5[:, 0:48], T.Hn, T.phi, False, True)[k::2], ["Hn", "phi%d" % k], ["PV0"])
+
+    def steps(k):
         ts(blk(T.X, k), T.lo[:], T.P0[:, k:k + 1], T.P0[:, 3:4], ALU.is_ge, MUL, ["lo", "P0"], ["X%d" % k])
-    mm([(T.P6[:, 0:48], T.Id16[:, 0, :], T.sw16[:], True, False)] + wrap(T.P6[:, 0:48], T.Hn, T.X, False, True), ["sw16", "X0", "X1", "X2"], ["PV1"])
+    steps(0)
+    steps(1)
 
     ts(T.Z[:], T.P5[:, 0:48], 32767.0, None, ADD, None, [], ["PV0", "Z"])
-    cp(T.co[:, 0:1], T.P1[:, 0:1], [], ["P1", "co"])
-    dma("y", T.cnt[:], T.co[0:128:4, 0:1], ["co"], ["cnt"])
+    steps(2)
+    mm([(T.P6[:, 0:48], Id, T.sw[:], True, False), (T.P6[:, 0:48], T.IdS[:, 8, :], T.ones[:, 0:48], False, False)]
+       + wrap(T.P6[:, 0:48], T.Hn, T.X, False, True), ["sw", "IdP", "X0", "X1", "X2"], ["PV1"])
     ts(T.zI[:, 0, :], T.Z[:], 8, 0xFFF, SHR, AND, ["Z"], ["z0"])
     ts(T.zI[:, 1, :], T.Z[:], 8, 0xFF0, SHR, AND, ["Z"], ["z1"])
-    ts(T.zI[:, 2, :], T.Z[:], 15, None, AND, None, ["Z"], ["z2"])
     cp(T.kL[:, 96:144], T.zI[:, 0, :], ["z0"], ["kB"])
-    tt(T.kF[:, 0:48], T.zI[:, 1, :], T.zI[:, 2, :], ADD, ["z1", "z2"], ["kF0"])
+    ts(T.zI[:, 2, :], T.Z[:], 15, None, AND, None, ["Z"], ["z2"])
     ts(T.zI[:, 3, :], T.Z[:], 4, 15, SHR, AND, ["Z"], ["z3"])
-    ts(T.zI[:, 4, :], T.Z[:], 12, 255, SHR, AND, ["Z"], ["z4"])
-    cp(T.kL[:, 0:48], T.kF[:, 0:48], ["kF0"], ["kA"])
+    tt(T.kF[:, 0:48], T.zI[:, 1, :], T.zI[:, 2, :], ADD, ["z1", "z2"], ["kF0"])
     tt(T.kF[:, 48:96], T.zI[:, 1, :], T.zI[:, 3, :], ADD, ["z1", "z3"], ["kF1"])
+    cp(T.kL[:, 0:48], T.kF[:, 0:48], ["kF0"], ["kA"])
 
     VTw = T.VT[:, 0:4096]
     for d in far + [sib, r]:
@@ -487,30 +543,44 @@ def rank_program(g, core, T, topo):
     def second(d):
         tt(mine if d == r else blk(T.ys, d, 1, 192), VTw.indirect(T.kL[:, 48 + 12 * d:48 + 12 * (d + 1)]), blk(T.tv, d, 1, 192), ADD,
            ["tv%d" % d, "kC"], ["ys%d" % d])
+    def numbers_out(d):
+        second(d)
+        send(one(d, "ya", blk(T.ys, d, 1, 192), mine), ["ys%d" % d])
+    ts(T.zI[:, 4, :], T.Z[:], 12, 255, SHR, AND, ["Z"], ["z4"])
+    first(far[0])
     ts(T.msg[:], T.zI[:, 4, :], 256.0 * r, None, ADD, None, ["z4"], ["msg"])
     send(to(others, "ma", lambda q: blk(T.msg, q, 1, 12), T.msgL[:, 16 * r:16 * r + 12]), ["msg"])
-    first(far[0])
     cp(T.kL[:, 48:96], T.kF[:, 48:96], ["kF1"], ["kC"])
     first(far[1])
-    second(far[0])
-    second(far[1])
-    send(to(far, "ya", lambda q: blk(T.ys, q, 1, 192), mine), ["ys%d" % q for q in far])
+    if YSPLIT:
+        numbers_out(far[0])
+        numbers_out(far[1])
+    else:
+        second(far[0])
+        second(far[1])
+        send(to(far, "ya", lambda q: blk(T.ys, q, 1, 192), mine), ["ys%d" % q for q in far])
     first(sib)
     ts(T.sigU[:], T.P6[:, 0:48], 768.0, None, ALU.min, None, [], ["PV1", "sigU"])
-    second(sib)
-    send(to([sib], "ya", lambda q: blk(T.ys, q, 1, 192), mine), ["ys%d" % sib])
+    numbers_out(sib)
     first(r)
+    cp(T.co[:, 0:1], T.P1[:, 0:1], [], ["P1", "co"])
+    dma("y", T.cnt[:], T.co[0:128:4, 0:1], ["co"], ["cnt"])
     second(r)
+    fill(T.EL[:, 768:776], 8, -1.0, ["EL_z"])
+    fill(T.Yl[:, 768:784], 16, 0.0, ["Yl_z"])
     gather(blk(T.EL, r, 1, 192), T.Et[:, 0:1024].indirect(blk(T.msg, r, 1, 12)), ACT.Copy, ["Et", "msg"], ["EL%d" % r])
     for q in others:
         gather(blk(T.EL, q, 1, 192), T.Et[:, 0:1024].indirect(T.msgL[:, 16 * q:16 * q + 12]), ACT.Copy, ["msgL"], ["EL%d" % q])
 
-    gather(T.wo[:], T.EL[:, 0:776].indirect(T.sigU[:, 0:48]), ACT.Copy, ["EL%d" % q for q in range(N)] + ["EL_z", "sigU"], ["wo"])
-    dma("s", T.who[:], T.wo[0:128:16, :], ["wo"], ["who"])
+    WR = ["EL%d" % q for q in range(N)] + ["EL_z", "sigU"]
+    if WV:
+        cp(T.wo[:, 0:16 * WV], T.EL[:, 0:776].indirect(T.sigU[:, 0:WV]), WR, ["wo0"])
+    gather(T.wo[:, 16 * WV:768], T.EL[:, 0:776].indirect(T.sigU[:, WV:48]), ACT.Copy, WR, ["wo1"])
+    dma("y", T.who[:], T.wo[0:128:16, :], ["wo0", "wo1"], ["who"])
     YR = ["sigU", "Yl_z", "Yl_r", "ys%d" % r]
-    cp(T.yo[:, 0:448], T.Yl[:, 0:784].indirect(T.sigU[:, 0:28]), YR, ["yo0"])
-    dma("y", T.y[:, 0:448], T.yo[:, 0:448], ["yo0"], ["y0"])
-    gather(T.yo[:, 448:768], T.Yl[:, 0:784].indirect(T.sigU[:, 28:48]), ACT.Copy, YR, ["yo1"])
-    dma("s", T.y[:, 448:768], T.yo[:, 448:768], ["yo1"], ["y1"])
+    cp(T.yo[:, 0:16 * YV], T.Yl[:, 0:784].indirect(T.sigU[:, 0:YV]), YR, ["yo0"])
+    dma("y", T.y[:, 0:16 * YV], T.yo[:, 0:16 * YV], ["yo0"], ["y0"])
+    gather(T.yo[:, 16 * YV:768], T.Yl[:, 0:784].indirect(T.sigU[:, YV:48]), ACT.Copy, YR, ["yo1"])
+    dma("s", T.y[:, 16 * YV:768], T.yo[:, 16 * YV:768], ["yo1"], ["y1"])
     for name, val in count.items():
         need("g", (name, val, {}))

from concourse.bass import DstId, RemoteDMATransfer
from concourse.mybir import AluOpType as ALU, ActivationFunctionType as ACT

S, P = "sbuf", "psum"
F32, BF, I32, U16, F16 = "float32", "bfloat16", "int32", "uint16", "float16"
KV, KS = 62, 66
NV = 16 * KV
REG, GAP, MID = 2080, 16, 503
WIDE = 3584
SCRATCH = {
    "entI": (S, [128, 128], I32), "attI": (S, [128, 128], I32), "kI": (S, [128, 128], I32), "kU": (S, [128, 128], U16),
    "formI": (S, [128, 2, 64], I32), "fI": (S, [128, 3, 2, 64], I32), "fB": (S, [128, 12, 2, 16], BF),
    "E1": (S, [128, 384], BF), "E2": (S, [128, 384], BF), "tabW": (S, [128, 384], F32), "tabR": (S, [128, 512], F32),
    "frm": (S, [128, 256], F16), "frmT": (S, [128, 8, 2, 16], F16), "Id32": (S, [128, 128], F32),
    "clsI": (S, [128, 32], I32), "clsF": (S, [128, 32], F32), "clsT": (S, [128, 32], F32), "clsU": (S, [128, 16], U16),
    "zero": (S, [128, 512], F32), "zeroB": (S, [128, 512], BF), "winV": (S, [128, 16384], BF), "winS": (S, [128, 16384], F32), "kJ": (S, [128, 128], I32),
    "payV": (S, [128, NV], F32), "payS": (S, [128, 16 * KS], F32), "baseV": (S, [128, 8 * KV // 2], F32), "baseS": (S, [128, 16 * KS // 3], F32),
    "tlV": (S, [128, 1024], BF), "tlS": (S, [128, 1024], F32), "tq": (S, [128, 1024], F16), "land": (S, [128, 1024], F16),
    "pres": (S, [128, 1024], BF), "clp": (S, [128, 256], F16), "posU": (S, [128, 256], U16),
    "allv": (S, [128, 4 * REG], BF), "VT": (S, [128, 4096], BF), "U": (S, [128, 512], I32), "ok": (S, [128, 256], BF),
    "okT": (S, [128, 8, 2, 16], BF), "cum": (S, [128, 272], BF), "Gt": (S, [128, 256], F32),
    "tz": (S, [128, 16], F32), "offU": (S, [128, 16], U16), "Gw": (S, [128, WIDE], F32), "Ww": (S, [128, WIDE], BF),
    "Ds": (S, [128, 768], F32), "Ws": (S, [128, 768], BF), "phi": (S, [128, 768], F16),
    "wid": (S, [128, 256], BF), "ones": (S, [128, 512], BF), "mone": (S, [128, 768], BF), "lo": (S, [128, 256], BF),
    "Id": (S, [128, 160], BF), "IdS": (S, [128, 9, 128], BF), "GB": (S, [128, 160], BF),
    "STR": (S, [128, 128], BF), "INC": (S, [128, 160], BF), "DT": (S, [128, 128], BF), "DD": (S, [128, 128], BF),
    "TM": (S, [128, 2, 160], BF), "IM": (S, [128, 2, 160], BF), "Wn": (S, [128, 2, 128], BF), "Sel": (S, [128, 512], BF),
    "dN": (S, [128, 132], BF), "dA": (S, [128, 132], BF), "dB": (S, [128, 128], BF),
    "w0": (S, [128, 64], F32), "w1": (S, [128, 64], F32), "rows": (S, [128, 224], F32), "cols": (S, [128, 224], F32),
    "H": (S, [128, 144], BF), "H4": (S, [128, 144], BF), "Hn": (S, [128, 144], BF), "TR": (S, [128, 16], F32),
    "sw": (S, [128, 48], BF),
    "Et": (S, [128, 1024], F32), "EL": (S, [128, 776], F32), "wo": (S, [128, 768], F32),
    "Z": (S, [128, 48], I32), "zI": (S, [128, 5, 48], I32), "kF": (S, [128, 96], I32), "kL": (S, [128, 144], U16),
    "msg": (S, [128, 48], U16), "msgL": (S, [128, 64], U16), "cntL": (S, [128, 32], BF), "nS": (S, [128, 8], BF), "cv": (S, [128, 8], BF),
    "Bv": (S, [128, 768], F32), "tv": (S, [128, 768], F32), "ys": (S, [128, 768], BF),
    "Yl": (S, [128, 784], BF), "yo": (S, [128, 768], BF), "X": (S, [128, 768], F16), "sigU": (S, [128, 48], U16), "co": (S, [128, 4], F32),
    "P0": (P, [128, 512], F32), "P1": (P, [128, 512], F32), "P2": (P, [128, 512], F32), "P3": (P, [128, 8, 2, 16], F32),
    "P4": (P, [128, 512], F32), "P5": (P, [128, 512], F32), "P6": (P, [128, 512], F32), "P7": (P, [128, 512], F32),
}
WORLD = 256
TWO_PLANES = True
NM = 2
EARLY = ["val0", "fillV", "fillS", "val1"]
CUTS = [0, 512, REG]
NP = len(CUTS) - 1
STEPS = [(0, 0, 1), (1, 0, 1)]
THIRD = True
YSPLIT = False
WV, YV = 16, 26
NDMA = 40
SEMAPHORES = ["qg", "qv", "qs", "qt", "rl", "va0", "va1", "va2", "vb0", "vb1", "vb2", "vs", "vf", "ts", "to", "ca", "ma", "ya"] + ["d%d" % i for i in range(NDMA)]
DIG = sum(8 ** k for k in range(8))
POW0, POW1 = -70.10015395, -2.10671760


def msk(es):
    return sum(1 << e for e in es)


def helpers(q, cores, topo):
    free = [c for c in topo.cores_of(cores[q]) if c not in cores and topo.die(c) == topo.die(cores[q])]
    mate = [c for c in range(WORLD) if topo.mates(c, cores[q])][0]
    inner = [c for c in free if not topo.may_write(c, mate)]
    return [inner[0], [c for c in free if topo.may_write(c, mate)][0], inner[1]]


def roles(r, cores, topo):
    others = [q for q in range(len(cores)) if q != r]
    sib = [q for q in others if cores[q] in topo.cores_of(cores[r])][0]
    far = [q for q in others if q != sib]
    peer = [q for q in far if topo.die(cores[q]) == topo.die(cores[r])][0]
    return sib, far, peer


def piece(T, q, i, h, j=0, parts=1):
    n = (CUTS[i + 1] - CUTS[i]) // 2
    c0 = REG * q + CUTS[i] + n * h + n // parts * j
    return T.allv[:, c0:c0 + n // parts]


def transfer(T, topo, core, c, es, sem, src, dst):
    rid, pid = topo.addr(c, core)
    return RemoteDMATransfer(dst_ids=[DstId(rid=rid, pnc=pid)], dma_engine_mask=msk(es), remote_sem=T.sem[sem], src=src, dst=dst)


def lander(q, h, cores, topo):
    if h == 0 or not TWO_PLANES:
        return [helpers(q, cores, topo)[2 if THIRD else h]]
    return [c for c in range(WORLD) if topo.mates(c, cores[q]) and topo.die(c) == topo.die(cores[q]) and topo.may_write(c, cores[q])][:NM]


def helper_program(g, core, cores, T, topo):
    sent = 0
    for q in range(len(cores)):
        sib, far, peer = roles(q, cores, topo)
        for h in range(2):
            if helpers(q, cores, topo)[h] == core:
                across = lander(peer, h, cores, topo)
                n = len(across)
                off = topo.engines(core, across[0])
                es = topo.engines(core, cores[q])
                on = [e for e in es if e not in off]
                for x, (i, u, m) in enumerate(STEPS):
                    if u == 0:
                        g.wait_ge(T.sem["va%d" % i], len(es) // 2)
                    trs = []
                    for j, c in enumerate(across):
                        ap = piece(T, q, i, h, n * u + j, n * m)
                        trs += [transfer(T, topo, core, c, off[len(off) // n * j:len(off) // n * (j + 1)], "vb%d" % x, ap, ap),
                                transfer(T, topo, core, cores[sib], on[len(on) // n * j:len(on) // n * (j + 1)], "vs", ap, ap)]
                    g.remote_dma_fused(trs, local_sem=T.sem.rl)
                    sent += len(es)
        for h in range(2):
            here = lander(q, h, cores, topo)
            if core in here:
                es = topo.engines(core, cores[q])
                k = len(es) // 2
                for x, (i, u, m) in enumerate(STEPS):
                    g.wait_ge(T.sem["vb%d" % x], len(topo.engines(helpers(peer, cores, topo)[h], core)) // len(here))
                    ap = piece(T, peer, i, h, len(here) * u + here.index(core), len(here) * m)
                    g.remote_dma_fused([transfer(T, topo, core, cores[q], es[:k], "vf", ap, ap),
                                        transfer(T, topo, core, cores[sib], es[k:], "vf", ap, ap)], local_sem=T.sem.rl)
                    sent += len(es)
    if sent:
        g.wait_ge(T.sem.rl, sent)


def rank_program(g, core, T, topo):
    cores = list(T.cores)
    N = len(cores)
    r = T.rank_of(core)
    if r is None:
        helper_program(g, core, cores, T, topo)
        return
    sib, far, peer = roles(r, cores, topo)
    others = far + [sib]
    off_eng = topo.engines(core, cores[peer])
    all_eng = topo.engines(core, cores[sib])
    on_eng = [e for e in all_eng if e not in off_eng]
    half = len(off_eng) // 2
    n_off, n_on, n_all = len(off_eng), len(on_eng), len(all_eng)
    eng_to = {far[0]: off_eng[:half], far[1]: off_eng[half:], sib: on_eng}
    n_vf = sum(len(STEPS) * len(topo.engines(c, core)) // 2 for q in (r, sib) for h in range(2) for c in lander(q, h, cores, topo))
    hf, hn = far[0] // 2, r // 2

    Q = {"g": g, "v": g.vector, "s": g.scalar, "t": g.tensor, "y": g.sync}
    known = {k: {} for k in Q}
    count = {}
    wr, rd = {}, {}
    ndma = [0]

    def need(q, ev):
        name, val, snap = ev
        if known[q].get(name, 0) >= val:
            return
        Q[q].wait_ge(T.sem[name], val)
        known[q][name] = val
        for k, x in snap.items():
            if known[q].get(k, 0) < x:
                known[q][k] = x

    def before(q, R, W):
        evs = []
        for t in list(R) + list(W):
            evs += wr.get(t, [])
        for t in W:
            evs += rd.get(t, [])
        for ev in sorted(evs, key=lambda e: -e[1]):
            need(q, ev)

    def after(ev, R, W):
        for t in W:
            wr[t] = [ev]
            rd[t] = []
        for t in R:
            rd.setdefault(t, []).append(ev)

    def do(q, calls, R, W):
        before(q, R, W)
        for c in calls[:-1]:
            c()
        name = "q" + q
        calls[-1]().then_inc(T.sem[name], 1)
        count[name] = count.get(name, 0) + 1
        after((name, count[name], dict(known[q])), R, W)

    def dma(q, out, in_, R, W):
        before(q, R, W)
        name = "d%d" % ndma[0]
        ndma[0] += 1
        Q[q].dma_start(out, in_).then_inc(T.sem[name], 16)
        count[name] = 16
        after((name, 16, dict(known[q])), R, W)

    def send(items, R):
        before("g", R, [])
        for it in items:
            count["rl"] = count.get("rl", 0) + len(it[1])
        g.remote_dma_fused([transfer(T, topo, core, *it) for it in items], local_sem=T.sem.rl)

    def to(qs, sem, src, dst):
        return [(cores[q], eng_to[q], sem, src(q), dst) for q in qs]

    def one(q, sem, src, dst):
        return [(cores[q], on_eng if q == sib else off_eng, sem, src, dst)]

    for tok, sem, val in (("vs", "vs", 2 * len(STEPS) * n_on), ("vf", "vf", n_vf), ("land_s", "ts", n_on), ("land_o", "to", n_off),
                          ("cntL", "ca", n_on + n_off), ("msgL", "ma", n_on + n_off), ("Yl_r", "ya", n_on + (2 if YSPLIT else 1) * n_off)):
        wr[tok] = [(sem, val, {})]
        count[sem] = val

    v, s, t = g.vector, g.scalar, g.tensor

    def ts(out, in0, s1, s2, o0, o1, R, W):
        if o1 is None:
            do("v", [lambda: v.tensor_scalar(out, in0, s1, None, o0)], R, W)
        else:
            do("v", [lambda: v.tensor_scalar(out, in0, s1, s2, o0, o1)], R, W)

    def tt(out, a, b, op, R, W):
        do("v", [lambda: v.tensor_tensor(out, a, b, op)], R, W)

    def cp(out, a, R, W):
        do("v", [lambda: v.tensor_copy(out, a)], R, W)

    def tr(out, a, R, W):
        do("v", [lambda: v.transpose(out, a)], R, W)

    def ms(ap, c, W):
        do("v", [lambda: v.memset(ap, c)], [], W)

    def scan(out, a, b, init, o0, o1, R, W):
        do("v", [lambda: v.tensor_tensor_scan(out, a, b, init, o0, o1)], R, W)

    def act(out, a, fn, R, W, bias=0.0, scale=1.0):
        do("s", [lambda: s.activation(out, a, fn, bias=bias, scale=scale)], R, W)

    def gather(out, a, fn, R, W):
        do("s", [lambda: s.activation(out, a, fn)], R, W)

    def fill(out, n, c, W):
        act(out, T.payS[:, 0:n], ACT.Identity, [], W, bias=c, scale=0.0)

    def mm(groups, R, W):
        calls = []
        for out, a, b, st, sp in groups:
            calls.append(lambda out=out, a=a, b=b, st=st, sp=sp: t.matmul(out, a, b, st, sp))
        do("t", calls, R, W)

    def wrap(out, Hm, src, first, last):
        return [(out, Hm[:, 15 - b:143 - b], src[:, b::16], first and b == 0, last and b == 15) for b in range(16)]

    def iota(out, pat, base, cm, W, flt=True):
        if flt:
            do("g", [lambda: g.iota(out, pat, base, cm, allow_small_or_imprecise_dtypes=True)], [], W)
        else:
            do("g", [lambda: g.iota(out, pat, base, cm)], [], W)

    def sel(out, a, pat, op, base, cm, R, W, fill=0.0):
        do("g", [lambda: g.affine_select(out, a, pat, op, fill, base, cm)], R, W)

    def blk(A, q, n=1, w=256):
        return A[:, w * q:w * (q + n)]

    def col(i):
        return T.cols[:, 32 * i:32 * i + 1]

    AND, SHR = ALU.bitwise_and, ALU.logical_shift_right
    MUL, ADD = ALU.mult, ALU.add
    Id, GB = T.Id[:, 16:144], T.GB[:, 16:144]
    hs = helpers(r, cores, topo)
    own = REG * r

    def val_out(i):
        send([(hs[h], all_eng[n_all // 2 * h:n_all // 2 * (h + 1)], "va%d" % i, piece(T, r, i, h), piece(T, r, i, h)) for h in range(2)],
             loaded[i] + ["gap0", "gap1"])

    loaded = []

    def val_in(i):
        loaded.append([])
        for lo, hi, shift in ((0, NV // 2, 0), (NV // 2 + GAP, 2048 + GAP, GAP)):
            a, b = max(lo, CUTS[i]), min(hi, CUTS[i + 1])
            if a < b:
                loaded[i].append("own%d" % a)
                dma("sy"[i], T.allv[:, own + a:own + b], T.val[:, a - shift:b - shift], [], [loaded[i][-1]])

    for q, src, dst, tag in (("y", T.ent, T.entI, "ent"), ("s", T.att, T.attI, "att")):
        dma(q, dst[:, KV:128], src[:, NV:2048], [], [tag + "S"])
        for m in range(4):
            dma(q, dst[m::4, 0:KV], src[:, 4 * KV * m:4 * KV * (m + 1)], [], [tag + str(m)])
    ent, att = [[tag + x for x in "S0123"] for tag in ("ent", "att")]
    ms(T.zeroB[:], 0.0, ["zeroB"])
    ms(T.zero[:], 0.0, ["zero"])
    iota(T.baseS[:], [[1, KS // 3], [KS, 16]], NV - 742, 0, ["baseS"])
    n1 = NV // 2
    for what in EARLY:
        if what == "fillV":
            for k in range(2):
                dma("ys"[k], T.winV[0:128:16, 8192 * k:8192 * (k + 1)], T.zeroB[:], ["zeroB"], ["winV%d" % k])
        if what == "fillS":
            for k in range(2):
                dma("y", T.winS[0:128:16, 8192 * k:8192 * (k + 1)], T.zero[:], ["zero"], ["winS%d" % k])
        if what[:3] == "val":
            val_in(int(what[3]))
    for gl in range(2):
        dma("y", T.formI[:, gl, :], T.form[gl::2, :], [], ["formI%d" % gl])
    iota(T.baseV[:], [[1, KV], [KV, 4]], 0, 0, ["baseV"])
    iota(T.payV[:, 0::4], [[1, KV], [KV, 4]], 255 - MID, 0, ["payV0"])
    iota(T.payV[:, 3::4], [[1, KV], [KV, 4]], 12 * KV + GAP - MID - 255, 0, ["payV3"])
    act(T.allv[:, own + n1:own + n1 + GAP], T.zeroB[:, 0:GAP], ACT.Silu, ["zeroB"], ["gap0"])
    for k in range(3):
        act(blk(T.payS, k, 1, 16 * KS // 3), T.baseS[:], ACT.Silu, ["baseS"], ["payS%d" % k], bias=float(KS // 3 * k))
    ms(T.ones[:], 1.0, ["ones"])
    ms(T.clsI[:], 0, ["clsI%d" % k for k in range(8)])
    for k in range(8):
        dma("y", T.clsI[32 * (k // 2):32 * (k // 2) + 16, 16 * (k % 2):16 * (k % 2) + 16], T.cls[k:k + 1, :], [], ["clsI%d" % k])
    ms(T.allv[:, own + 2048 + GAP:own + REG], 0.0, ["gap1"])
    ms(T.w0[:, 0:32], 0.125, ["w0"])

    def small(m):
        ts(T.payV[:, m::4], T.baseV[:], float(4 * KV * m + GAP * (m - 1) - MID), 1.0 / 256, ADD, MUL, ["baseV"], ["payV%d" % m])
    ts(T.P0[:, 0:128], T.attI[:], 512.0, None, MUL, None, att, ["P0"])
    ts(T.P1[:, 0:128], T.entI[:], 512.0, 7680.0, ALU.is_ge, MUL, ent, ["P1"])
    tt(T.kI[:], T.entI[:], T.P0[:, 0:128], ADD, ent, ["P0", "kI"])
    ms(T.w1[:], 0.0, ["w1"])
    tt(T.kI[:], T.kI[:], T.P1[:, 0:128], ADD, [], ["P1", "kI"])
    small(1)
    cp(T.kU[:], T.kI[:], ["kI"], ["kU"])
    small(2)
    cp(T.winV[:, 0:16384].indirect(T.kU[:, 0:KV]), T.payV[:], ["kU"] + ["payV%d" % k for k in range(4)], ["winV0", "winV1"])
    for h in (hf, hn):
        dma("y", blk(T.tlV, h, 1, 512), T.winV[0:128:16, 8192 * h:8192 * (h + 1)], ["winV0", "winV1"], ["tlV%d" % h])
    gather(T.winS[:, 0:16384].indirect(T.kU[:, KV:128]), T.payS[:], ACT.Silu, ["kU", "payS0", "payS1", "payS2"], ["winS0", "winS1"])
    for h, q in ((hf, "s"), (hn, "y")):
        dma(q, blk(T.tlS, h, 1, 512), T.winS[0:128:16, 8192 * h:8192 * (h + 1)], ["winS0", "winS1"], ["tlS%d" % h])

    val_out(0)
    sel(T.Id[:], T.ones[:, 0:160], [[-1, 160]], ALU.is_equal, 16, 1, ["ones"], ["Id"])
    sel(T.GB[:], T.ones[:, 0:160], [[-16, 10], [0, 16]], ALU.is_ge, 16, 1, ["ones"], ["GB"])
    iota(T.w0[:, 32:64], [[0, 32]], 8, 0, ["w0h"])
    sel(T.GB[:], T.GB[:], [[16, 10], [0, 16]], ALU.is_ge, -1, -1, ["GB"], ["GB"])
    val_out(1)
    before("g", ["w0", "w0h", "w1"], [])
    for a in (0, 1):
        iota(T.w0[:, a::16], [[0, 4]], 0, 0, ["w0%d" % a])
    iota(T.w0[:, 8:32:16], [[0, 2]], 0, 0, ["w08"])
    for h, a, c in ((0, 0, 2 ** 21), (0, 1, -3 * 8 ** 6), (1, 0, 2 ** 23), (1, 8, -3)):
        iota(T.w1[:, 32 * h + a:32 * h + 32:16], [[0, 2]], c, 0, ["w1%d%d" % (h, a)])
    for i in range(2, NP):
        val_out(i)
    iota(T.rows[:, 192:224], [[0, 32]], -192, 0, ["rows6"])
    iota(T.rows[:, 64:96], [[0, 2], [1, 16]], 0, 0, ["rows2"])
    iota(T.rows[:, 192:224:4], [[0, 8]], 576, 0, ["rows6"])
    iota(T.rows[:, 96:128], [[0, 2], [192, 4], [0, 4]], 0, 0, ["rows3"])
    iota(T.rows[:, 192:224:16], [[0, 2]], -1024, 0, ["rows6"])
    iota(T.rows[:, 128:160], [[-1, 2], [0, 16]], 1, 0, ["rows4"])
    iota(T.rows[:, 160:192], [[1, 2], [0, 16]], 0, 0, ["rows5"])

    fo = ["formI0", "formI1"]
    ts(T.fI[:, 0], T.formI[:], 15, None, AND, None, fo, ["fI0"])
    ts(T.fI[:, 1], T.formI[:], 4, 15, SHR, AND, fo, ["fI1"])
    ts(T.fI[:, 2], T.formI[:], 8, None, SHR, None, fo, ["fI2"])
    ts(T.IdS[:, 0, :], Id, 2.0 ** 58, -2.0 ** 58, MUL, MUL, ["Id"], ["IdS0"])
    for gl in range(2):
        cp(T.fB[:, :, gl, :], T.fI[:, :, gl, :], ["fI0", "fI1", "fI2"], ["fB%d" % gl])
    fB = ["fB0", "fB1"]
    for i, c in ((1, 256.0), (2, 16.0)):
        act(T.IdS[:, i, :], Id, ACT.Identity, ["Id"], ["IdS%d" % i], scale=c)
    fill(T.mone[:, 0:256], 256, -1.0, ["mone"])
    act(T.E1[:], T.fB[:], ACT.Silu, fB, ["E1"], bias=POW0, scale=POW1)
    act(T.E2[:], T.fB[:], ACT.Silu, fB, ["E2"], bias=POW0 + 15 * POW1, scale=-POW1)
    mm([(T.P7[:, 256:384], Id if i == 0 else T.IdS[:, i, :], T.fB[:, 4 * i:4 * (i + 1)], i == 0, i == 2) for i in range(3)], fB + ["IdS1", "IdS2"], ["P7"])
    PV = (T.P5, T.P6)
    mm([(PV[hf][:], Id, blk(T.tlV, hf, 1, 512), True, True)], ["tlV%d" % hf], ["PV%d" % hf])
    for k, E in enumerate((T.E1, T.E2)):
        mm([(blk(T.P7, k, 1, 128), T.IdS[:, 0, :], blk(E, i, 1, 128), i == 0, i == 2) for i in range(3)], ["IdS0", "E%d" % (k + 1)], ["P7"])
    mm([(PV[hn][:], Id, blk(T.tlV, hn, 1, 512), True, True)], ["tlV%d" % hn], ["PV%d" % hn])
    cl = ["clsI%d" % k for k in range(8)]
    ts(T.clsI[:], T.clsI[:], 129, None, MUL, None, [], cl)
    scan(T.rows[:, 0:64], T.w0[:], T.w1[:], 0.0, MUL, ADD, ["w00", "w01", "w08", "w100", "w101", "w110", "w118"], ["rows0"])
    ts(T.clsI[:], T.clsI[:], 2, 127, SHR, AND, [], cl)
    tr(T.cols[:], T.rows[:], ["rows0"] + ["rows%d" % k for k in range(2, 7)], ["cols"])
    cp(T.clsF[:], T.clsI[:], cl, ["clsF"])
    tr(T.clsT[:], T.clsF[:], ["clsF"], ["clsT"])
    tt(blk(T.tq, hf, 1, 512), blk(T.tlS, hf, 1, 512), PV[hf][:], ADD, ["tlS%d" % hf], ["PV%d" % hf, "tqf"])
    cp(T.clsU[:], T.clsT[:, 0:16], ["clsT"], ["clsU"])
    tr(T.tabW[:], T.P7[:, 0:384], [], ["P7", "tabW"])
    for k in range(2):
        act(T.Wn[:, k, :], GB, ACT.Identity, ["GB", "cols"], ["Wn%d" % k], scale=col(k))
    for q in range(1, N):
        act(T.IdS[:, 2 + q, :], Id, ACT.Identity, ["Id"], ["IdQ%d" % q], scale=float(REG * q))
    act(T.Id32[:], Id, ACT.Identity, ["Id"], ["Id32"])
    for x in range(2):
        act(T.IM[:, x, :], T.Id[:], ACT.Identity, ["Id", "cols"], ["IM%d" % x], scale=col(4 + x))
    for k in range(2):
        act(blk(T.tabR, k), blk(T.tabW, k, 1, 128).indirect(T.clsU[:, 0:16]), ACT.Identity, ["tabW", "clsU"], ["tabR%d" % k], bias=2.0 ** 23)
    act(T.IdS[:, 7, :], Id, ACT.Identity, ["Id"], ["Id255"], scale=255.0)
    act(T.IdS[:, 6, :], Id, ACT.Identity, ["Id"], ["IdN"], scale=-2.0 * REG)
    fill(T.cum[:, 0:16], 16, 0.0, ["cum0"])
    fill(T.Gw[:, 0:768], 768, -0.25, ["Gw"])
    fill(T.mone[:, 256:768], 512, -1.0, ["mone2"])
    act(T.cv[:, 0:1], col(6), ACT.Identity, ["cols"], ["cv"])
    act(T.IdS[:, 8, :], Id, ACT.Identity, ["Id", "cols"], ["IdP"], scale=col(2))

    def near(A, q):
        return A[:, 256 * (q % 2):256 * (q % 2 + 1)]
    iota(T.TR[:], [[1, 16]], 768, 16, ["TR"])
    iota(T.sw[:], [[16, 48]], 0, 0, ["sw"])
    sel(T.INC[:], T.GB[:], [[1, 160]], ALU.is_ge, -16, -1, ["GB"], ["INC"])
    sel(T.H[:], T.GB[:, 16:160], [[0, 9], [1, 16]], ALU.is_equal, -15, 0, ["GB"], ["H"])
    send(to(far, "to", lambda q: blk(T.tq, q), blk(T.land, r)), ["tqf"])
    tt(blk(T.tq, sib), blk(T.tlS, sib), near(PV[hn], sib), ADD, ["tlS%d" % hn], ["PV%d" % hn, "tqs"])
    send(to([sib], "ts", lambda q: blk(T.tq, q), blk(T.land, r)), ["tqs"])
    tt(blk(T.land, r), blk(T.tlS, r), near(PV[hn], r), ADD, [], ["PV%d" % hn, "land_r"])
    sel(T.INC[:], T.INC[:], [[1, 160]], ALU.not_equal, -16, -1, [], ["INC"], fill=0.5)
    sel(T.dA[0:4, :], T.ones[0:4, 0:132], [[0, 33], [1, 4]], ALU.is_equal, 0, -1, ["ones"], ["dA"])
    sel(T.dN[0:4, :], T.zeroB[0:4, 0:132], [[0, 33], [1, 4]], ALU.not_equal, 0, -1, ["zeroB"], ["dN"], fill=-1.0)
    sel(T.STR[:], GB, [[1, 128]], ALU.is_gt, 0, -1, ["GB"], ["STR"])
    sel(T.DT[:], T.STR[:], [[-4, 32], [0, 4]], ALU.is_ge, 0, 1, ["STR"], ["DT"])
    iota(T.wid[:], [[1, 16], [16, 16]], 0, 0, ["wid"])
    iota(T.Ww[:, 0:768], [[0, 768]], 0, 0, ["Ww"])
    for x in range(2):
        act(T.TM[:, x, :], T.INC[:], ACT.Identity, ["INC", "cols"], ["TM%d" % x], scale=col(4 + x))
    act(T.H4[:], T.H[:], ACT.Identity, ["H"], ["H4"], scale=4096.0)
    act(T.Hn[:], T.H[:], ACT.Identity, ["H"], ["Hn"], scale=-1.0)

    def mark(q, n, R, tag):
        ts(blk(T.pres, q, n), blk(T.land, q, n), 0.0, None, ALU.not_equal, None, R, ["pres" + tag])
    ts(T.frm[:], blk(T.tabW, 2, 1, 128).indirect(T.clsU[:, 0:16]), -1.0 / 8192, 2047.0 / 8192, MUL, ADD, ["tabW", "clsU"], ["frm"])
    mark(r, 1, ["land_r"], "r")
    tr(T.frmT[:], T.frm[:], ["frm"], ["frmT"])
    mark(sib, 1, ["land_s"], "s")

    def digits(k, qs, first, last):
        o = (T.P0, T.P1)[k][:, 0:256]
        return ([(o, T.Wn[:, k, :], T.mone[:, 0:256], True, False)] if first else []) + \
            [(o, T.Wn[:, k, :], blk(T.pres, q), False, last and q == qs[-1]) for q in qs]

    def tables(A, qs, first, last):
        return [(A[:, 0:256], Id, blk(T.land, q), first, last and q == qs[-1]) for q in qs]

    def shifts(qs):
        return [(T.P4[:, 0:256], T.IdS[:, 2 + q, :], blk(T.pres, q), False, False) for q in qs if q]

    def turned(M, src, last):
        return [(T.P3[:, :, x, :], M[:, x, 16 - 16 * (gl - x):144 - 16 * (gl - x)], src[:, :, gl, :], False, last and x + gl == 2)
                for x in range(2) for gl in range(2)]

    IdQ = ["IdQ%d" % q for q in range(1, N)]
    mm(digits(0, [], True, False), ["Wn0", "mone"], ["P0"])
    mm(digits(1, [], True, False), ["Wn1"], ["P1"])
    mm([(T.P6[:, 0:16], T.Id32[:], T.TR[:], True, False)], ["TR", "Id32"], ["PV1"])
    mm(tables(T.P2, [r], True, False), ["land_r"], ["P2"])
    mm(tables(T.P4, [r], True, False), [], ["P4"])
    mm(digits(0, [r], False, False), ["presr"], ["P0"])
    mm(digits(1, [r], False, False), [], ["P1"])
    mm(tables(T.P2, [sib], False, False), ["land_s"], ["P2"])
    mm(digits(0, [sib], False, False), ["press"], ["P0"])

    mm(tables(T.P2, far, False, True), ["land_o"], ["P2"])
    mark(far[0], 2, ["land_o"], "o")
    ts(T.clp[:], T.P2[:, 0:256], -1.0, 1.0, ALU.max, ALU.min, [], ["P2", "clp"])
    mm(digits(0, far, False, True), ["preso"], ["P0"])
    mm(digits(1, others, False, True), [], ["P1"])
    mm(tables(T.P4, others, False, False) + shifts(range(N)) + [(T.P4[:, 0:256], T.IdS[:, 7, :], T.clp[:], False, True)],
       ["clp", "Id255"] + IdQ, ["P4"])
    mm([(T.P3[:], Id, T.mone[:, 0:256], True, False)] + turned(T.IM, T.frmT, False), ["IM0", "IM1", "frmT"], ["P3"])
    mm([(T.P2[:, 0:128], T.dA[0:4, 1:129], T.dA[0:4, 0:128], True, False), (T.P2[:, 0:128], T.dA[0:4, 1:129], T.dN[0:4, 1:129], False, True)],
       ["dA", "dN"], ["P2"])
    tt(blk(T.U, 0), blk(T.tabR, 0), T.P0[:, 0:256], ADD, ["tabR0"], ["P0", "U0"])
    tt(blk(T.U, 1), blk(T.tabR, 1), T.P1[:, 0:256], ADD, ["tabR1"], ["P1", "U1"])
    ts(blk(T.U, 0), blk(T.U, 0), 4 * DIG, None, AND, None, [], ["U0"])
    ts(blk(T.U, 1), blk(T.U, 1), 4 * DIG, 1, AND, SHR, [], ["U1"])
    ts(T.posU[:], T.P4[:, 0:256], float(MID), None, ADD, None, [], ["P4", "posU"])
    gather(T.VT[:], T.allv[:, 0:4 * REG].indirect(T.posU[:, 0:256]), ACT.Copy, ["posU", "gap0", "gap1", "vs", "vf"] + sum(loaded, []), ["VT"])
    tt(T.ok[:], blk(T.U, 0), blk(T.U, 1), ALU.is_equal, ["U0", "U1"], ["ok"])

    scan(T.cum[:, 16:272], T.ones[:, 0:256], T.ok[:], 0.0, MUL, ADD, ["ones", "ok"], ["cum"])
    tr(T.okT[:], T.ok[:], ["ok"], ["okT"])
    mine_n = T.cum[:, 271:272]
    lo_, hi_ = T.cum[:, 15:271:16], T.cum[:, 31:272:16]
    mm([(T.P6[:, 0:16], T.IdS[:, 4, :], lo_, False, False), (T.P6[:, 0:16], T.IdS[:, 6, :], hi_, False, True)], ["cum", "cum0", "IdN"], ["PV1"])
    mm([(T.P4[:, 0:1], T.DT[:], mine_n, True, True)], ["DT", "cum"], ["P4"])
    mm(turned(T.TM, T.okT, True), ["TM0", "TM1", "okT"], ["P3"])
    send(to(others, "ca", lambda q: T.cum[:, 264:272], blk(T.cntL, r, 1, 8)), ["cum"])
    cp(T.dB[:], T.P2[:, 0:128], [], ["P2", "dB"])
    tt(T.tz[:], lo_, T.P6[:, 0:16], ALU.max, ["cum0"], ["PV1", "tz"])
    ts(T.offU[:], T.tz[:], T.P4[:, 0:1], col(3), ADD, ADD, ["tz", "cols"], ["P4", "offU"])
    ts(T.Gt[:], T.P3[:], 0.5, -0.25, ADD, ALU.max, [], ["P3", "Gt"])
    sel(T.Sel[:], T.ones[:], [[1, 4], [-64, 8], [-1, 16]], ALU.is_equal, -16 * r, 4, ["ones"], ["Sel"])
    sel(T.DD[:], T.dB[:], [[-16, 8], [0, 16]], ALU.is_ge, 0, 1, ["dB"], ["DD"])
    sel(T.DD[:], T.DD[:], [[1, 128]], ALU.is_gt, 0, -1, [], ["DD"])
    sel(T.STR[:, 0::16], T.GB[:, 16:144:16], [[0, 8]], ALU.is_ge, 0, 0, ["GB"], ["STR"])
    iota(T.lo[:], [[1, 256]], 0, 0, ["lo"])
    iota(T.Et[:], [[1, 1024]], 0, 0, ["Et"])
    oU = ["offU"]
    cp(T.Ww[:, 0:WIDE].indirect(T.offU[:, 0:16]), T.wid[:], oU + ["wid"], ["Ww"])
    cp(T.Gw[:, 0:WIDE].indirect(T.offU[:, 0:16]), T.Gt[:], oU + ["Gt"], ["Gw"])
    scan(T.Ws[:], T.Ww[:, 0:768], T.Ww[:, 0:768], 0.0, ALU.max, ALU.max, ["Ww"], ["Ws"])
    scan(T.Ds[:], T.mone[:], T.Gw[:, 0:768], -0.25, ADD, ALU.max, ["Gw", "mone", "mone2"], ["Ds"])

    def cn(q):
        return mine_n if q == r else T.cntL[:, 8 * q + 7:8 * q + 8]
    mm([(T.P7[:, 0:1], blk(T.Sel, q, 1, 128), cn(q), q == 0, q == N - 1) for q in range(N)], ["Sel", "cntL", "cum"], ["P7"])
    mm([(T.P1[:, 0:1], blk(T.Sel, 0, 1, 128), cn(q), q == 0, q == N - 1) for q in range(N)], [], ["P1"])
    mm(wrap(T.P5[:, 0:48], T.H4, T.Ws, True, False), ["H4", "Ws"], ["PV0"])
    cp(T.nS[:, 0:1], T.P7[:, 0:1], [], ["P7", "nS"])
    m1 = T.mone[:, 0:1]
    mm([x for k in range(3) for x in [(T.P0[:, k:k + 1], T.IdS[:, 1, :], m1, i == 0, False) for i in range(k)]
        + [(T.P0[:, k:k + 1], T.STR[:], T.nS[:, 0:1], k == 0, True)]]
       + [(T.P0[:, 3:4], T.DD[:], T.nS[:, 0:1], True, False), (T.P0[:, 3:4], Id, T.cv[:, 0:1], False, True)], ["STR", "DD", "nS", "cv"], ["P0"])
    for k in range(2):
        ts(T.phi[:, k::2], T.Ds[:, k::2], 8192.0, 2048.0, MUL, ALU.min, ["Ds"], ["phi%d" % k])
        mm(wrap(T.P5[:, 0:48], T.Hn, T.phi, False, True)[k::2], ["Hn", "phi%d" % k], ["PV0"])

    def steps(k):
        ts(blk(T.X, k), T.lo[:], T.P0[:, k:k + 1], T.P0[:, 3:4], ALU.is_ge, MUL, ["lo", "P0"], ["X%d" % k])
    steps(0)
    steps(1)

    ts(T.Z[:], T.P5[:, 0:48], 32767.0, None, ADD, None, [], ["PV0", "Z"])
    steps(2)
    mm([(T.P6[:, 0:48], Id, T.sw[:], True, False), (T.P6[:, 0:48], T.IdS[:, 8, :], T.ones[:, 0:48], False, False)]
       + wrap(T.P6[:, 0:48], T.Hn, T.X, False, True), ["sw", "IdP", "X0", "X1", "X2"], ["PV1"])
    ts(T.zI[:, 0, :], T.Z[:], 8, 0xFFF, SHR, AND, ["Z"], ["z0"])
    ts(T.zI[:, 1, :], T.Z[:], 8, 0xFF0, SHR, AND, ["Z"], ["z1"])
    cp(T.kL[:, 96:144], T.zI[:, 0, :], ["z0"], ["kB"])
    ts(T.zI[:, 2, :], T.Z[:], 15, None, AND, None, ["Z"], ["z2"])
    ts(T.zI[:, 3, :], T.Z[:], 4, 15, SHR, AND, ["Z"], ["z3"])
    tt(T.kF[:, 0:48], T.zI[:, 1, :], T.zI[:, 2, :], ADD, ["z1", "z2"], ["kF0"])
    tt(T.kF[:, 48:96], T.zI[:, 1, :], T.zI[:, 3, :], ADD, ["z1", "z3"], ["kF1"])
    cp(T.kL[:, 0:48], T.kF[:, 0:48], ["kF0"], ["kA"])

    VTw = T.VT[:, 0:4096]
    for d in far + [sib, r]:
        gather(blk(T.Bv, d, 1, 192), VTw.indirect(T.kL[:, 96 + 12 * d:96 + 12 * (d + 1)]), ACT.Copy, ["VT", "kB"], ["Bv%d" % d])
    mine = blk(T.Yl, r, 1, 192)

    def first(d):
        tt(blk(T.tv, d, 1, 192), VTw.indirect(blk(T.kL, d, 1, 12)), blk(T.Bv, d, 1, 192), ALU.subtract, ["VT", "kA", "Bv%d" % d], ["tv%d" % d])

    def second(d):
        tt(mine if d == r else blk(T.ys, d, 1, 192), VTw.indirect(T.kL[:, 48 + 12 * d:48 + 12 * (d + 1)]), blk(T.tv, d, 1, 192), ADD,
           ["tv%d" % d, "kC"], ["ys%d" % d])
    def numbers_out(d):
        second(d)
        send(one(d, "ya", blk(T.ys, d, 1, 192), mine), ["ys%d" % d])
    ts(T.zI[:, 4, :], T.Z[:], 12, 255, SHR, AND, ["Z"], ["z4"])
    first(far[0])
    ts(T.msg[:], T.zI[:, 4, :], 256.0 * r, None, ADD, None, ["z4"], ["msg"])
    send(to(others, "ma", lambda q: blk(T.msg, q, 1, 12), T.msgL[:, 16 * r:16 * r + 12]), ["msg"])
    cp(T.kL[:, 48:96], T.kF[:, 48:96], ["kF1"], ["kC"])
    first(far[1])
    if YSPLIT:
        numbers_out(far[0])
        numbers_out(far[1])
    else:
        second(far[0])
        second(far[1])
        send(to(far, "ya", lambda q: blk(T.ys, q, 1, 192), mine), ["ys%d" % q for q in far])
    first(sib)
    ts(T.sigU[:], T.P6[:, 0:48], 768.0, None, ALU.min, None, [], ["PV1", "sigU"])
    numbers_out(sib)
    first(r)
    cp(T.co[:, 0:1], T.P1[:, 0:1], [], ["P1", "co"])
    dma("y", T.cnt[:], T.co[0:128:4, 0:1], ["co"], ["cnt"])
    second(r)
    fill(T.EL[:, 768:776], 8, -1.0, ["EL_z"])
    fill(T.Yl[:, 768:784], 16, 0.0, ["Yl_z"])
    gather(blk(T.EL, r, 1, 192), T.Et[:, 0:1024].indirect(blk(T.msg, r, 1, 12)), ACT.Copy, ["Et", "msg"], ["EL%d" % r])
    for q in others:
        gather(blk(T.EL, q, 1, 192), T.Et[:, 0:1024].indirect(T.msgL[:, 16 * q:16 * q + 12]), ACT.Copy, ["msgL"], ["EL%d" % q])

    WR = ["EL%d" % q for q in range(N)] + ["EL_z", "sigU"]
    if WV:
        cp(T.wo[:, 0:16 * WV], T.EL[:, 0:776].indirect(T.sigU[:, 0:WV]), WR, ["wo0"])
    gather(T.wo[:, 16 * WV:768], T.EL[:, 0:776].indirect(T.sigU[:, WV:48]), ACT.Copy, WR, ["wo1"])
    dma("y", T.who[:], T.wo[0:128:16, :], ["wo0", "wo1"], ["who"])
    YR = ["sigU", "Yl_z", "Yl_r", "ys%d" % r]
    cp(T.yo[:, 0:16 * YV], T.Yl[:, 0:784].indirect(T.sigU[:, 0:YV]), YR, ["yo0"])
    dma("y", T.y[:, 0:16 * YV], T.yo[:, 0:16 * YV], ["yo0"], ["y0"])
    gather(T.yo[:, 16 * YV:768], T.Yl[:, 0:784].indirect(T.sigU[:, YV:48]), ACT.Copy, YR, ["yo1"])
    dma("s", T.y[:, 16 * YV:768], T.yo[:, 16 * YV:768], ["yo1"], ["y1"])
    for name, val in count.items():
        need("g", (name, val, {}))
